import numpy as np, ml_dtypes
CORES = [2,3,42,43,82,83,122,123]
N = 8
import mx_ref
BF = ml_dtypes.bfloat16
def cols(t, e):
    v = np.concatenate([t.reshape(128, -1, 4), np.zeros((128, 1, 4), BF)], axis=1)
    return np.ascontiguousarray(v[:, e]).reshape(128, -1)
def cut(t, i, w=512):
    return t[:, w * i:w * i + w]
def pick(q, e):
    c = np.concatenate([q[0].reshape(128, -1, 4), np.zeros((128, 1, 4), np.uint8)], axis=1); s = np.concatenate([q[1], np.ones((16, 1), np.uint8)], axis=1)
    return (np.ascontiguousarray(c[:, e].reshape(128, -1)), np.ascontiguousarray(s[:, e]))
def join(*qs):
    return (np.concatenate([q[0] for q in qs], axis=1), np.concatenate([q[1] for q in qs], axis=1))
def put(q, e, v):
    c, s = q[0].reshape(128, -1, 4).copy(), q[1].copy(); c[:, e] = v[0].reshape(128, -1, 4); s[:, e] = v[1]
    return (c.reshape(128, -1), s)
def pk(c, s):
    return (np.ascontiguousarray(c), mx_ref.live(s))
def emit(q):
    return q[0], q[1]
def decode(q):
    o = []
    for b in range(4):
        e = np.zeros((128, 128, 4), np.float32); e[np.arange(128), np.arange(128), b] = 1
        o.append(mx_ref.matmul(mx_ref.quantize(e.reshape(128, 512).astype(BF)), q))
    return np.stack(o, axis=2).reshape(128, -1)
def f(rng, *shape):
    return mx_ref.flush((rng.standard_normal(shape, dtype=np.float32) * np.exp2(rng.integers(-2, 3, shape[:-1] + (1,)))).astype(BF))
def wide(rng, *shape, cols=0):
    v = rng.standard_normal(shape, dtype=np.float32) * np.exp2(rng.integers(-12, 13, shape)).astype(np.float32)
    if cols: v *= np.repeat(np.exp2(rng.integers(-cols, cols + 1, shape[:-2] + (1, shape[-1] // 4))) * (rng.random(shape[:-2] + (1, shape[-1] // 4)) > 0.0625), 4, axis=-1).astype(np.float32)
    return mx_ref.flush(v.astype(BF))
P, K, R, O = 256, 32, 2, 1
def big(v):
    v = v.astype(np.float32)
    v[np.abs(v) < np.float32(2.0 ** -16)] = 0
    return v.astype(BF)
def times(t, k):
    return mx_ref.flush((t.astype(np.float32) * np.float32(k)).astype(BF))
def signs(d, v, s):
    g = np.where(d["u"][0, :, :4].astype(np.float32) < 0, -1, 1)
    a = np.abs(v.astype(np.float32)).reshape(N, 128, -1, 4) * g[None, :, None, :] * s[:, None, :, None]
    return big(a.reshape(N, 128, -1))
def counted(rng, d):
    n = P // 2 + rng.permutation(K)[:N]
    return signs(d, d["tb"], np.stack([np.where(rng.permutation(P) < n[r], 1, -1) for r in range(N)]))
def setup_inputs(rng):
    v = np.zeros((128, 512), np.float32)
    v[:, :4] = f(rng, 128, 4).astype(np.float32)
    return {"tb": big(f(rng, N, 128, 4 * P)), "nz": big(f(rng, N, 128, 4 * R * K)), "u": np.stack([v.astype(BF)] * N), "w": f(rng, N, 128, 512 * O)}
def setup_inputs_down(rng):
    d = setup_inputs(rng)
    d["tb"] = counted(rng, d)
    d["nz"] = signs(d, 64 * (1 + rng.random((N, 128, 4 * R * K))), np.full((N, R * K), -1))
    return d
def setup_inputs_spread(rng):
    d = setup_inputs(rng)
    t, r = big(wide(rng, N, 128, 4 * P, cols=6)), int(rng.integers(0, N))
    x = (1 + rng.random((N, 128, 4 * P))) * np.exp2(rng.integers(12, 18, (N, 128, 4 * P)) + np.repeat(rng.integers(0, 4, (N, 1, P)), 4, axis=2))
    t[r] = signs(d, x, np.ones((N, P), np.int64))[r]
    return {**d, "tb": t, "nz": big(wide(rng, N, 128, 4 * R * K, cols=6)), "u": times(d["u"], 2.0 ** 24)}
def setup_inputs_swap(rng):
    d = setup_inputs(rng)
    d["tb"] = counted(rng, d)
    d["nz"] = signs(d, 64 * (1 + rng.random((N, 128, 4 * R * K))), np.full((N, R * K), 1))
    return d
def setup_inputs_ties(rng):
    d = setup_inputs(rng)
    a = rng.permutation(N) <= N // 2
    d["tb"] = np.stack([cols(d["tb"][int(a[r])], rng.permutation(P) % (P // (K + 1))) for r in range(N)])
    d["nz"] = np.stack([d["nz"][0]] * N)
    return d
def setup_inputs_zero(rng):
    d = setup_inputs(rng)
    d["u"] = times(np.abs(d["u"].astype(np.float32)), 2.0 ** -26)
    d["tb"], d["nz"] = big(times(d["tb"], 2.0 ** -10)), big(times(d["nz"], 2.0 ** -10))
    s, a = np.zeros((N, P), np.int64), rng.permutation(N)
    for i in range(N - 1):
        m, n, e = P // 2 - 4 * i, K // 2 - i, rng.permutation(P)
        s[a[i], e[:m]] = 1
        s[a[i], e[m:m + n]] = -1
    d["tb"] = signs(d, d["tb"], s)
    for r in range(N):
        d["tb"][r].reshape(128, P, 4)[:, np.flatnonzero(s[r] == 0)[1::2]] = BF(-0.0)
    d["nz"] = big(d["nz"].astype(np.float32) * np.repeat(rng.random((N, 1, R * K)) > 0.25, 4, axis=2))
    return d
def check_inputs(d):
    b = []
    for k, low, high in (("tb", -16, 26), ("nz", -16, 26), ("u", -30, 30), ("w", -30, 30)):
        v = np.abs(d[k].astype(np.float32))
        if not (np.isfinite(v).all() and ((v == 0) | (v >= 2.0 ** low) & (v <= 2.0 ** high)).all()): b.append("a value of " + k)
    v = d["u"].astype(np.float32)
    if (v[:, :, 4:] != 0).any(): b.append("u has numbers behind its column 0")
    if (v != v[:1]).any(): b.append("u isn't the same on all ranks")
    return b
def reference(tb, nz, u, w):
    T = [mx_ref.quantize(tb[r]) for r in range(N)]
    qu = [mx_ref.quantize(u[r]) for r in range(N)]
    od = np.zeros((N, R, N), np.float32)
    for t in range(R):
        s = [mx_ref.matmul(qu[r], T[r])[0] + np.float32(0) for r in range(N)]
        fitness = np.array([np.count_nonzero(s[r] > 0) for r in range(N)])
        place = np.argsort(-fitness, kind="stable")
        od[:, t] = place
        new = T[:]
        for i in range(N // 2):
            a, b = place[i], place[N - 1 - i]
            j = np.argsort(s[a], kind="stable")[:K]
            noise = mx_ref.quantize(np.ascontiguousarray(nz[b][:, 4 * t * K:4 * (t + 1) * K]))
            v = np.float32(0.5) * decode(pick(T[a], j)) + np.float32(0.5) * decode(noise)
            new[b] = put(T[a], j, mx_ref.quantize(np.ascontiguousarray(v.astype(BF))))
        T = new
    oc, osc, y = np.zeros((N, 128, 4 * P), np.uint8), np.zeros((N, 16, P), np.uint8), np.zeros((N, 128, O * P), np.float32)
    for r in range(N):
        oc[r], osc[r] = emit(T[r])
        for o in range(O):
            y[r, :, o * P:(o + 1) * P] = mx_ref.matmul(mx_ref.quantize(np.ascontiguousarray(cut(w[r], o))), T[r])
    return {"oc": oc, "osc": osc, "od": od, "y": y}

@@ -1,0 +1,623 @@
+from concourse.bass import DstId, RemoteDMATransfer
+from concourse.mybir import dt, AluOpType, AxisListType, ActivationFunctionType
+
+A = AluOpType
+F = ActivationFunctionType
+CODE, PLANE, F32, BF, I32, U16 = "float8_e4m3fn_x4", "uint8", "float32", "bfloat16", "int32", "uint16"
+SCRATCH, PART = {}, {}
+
+
+def _bufs():
+    def b(dtype, **kw):
+        for k in kw:
+            SCRATCH[k] = ("sbuf", [128, kw[k]], dtype)
+
+    def parts(name, dtype, **kw):
+        n = 0
+        for k in kw:
+            PART[k] = (name, n)
+            n += kw[k]
+        SCRATCH[name] = ("sbuf", [128, n], dtype)
+
+    def q(**kw):
+        for k in kw:
+            SCRATCH[k] = ("sbuf", [128, kw[k]], CODE)
+            SCRATCH[k + "s"] = ("sbuf", [128, kw[k]], PLANE)
+    b(BF, tbx=1024, nzx=512, wx=512, ux=512, u4=8, eb=528, ct=1024, oh=512, vt=512, vt2=512, zb=128, hb=128, idn=128,
+      lt4=512, cmp=512, c1=256, s1=256)
+    parts("bconst", BF, m16=256, md16=256, r8=64, r32=256, md32=256, io=128, io64=128, mask=128, i32r=128)
+    parts("fconst", F32, hif=8, hi8=8, h16=8, h16b=8, wr=8, pf=8, c16r=8, c2=8, corr=8, corr32=8, wt=256)
+    parts("fown", F32, ft=8, sm=256, pos=8, ss=8, ds01=8, js=64, junk=512)
+    parts("flist", F32, xx=8, w256=8, tsum=64, tie5=64, tie=64, ri=64, ef=8, wc=8, x32=8,
+          ones=64, p256=64, tmp2=8, o0a=8, dd=64, nd=64, nl=8, nh=8, nj=8,
+          k1=64, cm=64, sc=64, ms=8, st=8, go=8, q0=64, g0=64, hit=64, hf=64, hfs=64, hh=64, hhs=64, tks=8, thr8=8,
+          thr=256, tmp=8, base1=8, wh8=8, w0=8, wh=64, cola=8, o0=8, sw=512, jr=512, ode=8, odc=8, odr=8,
+          k1b=64, x1b=64, cmb=64, scb=64, q1=64, g1=64, miss=64, bs=64, o1=8, st0=8, t32=8, csj=128, dgo=128,
+          ds=128, lt=128, eq=128, jl=128, eqj=128, cnt=128, tp=64, cr=64, crw=64, sel=64, zf=32,
+          off=64, jws=64, frow=256, fs=256)
+    b(F32, vi=8, fiti=8, jt=512, yo=256)
+    parts("iconst", I32, pi=8, hx=8, ai=8, yi=8, ei=8, bi=8, l2i=16)
+    b(U16, vl=64)
+    parts("lists", U16, jl4=4, in32=4, ou32=4, lrs=4, lq7=4, grs=4, gr=4, gis=4, l256=16, ofa=2, ofx=2, of=16, ofc=4,
+          ofj=4, pl=4, jw=4, fl=16)
+    q(uq=128, tq=384, nq=128, wq=128, eh=512, cq=256, oq=128, sp=64, land=256, cd=128, xw=192, xs=32, cw=512,
+      sl=256, sb=256, cc=128, np=128, fw=448, oq2=256, hq=264, ll=128)
+    SCRATCH["dv"] = ("psum", [128, 2048], F32)
+    SCRATCH["pp"] = ("psum", [128, 2048], F32)
+
+
+_bufs()
+SEMAPHORES = ["cv", "cs", "ct_", "cg", "lo", "a_v", "a_c", "a_s", "b_c", "b_s", "c_c", "c_s", "s_c", "s_s", "h_c",
+              "h_s", "h_l", "l_c", "l_s"] + ["d%d" % i for i in range(48)]
+
+
+def find_helpers(T, topo):
+    out = []
+    for c in T.cores:
+        for k in topo.cores_of(c):
+            if k in T.cores or k in out or topo.die(k) == topo.die(c):
+                continue
+            if all(topo.may_write(k, x) for x in T.cores):
+                out.append(k)
+                break
+    return out
+
+
+def bits(engines):
+    return sum(1 << e for e in engines)
+
+
+def ways(core, T, topo, me):
+    far = [r for r in range(len(T.cores)) if r != me and topo.chip(T.cores[r]) != topo.chip(core)]
+    near = [r for r in range(len(T.cores)) if r != me and topo.chip(T.cores[r]) == topo.chip(core)]
+    out = topo.engines(core, T.cores[far[0]])
+    inn = [e for e in topo.engines(core, T.cores[near[0]]) if e not in out][:2]
+    return far, near, out, inn
+
+
+def dest(T, topo, r):
+    rid, pid, _ = topo.addr(T.cores[r])
+    return DstId(rid=rid, pnc=pid)
+
+
+def one_each(g, T, topo, to, src, dst, sem):
+    g.remote_dma_fused([RemoteDMATransfer(dst_ids=[dest(T, topo, r)], dma_engine_mask=bits(e), remote_sem=sem,
+                                          src=src(r), dst=dst) for r, e in to], local_sem=T.sem.lo)
+    return sum(len(e) for _, e in to)
+
+
+def same_to_all(g, T, topo, to, src, dst, sem):
+    g.remote_dma_fused([RemoteDMATransfer(dst_ids=[dest(T, topo, r) for r in rs], dma_engine_mask=bits(e),
+                                          remote_sem=sem, srcs=[src], dsts=[dst] * len(rs)) for rs, e in to],
+                       local_sem=T.sem.lo)
+    return sum(len(e) for _, e in to)
+
+
+def hand_on(g, core, T, topo, r):
+    S = 32
+    c0, l0 = S * (len(T.cores) - 1 - r), 2 * (len(T.cores) - 1 - r)
+    far, near, out, inn = ways(core, T, topo, r)
+    to = [(s, out[i:i + 1]) for i, s in enumerate(far)] + [(s, inn[:1]) for s in near]
+    lists = [(far, out), (near, inn)]
+    g.wait_ge(T.sem.h_c, len(out))
+    n = one_each(g, T, topo, to, lambda s: T.hq[:, S * s:S * s + S].bitcast(dt.uint8),
+                 T.sl[:, c0:c0 + S].bitcast(dt.uint8), T.sem.s_c)
+    g.wait_ge(T.sem.h_l, len(out))
+    n += same_to_all(g, T, topo, lists, T.hq[:, 256:258].bitcast(dt.uint8), T.ll[:, l0:l0 + 2].bitcast(dt.uint8),
+                     T.sem.l_c)
+    g.wait_ge(T.sem.h_s, len(out))
+    n += same_to_all(g, T, topo, lists, T.hqs[:, 256:258], T.lls[:, l0:l0 + 2], T.sem.l_s)
+    n += one_each(g, T, topo, to, lambda s: T.hqs[:, S * s:S * s + S], T.sls[:, c0:c0 + S], T.sem.s_s)
+    g.wait_ge(T.sem.lo, n)
+
+
+def builder(g, T):
+    queue = {"v": g.vector, "s": g.scalar, "t": g.tensor, "g": g, "y": g.sync}
+    sem = {"v": "cv", "s": "cs", "t": "ct_", "g": "cg"}
+    count = {"v": 0, "s": 0, "t": 0, "g": 0}
+    seen, log, dmas = {}, {}, [0]
+
+    def ap(n, a, b, st=1, p=None, bc=None, off=None):
+        n, k = PART.get(n, (n, 0))
+        a, b, t = a + k, b + k, T[n]
+        rows = slice(None) if p is None else slice(p[0], p[1])
+        v = t[rows, a:b] if st == 1 else t[rows, a:b:st]
+        if bc is not None:
+            v = v.bitcast(bc)
+        if off is not None:
+            v = v.indirect(off["v"])
+        return {"v": v, "n": n, "a": a, "b": b, "st": st, "off": off}
+
+    def apart(x, y):
+        if x["n"] in ("dv", "pp"):
+            return x["a"] // 512 != y["a"] // 512
+        if x["a"] >= y["b"] or y["a"] >= x["b"]:
+            return True
+        return x["st"] == y["st"] and x["st"] > 1 and (x["a"] - y["a"]) % x["st"] != 0
+
+    def wait(q, tok):
+        if seen.get((q, tok[0]), 0) < tok[1]:
+            queue[q].wait_ge(T.sem[tok[0]], tok[1])
+            seen[(q, tok[0])] = tok[1]
+
+    def need(q, outs, ins):
+        toks = {}
+        for w, xs in ((True, outs), (False, ins)):
+            for x in xs:
+                for (y, yw, yq, tok) in log.get(x["n"], []):
+                    if apart(x, y):
+                        continue
+                    psum = x["n"] in ("dv", "pp")
+                    if yw or (w and yq != q) or (psum and yq != q):
+                        if yq == q == "t" and yw and w:
+                            continue
+                        toks[tok[0]] = max(toks.get(tok[0], 0), tok[1])
+        for k in toks:
+            wait(q, (k, toks[k]))
+
+    def note(q, outs, ins, tok):
+        for w, xs in ((True, outs), (False, ins)):
+            for x in xs:
+                log.setdefault(x["n"], []).append((x, w, q, tok))
+
+    def full(xs):
+        return [x for x in xs if x] + [x["off"] for x in xs if x and x["off"]]
+
+    def run(q, fn, outs, ins):
+        ins = full(ins) + [x["off"] for x in outs if x["off"]]
+        need(q, outs, ins)
+        count[q] += 1
+        fn(queue[q]).then_inc(T.sem[sem[q]], 1)
+        note(q, outs, ins, (sem[q], count[q]))
+
+    def dma(q, out, in_, outs, ins):
+        need(q, outs, ins)
+        s = "d%d" % dmas[0]
+        dmas[0] += 1
+        queue[q].dma_start(out, in_).then_inc(T.sem[s], 16)
+        note("dma", outs, ins, (s, 16))
+
+    def arrive(n, a, b, tok):
+        x = {"n": n, "a": a, "b": b, "st": 1, "off": None}
+        log.setdefault(n, []).append((x, True, "far", tok))
+
+    def ready(q, ins):
+        need(q, [], full(ins))
+
+    def finish():
+        for q in count:
+            wait("y", (sem[q], count[q]))
+        for k in range(dmas[0]):
+            wait("y", ("d%d" % k, 16))
+    return ap, run, dma, arrive, ready, finish
+
+
+def rank_program(g, core, T, topo):
+    me = T.rank_of(core)
+    helpers = find_helpers(T, topo)
+    if me is None:
+        if core in helpers:
+            hand_on(g, core, T, topo, helpers.index(core))
+        return
+    ap, run, dma, arrive, ready, finish = builder(g, T)
+    u8, u32 = dt.uint8, dt.uint32
+    slot = 7 - me
+    far, near, out, inn = ways(core, T, topo, me)
+    sent = [0]
+
+    def sca(x):
+        return x["v"] if isinstance(x, dict) else x
+
+    def dic(*xs):
+        return [x for x in xs if isinstance(x, dict)]
+
+    def ts(out, in0, s1, op0, s2=None, op1=None):
+        if op1 is None:
+            run("v", lambda q: q.tensor_scalar(out["v"], in0["v"], sca(s1), None, op0), [out], dic(in0, s1))
+        else:
+            run("v", lambda q: q.tensor_scalar(out["v"], in0["v"], sca(s1), sca(s2), op0, op1), [out],
+                dic(in0, s1, s2))
+
+    def tt(out, in0, in1, op):
+        run("v", lambda q: q.tensor_tensor(out["v"], in0["v"], in1["v"], op), [out], [in0, in1])
+
+    def scan(out, d0, d1, op0=A.mult, op1=A.add):
+        run("v", lambda q: q.tensor_tensor_scan(out["v"], d0["v"], d1["v"], 0.0, op0, op1), [out], [d0, d1])
+
+    def cp(out, in_):
+        run("v", lambda q: q.tensor_copy(out["v"], in_["v"]), [out], [in_])
+
+    def fill(out, c):
+        run("v", lambda q: q.memset(out["v"], c), [out], [])
+
+    def red(out, in_):
+        run("v", lambda q: q.tensor_reduce(out["v"], in_["v"], AxisListType.X, A.add), [out], [in_])
+
+    def act(out, in_, func=None, bias=0.0, scale=1.0, accum=None):
+        plain = not dic(bias, scale) and bias == 0.0 and scale == 1.0
+        func = func or (F.Copy if plain else F.Identity)
+        kw = {} if plain else {"bias": sca(bias), "scale": sca(scale)}
+        if accum:
+            kw["accum_out"] = accum["v"]
+        run("s", lambda q: q.activation(out["v"], in_["v"], func, **kw), [out] + dic(accum), [in_] + dic(bias, scale))
+
+    def quant(n, a, b, tile, x0=0):
+        o, p, x = ap(n, a, b), ap(n + "s", a, b), ap(tile, x0, x0 + 4 * (b - a))
+        run("v", lambda q: q.quantize_mx(o["v"], p["v"], x["v"]), [o, p], [x])
+
+    def mm(out, l, la, r, ra, rb, start=True, stop=True):
+        xs = [ap(l, la, la + 128), ap(l + "s", la, la + 128), ap(r, ra, rb), ap(r + "s", ra, rb)]
+        run("t", lambda q: q.matmul_mx(out["v"], xs[0]["v"], xs[1]["v"], xs[2]["v"], xs[3]["v"], start, stop),
+            [out], xs)
+
+    def pick(dn, c, d, sn, a, b, on, e, f):
+        off = ap(on, e, f)
+        cp(ap(dn, c, d, bc=u32), ap(sn, a, b, bc=u32, off=off))
+        act(ap(dn + "s", c, d), ap(sn + "s", a, b, off=off))
+
+    def move(dn, c, sn, a, n):
+        o, i = ap(dn, c, c + n, bc=u8), ap(sn, a, a + n, bc=u8)
+        dma("y", o["v"], i["v"], [o], [i])
+        o, i = ap(dn + "s", c, c + n), ap(sn + "s", a, a + n)
+        dma("y", o["v"], i["v"], [o], [i])
+
+    def load(q, n, a, b, src):
+        o = ap(n, a, b)
+        dma(q, o["v"], src, [o], [])
+
+    def to_all(src, dst, sem):
+        ready("g", [src])
+        sent[0] += same_to_all(g, T, topo, [(far, out), (near, inn)], src["v"], dst["v"], T.sem[sem])
+
+    def c(n, k=0):
+        return ap(n, k, k + 1)
+
+    def iota(n, k, pat, base=0, cm=0):
+        o, small = ap(n, 0, k), SCRATCH[PART[n][0]][2] != I32
+        kw = {"allow_small_or_imprecise_dtypes": True} if small else {}
+        run("g", lambda q: q.iota(o["v"], pat, base, cm, **kw), [o], [])
+
+    def wrap(s, row, w):
+        scan(ap(s, 0, w), ap("wt", 0, w), row, A.add, A.max)
+
+    def listed(lst, s, w, corr="corr", a=0):
+        ts(ap(lst, a // 16, w // 16), ap(s, a + 15, w, 16), c(corr), A.add)
+
+    load("s", "u4", 0, 4, T.u[:, 0:4])
+    load("y", "tbx", 0, 512, T.tb[:, 0:512])
+    load("s", "tbx", 512, 1024, T.tb[:, 512:1024])
+    load("y", "nzx", 0, 256, T.nz[:, 0:256])
+    load("y", "wx", 0, 512, T.w[:, 0:512])
+    iota("pi", 4, [[0, 4]], 0, 1)
+    iota("c16r", 4, [[16, 4]])
+    iota("io", 128, [[1, 128]])
+    iota("io64", 128, [[0, 2], [1, 64]])
+    iota("md16", 256, [[0, 16], [1, 16]])
+    zb = ap("zb", 0, 128)
+    fill(zb, 0.0)
+    fill(ap("ct", 512, 1024), 0.0)
+    pi, ai, yi = ap("pi", 0, 4), ap("ai", 0, 4), ap("yi", 0, 4)
+    ts(ai, pi, 15, A.bitwise_and)
+    ts(c("hx"), c("pi"), 4, A.logical_shift_right)
+    ts(yi, pi, 7, A.bitwise_and)
+    tt(c("h16"), c("pi"), c("ai"), A.subtract)
+    cp(c("hif"), c("hx"))
+    tt(ap("wr", 0, 4), ai, ap("c16r", 0, 4), A.add)
+    cp(c("pf"), c("pi"))
+    ts(c("h16b"), c("h16"), 128.0, A.add)
+    ts(c("hi8"), c("hif"), 8.0, A.add)
+    hi, lo = c("hif"), c("wr")
+    for t, col in ((0, c("h16")), (1, c("h16b")), (2, lo), (3, lo)):
+        act(ap("ct", t, 512, 4), zb, bias=col)
+    act(c("ct", 512), c("zb"), bias=hi)
+    act(c("ct", 513), c("zb"), bias=c("hi8"))
+    act(ap("ct", 518, 520), ap("zb", 0, 2), bias=lo)
+    fill(ap("hb", 0, 128), 0.5)
+    o, i = ap("idn", 0, 128), ap("hb", 0, 128)
+    run("g", lambda q: q.affine_select(o["v"], i["v"], [[-1, 128]], A.is_equal, 0.0, 0, 1), [o], [i])
+    fill(ap("eb", 0, 528), 0.0)
+    iota("tsum", 64, [[1, 8], [1, 8]])
+    iota("ri", 64, [[0, 8], [1, 8]])
+    iota("c2", 4, [[2, 4]])
+    ts(ap("mask", 0, 128), ap("io", 0, 128), c("pf"), A.is_lt)
+    ts(c("corr"), lo, 512.0, A.mult, -7680.0, A.add)
+    fill(ap("vt", 128, 512), 0.0)
+    fill(ap("nzx", 256, 512), 0.0)
+    fill(ap("zf", 0, 32), 0.5)
+    fill(ap("lt4", 0, 512), 0.0)
+    for t in (0, 1, 2, 3):
+        if t < 2:
+            act(ap("ux", t, 512, 4), zb, bias=c("u4", t))
+        else:
+            ts(ap("ux", t, 512, 4), zb, c("u4", t), A.add)
+    quant("uq", 0, 128, "ux")
+
+    P0, P1, P2, P3 = 0, 512, 1024, 1536
+    quant("tq", 0, 128, "tbx")
+    mm(ap("pp", P1, P1 + 128), "tq", 0, "uq", 0, 128)
+    mm(ap("pp", P0, P0 + 128), "uq", 0, "tq", 0, 128)
+    quant("tq", 128, 256, "tbx", 512)
+    mm(ap("pp", P2, P2 + 128), "tq", 128, "uq", 0, 128)
+    mm(ap("pp", P3, P3 + 128), "uq", 0, "tq", 128, 256)
+    mm(ap("dv", 0, 256), "uq", 0, "tq", 0, 256)
+    rid, pid, _ = topo.addr(helpers[me])
+
+    def to_helper(n, o, sem):
+        ready("g", [n])
+        g.remote_dma(o["v"], n["v"], T.sem[sem], T.sem.lo, pid, rid, bits(out))
+        sent[0] += len(out)
+    to_helper(ap("tq", 0, 256, bc=u8), ap("hq", 0, 256, bc=u8), "h_c")
+    low, high = ap("pp", P0, P0 + 128), ap("pp", P3, P3 + 128)
+    s0, s1 = c("ss", 0), c("ss", 1)
+    for h, pk in ((0, P1), (1, P2)):
+        act(c("ss", h), c("pp", pk))
+        act(c("ds01", h), c("pp", pk), F.Abs, bias=2.0 ** -120, scale=0.7 * 2.0 ** -23)
+    quant("cq", 0, 256, "ct")
+    ts(ap("sm", 0, 128), ap("mask", 0, 128), c("ds01", 0), A.mult, s0, A.add)
+    act(ap("sm", 128, 256), ap("mask", 0, 128), bias=s1, scale=c("ds01", 1))
+    ts(ap("cmp", 0, 128), high, s0, A.is_lt)
+    ts(ap("cmp", 256, 384), low, s1, A.is_le)
+    tt(ap("cmp", 128, 256), low, ap("sm", 0, 128), A.is_lt)
+    tt(ap("cmp", 384, 512), high, ap("sm", 128, 256), A.is_lt)
+    act(ap("junk", 256, 384), ap("cmp", 256, 384), accum=c("pos", 1))
+    act(ap("junk", 0, 256), ap("cmp", 0, 256), accum=c("pos", 0))
+    act(ap("junk", 256, 512), ap("dv", 0, 256), F.Sign, bias=-2.0 ** -100, accum=c("ft"))
+    ts(ap("m16", 0, 256), ap("md16", 0, 256), lo, A.is_equal)
+    act(ap("wt", 0, 256), ap("m16", 0, 256), scale=-1000512.0, bias=512.0)
+    red(c("pos", 4), ap("cmp", 384, 512))
+    for t in (1, 3):
+        ts(ap("oh", t, 512, 4), ap("io64", 0, 128), c("pos", 1), A.subtract, c("pos", 4), A.is_equal)
+    for t in (0, 2):
+        ts(ap("oh", t, 512, 4), ap("io64", 0, 128), c("pos", 0), A.is_equal)
+    v = c("vl", 8 * slot)
+    ts(v, c("ft"), 256.0, A.add)
+    to_all(v, v, "a_v")
+    quant("oq", 0, 128, "oh")
+    mm(ap("dv", 512, 640), "oq", 0, "cq", 128, 256)
+    mm(ap("pp", P0, P0 + 128), "cq", 0, "oq", 0, 128)
+    ts(ap("bi", 0, 4), ai, 3, A.logical_shift_right)
+    cp(ap("lq7", 0, 4), yi)
+    ts(ap("gis", 0, 4), yi, -8.0, A.mult, 63.0, A.add)
+    ts(ap("in32", 0, 4), yi, 32.0, A.mult, 31.0, A.add)
+    act(ap("r8", 0, 64), ap("ri", 0, 64), F.Sign)
+    act(ap("eb", 3, 515, 4), ap("idn", 0, 128))
+    wrap("js", ap("pp", P0, P0 + 64), 64)
+    xx = ap("xx", 0, 4)
+    tt(xx, ap("bi", 0, 4), ap("c2", 0, 4), A.add)
+    listed("jl4", "js", 32)
+    pick("sp", 0, 32, "tq", 0, 256, "jl4", 0, 2)
+    listed("jl4", "js", 64, a=32)
+
+    to_all(ap("sp", 0, 32, bc=u8), ap("land", 32 * slot, 32 * slot + 32, bc=u8), "a_c")
+    to_all(ap("sps", 0, 32), ap("lands", 32 * slot, 32 * slot + 32), "a_s")
+    cp(ap("lt4", 0, 2), ap("dv", 512, 514))
+    quant("tq", 256, 384, "lt4")
+    to_helper(ap("tq", 256, 258, bc=u8), ap("hq", 256, 258, bc=u8), "h_l")
+    to_helper(ap("tqs", 0, 258), ap("hqs", 0, 258), "h_s")
+    move("land", 32 * slot, "sp", 0, 32)
+    move("cd", 0, "tq", 0, 128)
+
+    ts(ap("tie5", 0, 64), ap("tsum", 0, 64), 7.5, A.is_gt, -1.0, A.mult)
+    ts(ap("lrs", 0, 4), xx, -1.0, A.mult, 7.0, A.add)
+    pick("sp", 32, 64, "tq", 0, 256, "jl4", 2, 4)
+    move("xw", 128, "sp", 0, 64)
+    move("sl", 32 * slot, "tq", 32 * me, 32)
+    move("ll", 2 * slot, "tq", 256, 2)
+    move("ll", 16, "tq", 0, 112)
+    ts(ap("tie", 0, 64), ap("tie5", 0, 64), 0.5, A.add, 2.0, A.mult)
+    for b in range(4):
+        quant("eh", 128 * b, 128 * b + 128, "eb", 3 - b)
+    quant("nq", 0, 128, "nzx")
+    for b in range(4):
+        mm(ap("dv", 512 * b, 512 * b + 128), "eh", 128 * b, "nq", 0, 128, True, False)
+    fill(ap("wc", 0, 8), 32.0)
+    ts(ap("grs", 0, 4), xx, -8.0, A.mult, 63.0, A.add)
+    iota("l2i", 16, [[1, 8], [0, 2]])
+    iota("md32", 256, [[0, 8], [1, 32]])
+    iota("x32", 8, [[32, 8]], 256)
+    iota("p256", 64, [[1, 64]], 256)
+    iota("frow", 256, [[1, 256]])
+    act(ap("r32", 0, 256), ap("md32", 0, 256), F.Sign)
+
+    n8 = len(far) * len(out) + len(near) * len(inn)
+    arrive("vl", 0, 8 * slot, ("a_v", n8))
+    arrive("vl", 8 * slot + 8, 64, ("a_v", n8))
+    for k in ((0, 32 * slot), (32 * slot + 32, 256)):
+        arrive("land", k[0], k[1], ("a_c", n8))
+        arrive("lands", k[0], k[1], ("a_s", n8))
+    cp(ap("vi", 0, 8), ap("vl", 0, 64, 8))
+    ts(ap("ou32", 0, 4), xx, -32.0, A.mult, 255.0, A.add)
+    lq7, lrs, r8 = ap("lq7", 0, 4), ap("lrs", 0, 4), ap("r8", 0, 64)
+    tt(ap("k1", 0, 64), ap("vi", 0, 8, off=lrs), ap("tie", 0, 64), A.add)
+    tt(ap("cm", 0, 64), ap("vi", 0, 8, off=lq7), ap("k1", 0, 64), A.is_gt)
+    scan(ap("sc", 0, 64), r8, ap("cm", 0, 64))
+    ts(ap("fiti", 0, 8), ap("vi", 0, 8), 0.5, A.mult)
+    mine = c("sc", 8 * me + 7)
+    ts(ap("ms", 0, 8), ap("sc", 7, 64, 8), mine, A.add, 7.0, A.not_equal)
+    ts(c("go"), mine, 3.5, A.is_lt, 160.0, A.mult)
+    scan(ap("st", 0, 8), ap("wc", 0, 8), ap("ms", 0, 8), A.add, A.mult)
+    ts(ap("ofx", 0, 2), ap("wr", 0, 2), c("go"), A.add)
+    ts(ap("ofa", 0, 2), ap("wr", 0, 2), c("st", 7), A.add)
+    gi, grs = ap("gis", 0, 4), ap("grs", 0, 4)
+    act(ap("q0", 0, 64), ap("sc", 0, 64, off=grs), F.Abs, bias=-3.5)
+    pick("cd", 0, 32, "land", 0, 256, "ofa", 0, 2)
+    for b in range(4):
+        mm(ap("dv", 512 * b, 512 * b + 128), "eh", 128 * b, "cd", 0, 128, False, True)
+
+    def packed(vt, w, out, a):
+        for b in (0, 1, 2, 3):
+            o, i = ap(vt, b, 4 * w, 4), ap("dv", 512 * b, 512 * b + w)
+            if b % 2:
+                cp(o, i)
+            else:
+                act(o, i)
+        quant(out, a, a + 128, vt)
+    ts(ap("g0", 0, 64), ap("sc", 0, 64, off=gi), -1.0, A.mult, 3.5, A.add)
+    ts(ap("tie5", 0, 64), ap("tie5", 0, 64), 0.5, A.add)
+    ts(ap("gr", 0, 4), xx, 8.0, A.mult, 7.0, A.add)
+    tt(ap("hit", 0, 64), ap("g0", 0, 64), ap("q0", 0, 64), A.is_equal)
+    ts(ap("tks", 0, 8), ap("g0", 0, 8), 0.0, A.is_lt)
+    tt(ap("hf", 0, 64), ap("fiti", 0, 8, off=lq7), ap("hit", 0, 64), A.mult)
+    tt(ap("hh", 0, 64), ap("hit", 0, 64), ap("ri", 0, 64), A.mult)
+    packed("vt", 32, "xw", 0)
+    ts(ap("thr8", 0, 8), ap("tks", 0, 8), -1e29, A.mult, 1e29, A.add)
+    pick("xs", 0, 32, "xw", 0, 192, "ofx", 0, 2)
+
+    to_all(ap("xs", 0, 32, bc=u8), ap("cw", 32 * slot, 32 * slot + 32, bc=u8), "b_c")
+    to_all(ap("xss", 0, 32), ap("cws", 32 * slot, 32 * slot + 32), "b_s")
+    move("cw", 32 * slot, "xs", 0, 32)
+
+    move("cw", 256, "land", 0, 256)
+    move("cc", 64, "tq", 0, 64)
+    move("np", 64, "nq", 64, 64)
+    scan(ap("hfs", 0, 64), r8, ap("hf", 0, 64))
+    scan(ap("hhs", 0, 64), r8, ap("hh", 0, 64))
+    cp(ap("l256", 0, 16), ap("l2i", 0, 16))
+    act(ap("thr", 0, 256), ap("thr8", 0, 8, off=ap("l256", 0, 16)))
+    fh = ap("hfs", 7, 64, 8)
+    ts(ap("tmp", 0, 8), fh, -224.0, A.add, 0.0, A.max)
+    fill(ap("wh8", 0, 1), 0.0)
+    fill(ap("w0", 0, 1), 0.0)
+    tt(ap("wh8", 1, 8), ap("hhs", 7, 56, 8), ap("hhs", 15, 64, 8), A.subtract)
+    tt(ap("tmp2", 0, 8), ap("tmp", 0, 8), ap("tks", 0, 8), A.mult)
+    ts(ap("o0a", 0, 8), ap("tks", 0, 8), -256.0, A.mult)
+    ts(ap("wh", 0, 64), ap("wh8", 0, 8, off=lq7), 32.0, A.mult)
+    tt(ap("base1", 0, 8), fh, ap("tmp2", 0, 8), A.subtract)
+    ts(c("cola", 0), c("hhs", 63), 32.0, A.mult, c("wr", 0), A.add)
+    ts(c("cola", 1), c("hhs", 63), 32.0, A.mult, c("wr", 1), A.add)
+    tt(ap("dd", 0, 64), ap("base1", 0, 8, off=lrs), ap("tie5", 0, 64), A.add)
+    ts(c("cola", 2), c("hhs", 63), 32.0, A.mult)
+    tt(ap("o0", 0, 8), ap("o0a", 0, 8), ap("x32", 0, 8), A.add)
+    tt(ap("nd", 0, 64), ap("base1", 0, 8, off=lq7), ap("dd", 0, 64), A.subtract)
+    mm(ap("pp", P1, P1 + 256), "uq", 0, "land", 0, 256)
+    act(ap("sw", 256, 512), ap("pp", P1, P1 + 256))
+    for k in ((0, 2 * slot), (2 * slot + 2, 16)):
+        arrive("ll", k[0], k[1], ("l_c", n8))
+        arrive("lls", k[0], k[1], ("l_s", n8))
+    mm(ap("pp", P2, P2 + 128), "eh", 0, "ll", 0, 128)
+    mm(ap("pp", P3, P3 + 128), "eh", 128, "ll", 0, 128)
+    ts(ap("nh", 0, 8), ap("pp", P2, P2 + 16, 2), 32.0, A.mult)
+    ts(ap("nl", 0, 8), ap("pp", P3, P3 + 16, 2), 2.0, A.mult)
+    tt(ap("nj", 0, 8), ap("nh", 0, 8), ap("nl", 0, 8), A.add)
+    o, i = ap("jt", 0, 512, p=(0, 1)), ap("nj", 0, 8, p=(0, 64))
+    dma("y", o["v"], i["v"], [o], [i])
+    jr = ap("jr", 0, 512)
+    run("g", lambda q: q.partition_broadcast(jr["v"], o["v"], 128), [jr], [o])
+    ts(c("ei"), c("pi"), 31, A.bitwise_and)
+    tt(ap("w0", 1, 8), ap("o0", 0, 7), ap("o0", 1, 8), A.subtract)
+    fill(ap("ones", 0, 64), 1.0)
+    cp(c("ef"), c("ei"))
+    ts(ap("w256", 0, 4), ap("wr", 0, 4), 256.0, A.mult)
+    ts(c("corr32"), c("corr"), 32.0, A.add)
+    ts(ap("i32r", 0, 128), ap("md32", 0, 128), c("ef"), A.is_equal)
+    quant("wq", 0, 128, "wx")
+    fill(ap("vt2", 256, 512), 0.0)
+
+    def order_out(t):
+        scan(ap("odc", 0, 8), ap("ones", 0, 8), ap("ode", 0, 8), A.add, A.mult)
+        act(c("odr", t), c("odc", 7), scale=-1.0, bias=7.0)
+        x = ap("odr", t, t + 1, p=(0, 8))
+        dma("y", T.od[t:t + 1, 0:8], x["v"], [], [x])
+    ts(ap("ode", 0, 8), ap("sc", 7, 64, 8), c("pf"), A.not_equal)
+    order_out(0)
+
+    for k in ((0, 32 * slot), (32 * slot + 32, 256)):
+        arrive("cw", k[0], k[1], ("b_c", n8))
+        arrive("cws", k[0], k[1], ("b_s", n8))
+        arrive("sl", k[0], k[1], ("s_c", 7))
+        arrive("sls", k[0], k[1], ("s_s", 7))
+    mm(ap("pp", P0, P0 + 128), "uq", 0, "cw", 0, 128)
+    mm(ap("pp", P3, P3 + 128), "uq", 0, "cw", 128, 256)
+    for k, pk in ((0, P0), (128, P3)):
+        tt(ap("c1", k, k + 128), ap("pp", pk, pk + 128), ap("thr", k, k + 128), A.is_gt)
+    scan(ap("s1", 0, 256), ap("r32", 0, 256), ap("c1", 0, 256))
+    act(ap("x1b", 0, 64), ap("s1", 0, 256, off=ap("ou32", 0, 4)))
+    tt(ap("k1b", 0, 64), ap("s1", 0, 256, off=ap("in32", 0, 4)), ap("nd", 0, 64), A.add)
+    for k, pk in ((0, P0), (128, P3)):
+        act(ap("sw", k, k + 128), ap("pp", pk, pk + 128))
+    tt(ap("cmb", 0, 64), ap("x1b", 0, 64), ap("k1b", 0, 64), A.is_lt)
+    scan(ap("scb", 0, 64), r8, ap("cmb", 0, 64))
+    act(ap("q1", 0, 64), ap("scb", 0, 64, off=ap("gr", 0, 4)), F.Abs, bias=-3.5)
+    ts(ap("g1", 0, 64), ap("scb", 0, 64, off=gi), -1.0, A.mult, 3.5, A.add)
+    tt(ap("miss", 0, 64), ap("g1", 0, 64), ap("q1", 0, 64), A.not_equal)
+    ts(c("t32"), c("scb", 8 * me + 7), 3.5, A.is_gt, 32.0, A.mult)
+    scan(ap("bs", 0, 64), ap("wh", 0, 64), ap("miss", 0, 64), A.add, A.mult)
+    scan(ap("st0", 0, 8), ap("w0", 0, 8), ap("miss", 8 * me, 8 * me + 8), A.add, A.mult)
+    mh = 4 * (me // 4)
+    halves = (4 - mh, mh)
+    ts(ap("of", 0, 16, 2), ap("bs", 7, 64, 8), c("cola", 0), A.add)
+    ts(ap("of", 1, 16, 2), ap("bs", 7, 64, 8), c("cola", 1), A.add)
+    for r0 in halves:
+        pick("sb", 32 * r0, 32 * r0 + 128, "sl", 0, 256, "of", 2 * r0, 2 * r0 + 8)
+
+    for n, b, sem in (("sb", u8, "c_c"), ("sbs", None, "c_s")):
+        for r0 in halves:
+            to = [r for r in range(r0, r0 + 4) if r in far]
+            w = len(out) // len(to)
+            to = [(r, out[w * i:w * i + w]) for i, r in enumerate(to)] + [(r, inn) for r in near if r0 == mh]
+            ready("g", [ap(n, 32 * r0, 32 * r0 + 128)])
+            sent[0] += one_each(g, T, topo, to, lambda r: ap(n, 32 * r, 32 * r + 32, bc=b)["v"],
+                                ap("fw" + n[2:], 32 * me, 32 * me + 32, bc=b)["v"], T.sem[sem])
+    n3 = 4 * len(out) // 4 + 2 * len(out) // 2 + len(inn)
+    move("fw", 32 * me, "sb", 32 * me, 32)
+
+    tt(c("o1"), c("bs", 8 * me + 7), c("cola", 2), A.add)
+    ts(ap("ofc", 0, 2), ap("wr", 0, 2), c("st0", 7), A.add, c("o0", 7), A.add)
+    ts(ap("ofj", 0, 4), ap("w256", 0, 4), c("o1"), A.add, 1.0 / 32, A.mult)
+    ts(ap("ofc", 2, 4), ap("wr", 0, 2), c("o1"), A.add)
+    cs, cj, cr, tp = ap("csj", 0, 64), ap("csj", 64, 128), ap("cr", 0, 64), ap("tp", 0, 64)
+    cp(cj, ap("jr", 0, 512, off=ap("ofj", 0, 4)))
+    cp(cs, ap("sw", 0, 512, off=ap("ofc", 0, 4)))
+    tt(ap("dgo", 64, 128), cj, ap("i32r", 64, 128), A.mult)
+    tt(ap("dgo", 0, 64), cs, ap("i32r", 0, 64), A.mult)
+    wrap("jws", cj, 64)
+    scan(ap("ds", 0, 128), ap("r32", 0, 128), ap("dgo", 0, 128))
+    pick("cc", 0, 64, "cw", 0, 512, "ofc", 0, 4)
+    move("fw", 256, "cc", 0, 64)
+    for b in range(4):
+        mm(ap("dv", 512 * b, 512 * b + 128), "eh", 128 * b, "cc", 0, 128, True, False)
+    two = [(e, (64 * e, 64 * e + 64)) for e in (0, 1)]
+    for e, w in two:
+        act(ap("jl", *w), cj, F.Sign, bias=c("ds", 64 + 32 * e + 31), scale=-1.0)
+        ts(ap("eq", *w), cs, c("ds", 32 * e + 31), A.is_equal)
+    for e, w in two:
+        act(ap("lt", *w), cs, F.Sign, bias=c("ds", 32 * e + 31), scale=-1.0)
+        tt(ap("eqj", *w), ap("eq", *w), ap("jl", *w), A.mult)
+    listed("jw", "jws", 64)
+    for e, w in two:
+        scan(ap("cnt", *w), ap("lt", *w), ap("eqj", *w), A.add, A.add)
+    for e, w in two:
+        ts(ap("tp", 32 * e, 32 * e + 32), ap("zf", 0, 32), c("cnt", 64 * e + 63), A.mult, 31.5, A.add)
+    ts(ap("ode", 0, 8), ap("scb", 7, 64, 8), c("pf"), A.not_equal)
+    run("v", lambda q: q.transpose(cr["v"], tp["v"]), [cr], [tp])
+    order_out(1)
+    wrap("crw", cr, 64)
+    ts(ap("sel", 0, 64), cr, c("t32"), A.is_lt, 64.0, A.mult)
+    listed("pl", "crw", 64, "corr32")
+    tt(ap("off", 0, 64), ap("sel", 0, 64), ap("p256", 0, 64), A.add)
+    pick("np", 0, 64, "nq", 0, 128, "pl", 0, 4)
+    for b in range(4):
+        mm(ap("dv", 512 * b, 512 * b + 128), "eh", 128 * b, "np", 0, 128, False, True)
+    cp(ap("frow", 0, 256, off=ap("jw", 0, 4)), ap("off", 0, 64))
+    wrap("fs", ap("frow", 0, 256), 256)
+    packed("vt2", 64, "fw", 320)
+    listed("fl", "fs", 256)
+
+    for k in ((0, 32 * me), (32 * me + 32, 256)):
+        arrive("fw", k[0], k[1], ("c_c", n3))
+        arrive("fws", k[0], k[1], ("c_s", n3))
+    for k, pk in ((0, P2), (1, P3)):
+        pick("oq2", 128 * k, 128 * k + 128, "fw", 0, 448, "fl", 8 * k, 8 * k + 8)
+        mm(ap("pp", pk, pk + 128), "wq", 0, "oq2", 128 * k, 128 * k + 128)
+    x = ap("oq2", 0, 256, bc=u8)
+    dma("y", T.oc[:, 0:1024], x["v"], [], [x])
+    for k in range(4):
+        x = ap("oq2s", 0, 256, p=(32 * k, 32 * k + 4))
+        dma("y", T.osc[4 * k:4 * k + 4, 0:256], x["v"], [], [x])
+    act(ap("yo", 0, 128), ap("pp", P2, P2 + 128))
+    cp(ap("yo", 128, 256), ap("pp", P3, P3 + 128))
+    for k, q in ((0, "s"), (1, "y")):
+        x = ap("yo", 128 * k, 128 * k + 128)
+        dma(q, T.y[:, 128 * k:128 * k + 128], x["v"], [], [x])
+    finish()
+    g.wait_ge(T.sem.lo, sent[0])

@@ -29,10 +29,10 @@ def _bufs():
     parts("fconst", F32, hif=8, hi8=8, h16=8, h16b=8, wr=8, pf=8, c16r=8, c2=8, corr=8, corr32=8, wt=256)
     parts("fown", F32, ft=8, sm=256, pos=8, ss=8, ds01=8, js=64, junk=512)
     parts("flist", F32, xx=8, w256=8, tsum=64, tie5=64, tie=64, ri=64, ef=8, wc=8, x32=8,
-          ones=64, p256=64, tmp2=8, o0a=8, dd=64, nd=64, nl=8, nh=8, nj=8,
+          ones=16, p256=64, tmp2=8, o0a=8, dd=64, nd=64, nl=8, nh=8, nj=8,
           k1=64, cm=64, sc=64, ms=8, st=8, go=8, q0=64, g0=64, hit=64, hf=64, hfs=64, hh=64, hhs=64, tks=8, thr8=8,
-          thr=256, tmp=8, base1=8, wh8=8, w0=8, wh=64, cola=8, o0=8, sw=512, jr=512, ode=8, odc=8, odr=8,
-          k1b=64, x1b=64, cmb=64, scb=64, q1=64, g1=64, miss=64, bs=64, o1=8, st0=8, t32=8, csj=128, dgo=128,
+          thr=256, tmp=8, base1=8, wh8=8, w0=8, wh=64, cola=8, o0=8, sw=512, jr=512, ode=16, odc=16, odr=8,
+          k1b=64, x1b=64, cmb=64, scb=64, q1=64, g1=64, miss=64, bs=64, st0=8, t32=8, csj=128, dgo=128,
           ds=128, lt=128, eq=128, jl=128, eqj=128, cnt=128, tp=64, cr=64, crw=64, sel=64, zf=32,
           off=64, jws=64, frow=256, fs=256)
     b(F32, vi=8, fiti=8, jt=512, yo=256)
@@ -42,13 +42,14 @@ def _bufs():
           ofj=4, pl=4, jw=4, fl=16)
     q(uq=128, tq=384, nq=128, wq=128, eh=512, cq=256, oq=128, sp=64, land=256, cd=128, xw=192, xs=32, cw=512,
       sl=256, sb=256, cc=128, np=128, fw=448, oq2=256, hq=264, ll=128)
+    b(CODE, h3=128)
     SCRATCH["dv"] = ("psum", [128, 2048], F32)
     SCRATCH["pp"] = ("psum", [128, 2048], F32)
 
 
 _bufs()
 SEMAPHORES = ["cv", "cs", "ct_", "cg", "lo", "a_v", "a_c", "a_s", "b_c", "b_s", "c_c", "c_s", "s_c", "s_s", "h_c",
-              "h_s", "h_l", "l_c", "l_s"] + ["d%d" % i for i in range(48)]
+              "h_s", "h_l", "l_c", "l_s", "a_cf", "b_cf", "h_3"] + ["d%d" % i for i in range(48)]
 
 
 def find_helpers(T, topo):
@@ -71,8 +72,18 @@ def ways(core, T, topo, me):
     far = [r for r in range(len(T.cores)) if r != me and topo.chip(T.cores[r]) != topo.chip(core)]
     near = [r for r in range(len(T.cores)) if r != me and topo.chip(T.cores[r]) == topo.chip(core)]
     out = topo.engines(core, T.cores[far[0]])
-    inn = [e for e in topo.engines(core, T.cores[near[0]]) if e not in out][:2]
+    inn = [e for e in topo.engines(core, T.cores[near[0]]) if e not in out]
     return far, near, out, inn
+
+
+def taken_by(T, topo, d):
+    n = len(T.cores)
+    here = [r for r in range(n) if topo.chip(T.cores[r]) == topo.chip(T.cores[d])]
+    far = [r for r in range(n) if r not in here]
+    cut = len([r for r in far if r < here[0]])
+    if cut in (0, len(far)):
+        cut = len(far) // 2
+    return far[:cut] if d == here[0] else far[cut:]
 
 
 def dest(T, topo, r):
@@ -98,16 +109,21 @@ def hand_on(g, core, T, topo, r):
     c0, l0 = S * (len(T.cores) - 1 - r), 2 * (len(T.cores) - 1 - r)
     far, near, out, inn = ways(core, T, topo, r)
     to = [(s, out[i:i + 1]) for i, s in enumerate(far)] + [(s, inn[:1]) for s in near]
-    lists = [(far, out), (near, inn)]
-    g.wait_ge(T.sem.h_c, len(out))
+    lists = [(far, out), (near, inn[:2])]
+    g.wait_ge(T.sem.h_c, len(out) + len(inn))
     n = one_each(g, T, topo, to, lambda s: T.hq[:, S * s:S * s + S].bitcast(dt.uint8),
                  T.sl[:, c0:c0 + S].bitcast(dt.uint8), T.sem.s_c)
-    g.wait_ge(T.sem.h_l, len(out))
+    g.wait_ge(T.sem.h_l, len(inn))
     n += same_to_all(g, T, topo, lists, T.hq[:, 256:258].bitcast(dt.uint8), T.ll[:, l0:l0 + 2].bitcast(dt.uint8),
                      T.sem.l_c)
-    g.wait_ge(T.sem.h_s, len(out))
+    g.wait_ge(T.sem.h_s, len(inn))
     n += same_to_all(g, T, topo, lists, T.hqs[:, 256:258], T.lls[:, l0:l0 + 2], T.sem.l_s)
     n += one_each(g, T, topo, to, lambda s: T.hqs[:, S * s:S * s + S], T.sls[:, c0:c0 + S], T.sem.s_s)
+    r0, w = 4 - 4 * (r // 4), len(out) // 4
+    g.wait_ge(T.sem.h_3, len(inn))
+    n += one_each(g, T, topo, [(r0 + i, out[w * i:w * i + w]) for i in range(4)],
+                  lambda d: T.h3[:, S * (d - r0):S * (d - r0) + S].bitcast(dt.uint8),
+                  T.fw[:, S * r:S * r + S].bitcast(dt.uint8), T.sem.c_c)
     g.wait_ge(T.sem.lo, n)
 
 
@@ -184,11 +200,12 @@ def builder(g, T):
     def ready(q, ins):
         need(q, [], full(ins))
 
-    def finish():
-        for q in count:
-            wait("y", (sem[q], count[q]))
+    def finish(last=True):
         for k in range(dmas[0]):
             wait("y", ("d%d" % k, 16))
+        if last:
+            for q in count:
+                wait("y", (sem[q], count[q]))
     return ap, run, dma, arrive, ready, finish
 
 
@@ -203,6 +220,8 @@ def rank_program(g, core, T, topo):
     u8, u32 = dt.uint8, dt.uint32
     slot = 7 - me
     far, near, out, inn = ways(core, T, topo, me)
+    gates = [r for r in far if me in taken_by(T, topo, r)]
+    nv = len(far) * len(out) + len(near) * len(inn)
     sent = [0]
 
     def sca(x):
@@ -265,9 +284,24 @@ def rank_program(g, core, T, topo):
         o = ap(n, a, b)
         dma(q, o["v"], src, [o], [])
 
-    def to_all(src, dst, sem):
+    def to_all(src, dst, sem, ranks):
         ready("g", [src])
-        sent[0] += same_to_all(g, T, topo, [(far, out), (near, inn)], src["v"], dst["v"], T.sem[sem])
+        sent[0] += same_to_all(g, T, topo, [(ranks, out), (near, inn)], src["v"], dst["v"], T.sem[sem])
+
+    def slots(rs):
+        return 32 * (7 - rs[-1]), 32 * (8 - rs[0])
+
+    def pass_on(n, ex):
+        own, other = taken_by(T, topo, me), taken_by(T, topo, near[0])
+        tok = (ex + "_c", len(own) * len(out) + len(inn))
+        arrive(n, *slots(own), tok)
+        arrive(n, *slots(near), tok)
+        arrive(n, *slots(other), (ex + "_cf", len(inn)))
+        for rs in (own, near, other):
+            arrive(n + "s", *slots(rs), (ex + "_s", nv))
+        x = ap(n, *slots(own), bc=u8)
+        ready("g", [x])
+        sent[0] += same_to_all(g, T, topo, [(near, inn)], x["v"], x["v"], T.sem[ex + "_cf"])
 
     def c(n, k=0):
         return ap(n, k, k + 1)
@@ -342,11 +376,11 @@ def rank_program(g, core, T, topo):
     mm(ap("dv", 0, 256), "uq", 0, "tq", 0, 256)
     rid, pid, _ = topo.addr(helpers[me])
 
-    def to_helper(n, o, sem):
+    def to_helper(n, o, sem, engines):
         ready("g", [n])
-        g.remote_dma(o["v"], n["v"], T.sem[sem], T.sem.lo, pid, rid, bits(out))
-        sent[0] += len(out)
-    to_helper(ap("tq", 0, 256, bc=u8), ap("hq", 0, 256, bc=u8), "h_c")
+        g.remote_dma(o["v"], n["v"], T.sem[sem], T.sem.lo, pid, rid, bits(engines))
+        sent[0] += len(engines)
+    to_helper(ap("tq", 0, 256, bc=u8), ap("hq", 0, 256, bc=u8), "h_c", out + inn)
     low, high = ap("pp", P0, P0 + 128), ap("pp", P3, P3 + 128)
     s0, s1 = c("ss", 0), c("ss", 1)
     for h, pk in ((0, P1), (1, P2)):
@@ -371,7 +405,7 @@ def rank_program(g, core, T, topo):
         ts(ap("oh", t, 512, 4), ap("io64", 0, 128), c("pos", 0), A.is_equal)
     v = c("vl", 8 * slot)
     ts(v, c("ft"), 256.0, A.add)
-    to_all(v, v, "a_v")
+    to_all(v, v, "a_v", far)
     quant("oq", 0, 128, "oh")
     mm(ap("dv", 512, 640), "oq", 0, "cq", 128, 256)
     mm(ap("pp", P0, P0 + 128), "cq", 0, "oq", 0, 128)
@@ -388,50 +422,54 @@ def rank_program(g, core, T, topo):
     pick("sp", 0, 32, "tq", 0, 256, "jl4", 0, 2)
     listed("jl4", "js", 64, a=32)
 
-    to_all(ap("sp", 0, 32, bc=u8), ap("land", 32 * slot, 32 * slot + 32, bc=u8), "a_c")
-    to_all(ap("sps", 0, 32), ap("lands", 32 * slot, 32 * slot + 32), "a_s")
+    to_all(ap("sp", 0, 32, bc=u8), ap("land", 32 * slot, 32 * slot + 32, bc=u8), "a_c", gates)
+    to_all(ap("sps", 0, 32), ap("lands", 32 * slot, 32 * slot + 32), "a_s", far)
     cp(ap("lt4", 0, 2), ap("dv", 512, 514))
     quant("tq", 256, 384, "lt4")
-    to_helper(ap("tq", 256, 258, bc=u8), ap("hq", 256, 258, bc=u8), "h_l")
-    to_helper(ap("tqs", 0, 258), ap("hqs", 0, 258), "h_s")
+    to_helper(ap("tq", 256, 258, bc=u8), ap("hq", 256, 258, bc=u8), "h_l", inn)
+    to_helper(ap("tqs", 0, 258), ap("hqs", 0, 258), "h_s", inn)
     move("land", 32 * slot, "sp", 0, 32)
     move("cd", 0, "tq", 0, 128)
 
-    ts(ap("tie5", 0, 64), ap("tsum", 0, 64), 7.5, A.is_gt, -1.0, A.mult)
+    act(ap("tie", 0, 64), ap("tsum", 0, 64), F.Sign, bias=7.5, scale=-1.0)
+    act(ap("wc", 0, 8), ap("zb", 0, 8), bias=32.0)
     ts(ap("lrs", 0, 4), xx, -1.0, A.mult, 7.0, A.add)
     pick("sp", 32, 64, "tq", 0, 256, "jl4", 2, 4)
     move("xw", 128, "sp", 0, 64)
     move("sl", 32 * slot, "tq", 32 * me, 32)
     move("ll", 2 * slot, "tq", 256, 2)
     move("ll", 16, "tq", 0, 112)
-    ts(ap("tie", 0, 64), ap("tie5", 0, 64), 0.5, A.add, 2.0, A.mult)
+    act(ap("tie5", 0, 64), ap("tie", 0, 64), scale=0.5)
+    act(c("wh8"), c("zb"))
+    act(c("w0"), c("zb"))
+    act(ap("ones", 0, 16), ap("zb", 0, 16), bias=1.0)
+    act(c("corr32"), c("corr"), bias=32.0)
     for b in range(4):
         quant("eh", 128 * b, 128 * b + 128, "eb", 3 - b)
     quant("nq", 0, 128, "nzx")
     for b in range(4):
         mm(ap("dv", 512 * b, 512 * b + 128), "eh", 128 * b, "nq", 0, 128, True, False)
-    fill(ap("wc", 0, 8), 32.0)
     ts(ap("grs", 0, 4), xx, -8.0, A.mult, 63.0, A.add)
     iota("l2i", 16, [[1, 8], [0, 2]])
+    pass_on("land", "a")
     iota("md32", 256, [[0, 8], [1, 32]])
     iota("x32", 8, [[32, 8]], 256)
     iota("p256", 64, [[1, 64]], 256)
     iota("frow", 256, [[1, 256]])
-    act(ap("r32", 0, 256), ap("md32", 0, 256), F.Sign)
 
-    n8 = len(far) * len(out) + len(near) * len(inn)
-    arrive("vl", 0, 8 * slot, ("a_v", n8))
-    arrive("vl", 8 * slot + 8, 64, ("a_v", n8))
-    for k in ((0, 32 * slot), (32 * slot + 32, 256)):
-        arrive("land", k[0], k[1], ("a_c", n8))
-        arrive("lands", k[0], k[1], ("a_s", n8))
+    n8 = len(far) * len(out) + len(near) * 2
+    arrive("vl", 0, 8 * slot, ("a_v", nv))
+    arrive("vl", 8 * slot + 8, 64, ("a_v", nv))
     cp(ap("vi", 0, 8), ap("vl", 0, 64, 8))
     ts(ap("ou32", 0, 4), xx, -32.0, A.mult, 255.0, A.add)
     lq7, lrs, r8 = ap("lq7", 0, 4), ap("lrs", 0, 4), ap("r8", 0, 64)
     tt(ap("k1", 0, 64), ap("vi", 0, 8, off=lrs), ap("tie", 0, 64), A.add)
+    act(ap("fiti", 0, 8), ap("vi", 0, 8), scale=0.5)
+    ts(ap("gr", 0, 4), xx, 8.0, A.mult, 7.0, A.add)
     tt(ap("cm", 0, 64), ap("vi", 0, 8, off=lq7), ap("k1", 0, 64), A.is_gt)
+    ts(c("ei"), c("pi"), 31, A.bitwise_and)
     scan(ap("sc", 0, 64), r8, ap("cm", 0, 64))
-    ts(ap("fiti", 0, 8), ap("vi", 0, 8), 0.5, A.mult)
+    cp(c("ef"), c("ei"))
     mine = c("sc", 8 * me + 7)
     ts(ap("ms", 0, 8), ap("sc", 7, 64, 8), mine, A.add, 7.0, A.not_equal)
     ts(c("go"), mine, 3.5, A.is_lt, 160.0, A.mult)
@@ -440,6 +478,8 @@ def rank_program(g, core, T, topo):
     ts(ap("ofa", 0, 2), ap("wr", 0, 2), c("st", 7), A.add)
     gi, grs = ap("gis", 0, 4), ap("grs", 0, 4)
     act(ap("q0", 0, 64), ap("sc", 0, 64, off=grs), F.Abs, bias=-3.5)
+    act(ap("g0", 0, 64), ap("sc", 0, 64, off=gi), scale=-1.0, bias=3.5)
+    ts(ap("ode", 0, 8), ap("sc", 7, 64, 8), c("pf"), A.not_equal)
     pick("cd", 0, 32, "land", 0, 256, "ofa", 0, 2)
     for b in range(4):
         mm(ap("dv", 512 * b, 512 * b + 128), "eh", 128 * b, "cd", 0, 128, False, True)
@@ -452,9 +492,6 @@ def rank_program(g, core, T, topo):
             else:
                 act(o, i)
         quant(out, a, a + 128, vt)
-    ts(ap("g0", 0, 64), ap("sc", 0, 64, off=gi), -1.0, A.mult, 3.5, A.add)
-    ts(ap("tie5", 0, 64), ap("tie5", 0, 64), 0.5, A.add)
-    ts(ap("gr", 0, 4), xx, 8.0, A.mult, 7.0, A.add)
     tt(ap("hit", 0, 64), ap("g0", 0, 64), ap("q0", 0, 64), A.is_equal)
     ts(ap("tks", 0, 8), ap("g0", 0, 8), 0.0, A.is_lt)
     tt(ap("hf", 0, 64), ap("fiti", 0, 8, off=lq7), ap("hit", 0, 64), A.mult)
@@ -463,67 +500,53 @@ def rank_program(g, core, T, topo):
     ts(ap("thr8", 0, 8), ap("tks", 0, 8), -1e29, A.mult, 1e29, A.add)
     pick("xs", 0, 32, "xw", 0, 192, "ofx", 0, 2)
 
-    to_all(ap("xs", 0, 32, bc=u8), ap("cw", 32 * slot, 32 * slot + 32, bc=u8), "b_c")
-    to_all(ap("xss", 0, 32), ap("cws", 32 * slot, 32 * slot + 32), "b_s")
+    to_all(ap("xs", 0, 32, bc=u8), ap("cw", 32 * slot, 32 * slot + 32, bc=u8), "b_c", gates)
+    to_all(ap("xss", 0, 32), ap("cws", 32 * slot, 32 * slot + 32), "b_s", far)
+    pass_on("cw", "b")
     move("cw", 32 * slot, "xs", 0, 32)
 
     move("cw", 256, "land", 0, 256)
     move("cc", 64, "tq", 0, 64)
     move("np", 64, "nq", 64, 64)
-    scan(ap("hfs", 0, 64), r8, ap("hf", 0, 64))
-    scan(ap("hhs", 0, 64), r8, ap("hh", 0, 64))
-    cp(ap("l256", 0, 16), ap("l2i", 0, 16))
-    act(ap("thr", 0, 256), ap("thr8", 0, 8, off=ap("l256", 0, 16)))
-    fh = ap("hfs", 7, 64, 8)
-    ts(ap("tmp", 0, 8), fh, -224.0, A.add, 0.0, A.max)
-    fill(ap("wh8", 0, 1), 0.0)
-    fill(ap("w0", 0, 1), 0.0)
-    tt(ap("wh8", 1, 8), ap("hhs", 7, 56, 8), ap("hhs", 15, 64, 8), A.subtract)
-    tt(ap("tmp2", 0, 8), ap("tmp", 0, 8), ap("tks", 0, 8), A.mult)
-    ts(ap("o0a", 0, 8), ap("tks", 0, 8), -256.0, A.mult)
-    ts(ap("wh", 0, 64), ap("wh8", 0, 8, off=lq7), 32.0, A.mult)
-    tt(ap("base1", 0, 8), fh, ap("tmp2", 0, 8), A.subtract)
-    ts(c("cola", 0), c("hhs", 63), 32.0, A.mult, c("wr", 0), A.add)
-    ts(c("cola", 1), c("hhs", 63), 32.0, A.mult, c("wr", 1), A.add)
-    tt(ap("dd", 0, 64), ap("base1", 0, 8, off=lrs), ap("tie5", 0, 64), A.add)
-    ts(c("cola", 2), c("hhs", 63), 32.0, A.mult)
-    tt(ap("o0", 0, 8), ap("o0a", 0, 8), ap("x32", 0, 8), A.add)
-    tt(ap("nd", 0, 64), ap("base1", 0, 8, off=lq7), ap("dd", 0, 64), A.subtract)
-    mm(ap("pp", P1, P1 + 256), "uq", 0, "land", 0, 256)
-    act(ap("sw", 256, 512), ap("pp", P1, P1 + 256))
     for k in ((0, 2 * slot), (2 * slot + 2, 16)):
         arrive("ll", k[0], k[1], ("l_c", n8))
         arrive("lls", k[0], k[1], ("l_s", n8))
     mm(ap("pp", P2, P2 + 128), "eh", 0, "ll", 0, 128)
     mm(ap("pp", P3, P3 + 128), "eh", 128, "ll", 0, 128)
-    ts(ap("nh", 0, 8), ap("pp", P2, P2 + 16, 2), 32.0, A.mult)
+    mm(ap("pp", P1, P1 + 256), "uq", 0, "land", 0, 256)
+    scan(ap("hfs", 0, 64), r8, ap("hf", 0, 64))
+    scan(ap("hhs", 0, 64), r8, ap("hh", 0, 64))
+    cp(ap("l256", 0, 16), ap("l2i", 0, 16))
+    fh = ap("hfs", 7, 64, 8)
+    act(ap("tmp", 0, 8), fh, F.Relu, bias=-224.0)
+    act(ap("nh", 0, 8), ap("pp", P2, P2 + 16, 2), scale=32.0)
+    tt(ap("wh8", 1, 8), ap("hhs", 7, 56, 8), ap("hhs", 15, 64, 8), A.subtract)
     ts(ap("nl", 0, 8), ap("pp", P3, P3 + 16, 2), 2.0, A.mult)
+    tt(ap("tmp2", 0, 8), ap("tmp", 0, 8), ap("tks", 0, 8), A.mult)
     tt(ap("nj", 0, 8), ap("nh", 0, 8), ap("nl", 0, 8), A.add)
     o, i = ap("jt", 0, 512, p=(0, 1)), ap("nj", 0, 8, p=(0, 64))
     dma("y", o["v"], i["v"], [o], [i])
     jr = ap("jr", 0, 512)
     run("g", lambda q: q.partition_broadcast(jr["v"], o["v"], 128), [jr], [o])
-    ts(c("ei"), c("pi"), 31, A.bitwise_and)
+    z2, z1 = ap("vt2", 256, 512), ap("vt", 256, 512)
+    dma("y", z2["v"], z1["v"], [z2], [z1])
+    act(ap("o0a", 0, 8), ap("tks", 0, 8), scale=-256.0)
+    act(ap("thr", 0, 256), ap("thr8", 0, 8, off=ap("l256", 0, 16)))
+    act(ap("r32", 0, 256), ap("md32", 0, 256), F.Sign)
+    act(c("cola", 2), c("hhs", 63), scale=32.0)
+    act(ap("wh", 0, 64), ap("wh8", 0, 8, off=lq7), scale=32.0)
+    act(ap("cola", 0, 2), ap("wr", 0, 2), bias=c("cola", 2))
+    act(ap("w256", 0, 4), ap("wr", 0, 4), scale=256.0, bias=c("cola", 2))
+    act(ap("sw", 256, 512), ap("pp", P1, P1 + 256))
+    tt(ap("base1", 0, 8), fh, ap("tmp2", 0, 8), A.subtract)
+    ts(ap("i32r", 0, 64), ap("md32", 0, 64), c("ef"), A.is_equal)
+    tt(ap("dd", 0, 64), ap("base1", 0, 8, off=lrs), ap("tie5", 0, 64), A.add)
+    tt(ap("o0", 0, 8), ap("o0a", 0, 8), ap("x32", 0, 8), A.add)
+    tt(ap("nd", 0, 64), ap("base1", 0, 8, off=lq7), ap("dd", 0, 64), A.subtract)
     tt(ap("w0", 1, 8), ap("o0", 0, 7), ap("o0", 1, 8), A.subtract)
-    fill(ap("ones", 0, 64), 1.0)
-    cp(c("ef"), c("ei"))
-    ts(ap("w256", 0, 4), ap("wr", 0, 4), 256.0, A.mult)
-    ts(c("corr32"), c("corr"), 32.0, A.add)
-    ts(ap("i32r", 0, 128), ap("md32", 0, 128), c("ef"), A.is_equal)
     quant("wq", 0, 128, "wx")
-    fill(ap("vt2", 256, 512), 0.0)
-
-    def order_out(t):
-        scan(ap("odc", 0, 8), ap("ones", 0, 8), ap("ode", 0, 8), A.add, A.mult)
-        act(c("odr", t), c("odc", 7), scale=-1.0, bias=7.0)
-        x = ap("odr", t, t + 1, p=(0, 8))
-        dma("y", T.od[t:t + 1, 0:8], x["v"], [], [x])
-    ts(ap("ode", 0, 8), ap("sc", 7, 64, 8), c("pf"), A.not_equal)
-    order_out(0)
 
     for k in ((0, 32 * slot), (32 * slot + 32, 256)):
-        arrive("cw", k[0], k[1], ("b_c", n8))
-        arrive("cws", k[0], k[1], ("b_s", n8))
         arrive("sl", k[0], k[1], ("s_c", 7))
         arrive("sls", k[0], k[1], ("s_s", 7))
     mm(ap("pp", P0, P0 + 128), "uq", 0, "cw", 0, 128)
@@ -539,36 +562,38 @@ def rank_program(g, core, T, topo):
     scan(ap("scb", 0, 64), r8, ap("cmb", 0, 64))
     act(ap("q1", 0, 64), ap("scb", 0, 64, off=ap("gr", 0, 4)), F.Abs, bias=-3.5)
     ts(ap("g1", 0, 64), ap("scb", 0, 64, off=gi), -1.0, A.mult, 3.5, A.add)
-    tt(ap("miss", 0, 64), ap("g1", 0, 64), ap("q1", 0, 64), A.not_equal)
     ts(c("t32"), c("scb", 8 * me + 7), 3.5, A.is_gt, 32.0, A.mult)
+    tt(ap("miss", 0, 64), ap("g1", 0, 64), ap("q1", 0, 64), A.not_equal)
+    ts(ap("ode", 8, 16), ap("scb", 7, 64, 8), c("pf"), A.not_equal)
     scan(ap("bs", 0, 64), ap("wh", 0, 64), ap("miss", 0, 64), A.add, A.mult)
     scan(ap("st0", 0, 8), ap("w0", 0, 8), ap("miss", 8 * me, 8 * me + 8), A.add, A.mult)
     mh = 4 * (me // 4)
     halves = (4 - mh, mh)
     ts(ap("of", 0, 16, 2), ap("bs", 7, 64, 8), c("cola", 0), A.add)
     ts(ap("of", 1, 16, 2), ap("bs", 7, 64, 8), c("cola", 1), A.add)
+    mb = c("bs", 8 * me + 7)
+    ts(ap("ofj", 0, 4), ap("w256", 0, 4), mb, A.add, 1.0 / 32, A.mult)
     for r0 in halves:
         pick("sb", 32 * r0, 32 * r0 + 128, "sl", 0, 256, "of", 2 * r0, 2 * r0 + 8)
+        if r0 != mh:
+            ts(ap("ofc", 0, 2), ap("wr", 0, 2), c("st0", 7), A.add, c("o0", 7), A.add)
+            ts(ap("ofc", 2, 4), ap("cola", 0, 2), mb, A.add)
 
-    for n, b, sem in (("sb", u8, "c_c"), ("sbs", None, "c_s")):
-        for r0 in halves:
-            to = [r for r in range(r0, r0 + 4) if r in far]
-            w = len(out) // len(to)
-            to = [(r, out[w * i:w * i + w]) for i, r in enumerate(to)] + [(r, inn) for r in near if r0 == mh]
-            ready("g", [ap(n, 32 * r0, 32 * r0 + 128)])
-            sent[0] += one_each(g, T, topo, to, lambda r: ap(n, 32 * r, 32 * r + 32, bc=b)["v"],
-                                ap("fw" + n[2:], 32 * me, 32 * me + 32, bc=b)["v"], T.sem[sem])
+    to_helper(ap("sb", 32 * halves[0], 32 * halves[0] + 128, bc=u8), ap("h3", 0, 128, bc=u8), "h_3", inn)
+    for n, b, sem, r0 in (("sbs", None, "c_s", halves[0]), ("sb", u8, "c_c", mh), ("sbs", None, "c_s", mh)):
+        to = [r for r in range(r0, r0 + 4) if r in far]
+        w = len(out) // len(to)
+        to = [(r, out[w * i:w * i + w]) for i, r in enumerate(to)] + [(r, inn) for r in near if r0 == mh]
+        ready("g", [ap(n, 32 * r0, 32 * r0 + 128)])
+        sent[0] += one_each(g, T, topo, to, lambda r: ap(n, 32 * r, 32 * r + 32, bc=b)["v"],
+                            ap("fw" + n[2:], 32 * me, 32 * me + 32, bc=b)["v"], T.sem[sem])
     n3 = 4 * len(out) // 4 + 2 * len(out) // 2 + len(inn)
     move("fw", 32 * me, "sb", 32 * me, 32)
 
-    tt(c("o1"), c("bs", 8 * me + 7), c("cola", 2), A.add)
-    ts(ap("ofc", 0, 2), ap("wr", 0, 2), c("st0", 7), A.add, c("o0", 7), A.add)
-    ts(ap("ofj", 0, 4), ap("w256", 0, 4), c("o1"), A.add, 1.0 / 32, A.mult)
-    ts(ap("ofc", 2, 4), ap("wr", 0, 2), c("o1"), A.add)
     cs, cj, cr, tp = ap("csj", 0, 64), ap("csj", 64, 128), ap("cr", 0, 64), ap("tp", 0, 64)
     cp(cj, ap("jr", 0, 512, off=ap("ofj", 0, 4)))
     cp(cs, ap("sw", 0, 512, off=ap("ofc", 0, 4)))
-    tt(ap("dgo", 64, 128), cj, ap("i32r", 64, 128), A.mult)
+    tt(ap("dgo", 64, 128), cj, ap("i32r", 0, 64), A.mult)
     tt(ap("dgo", 0, 64), cs, ap("i32r", 0, 64), A.mult)
     wrap("jws", cj, 64)
     scan(ap("ds", 0, 128), ap("r32", 0, 128), ap("dgo", 0, 128))
@@ -588,9 +613,13 @@ def rank_program(g, core, T, topo):
         scan(ap("cnt", *w), ap("lt", *w), ap("eqj", *w), A.add, A.add)
     for e, w in two:
         ts(ap("tp", 32 * e, 32 * e + 32), ap("zf", 0, 32), c("cnt", 64 * e + 63), A.mult, 31.5, A.add)
-    ts(ap("ode", 0, 8), ap("scb", 7, 64, 8), c("pf"), A.not_equal)
+    scan(ap("odc", 0, 16), ap("ones", 0, 16), ap("ode", 0, 16), A.add, A.mult)
     run("v", lambda q: q.transpose(cr["v"], tp["v"]), [cr], [tp])
-    order_out(1)
+    finish(False)
+    act(ap("odr", 0, 2), ap("odc", 7, 16, 8), scale=-1.0, bias=7.0)
+    for t in (0, 1):
+        x = ap("odr", t, t + 1, p=(0, 8))
+        dma("y", T.od[t:t + 1, 0:8], x["v"], [], [x])
     wrap("crw", cr, 64)
     ts(ap("sel", 0, 64), cr, c("t32"), A.is_lt, 64.0, A.mult)
     listed("pl", "crw", 64, "corr32")
@@ -611,13 +640,18 @@ def rank_program(g, core, T, topo):
         mm(ap("pp", pk, pk + 128), "wq", 0, "oq2", 128 * k, 128 * k + 128)
     x = ap("oq2", 0, 256, bc=u8)
     dma("y", T.oc[:, 0:1024], x["v"], [], [x])
-    for k in range(4):
+
+    def scales_out(k, q):
         x = ap("oq2s", 0, 256, p=(32 * k, 32 * k + 4))
-        dma("y", T.osc[4 * k:4 * k + 4, 0:256], x["v"], [], [x])
+        dma(q, T.osc[4 * k:4 * k + 4, 0:256], x["v"], [], [x])
+    scales_out(0, "y")
+    scales_out(1, "y")
     act(ap("yo", 0, 128), ap("pp", P2, P2 + 128))
     cp(ap("yo", 128, 256), ap("pp", P3, P3 + 128))
     for k, q in ((0, "s"), (1, "y")):
         x = ap("yo", 128 * k, 128 * k + 128)
         dma(q, T.y[:, 128 * k:128 * k + 128], x["v"], [], [x])
+    scales_out(2, "s")
+    scales_out(3, "s")
     finish()
     g.wait_ge(T.sem.lo, sent[0])

@@ -5,6 +5,22 @@ A = AluOpType
 F = ActivationFunctionType
 CODE, PLANE, F32, BF, I32, U16 = "float8_e4m3fn_x4", "uint8", "float32", "bfloat16", "int32", "uint16"
 SCRATCH, PART = {}, {}
+TINY = 2.0 ** -100
+ORDER = [0, 1, 5, 24, 2, 4, 3, 6, 19, 7, 21, 44, 23, 31, 26, 30, 29, 10, 20, 38, 43, 8, 36, 40, 33, 35, 45, 76, 79, 78,
+         77, 83, 82, 86, 80, 84, 88, 81, 87, 98, 92, 85, 94, 32, 102, 100, 46, 99, 34, 37, 101, 138, 95, 106, 96, 74,
+         97, 111, 89, 93, 103, 105, 109, 112, 110, 104, 115, 114, 113, 107, 116, 62, 108, 39, 117, 121, 143, 118, 139,
+         119, 27, 120, 128, 122, 129, 130, 41, 65, 47, 131, 123, 147, 145, 151, 22, 124, 25, 152, 141, 42, 144, 125,
+         184, 149, 153, 140, 126, 127, 132, 154, 185, 142, 15, 155, 187, 135, 18, 188, 156, 136, 193, 90, 190, 137,
+         158, 9, 91, 189, 157, 176, 161, 160, 14, 134, 200, 192, 17, 166, 159, 168, 133, 164, 177, 167, 169, 162, 191,
+         165, 163, 150, 68, 170, 13, 171, 172, 178, 205, 194, 173, 179, 51, 63, 174, 195, 75, 11, 146, 186, 70, 52,
+         181, 48, 72, 196, 56, 55, 202, 71, 197, 180, 148, 175, 198, 201, 183, 28, 59, 64, 182, 60, 49, 203, 16, 204,
+         199, 210, 69, 61, 53, 206, 73, 207, 212, 211, 229, 12, 213, 228, 214, 230, 50, 233, 216, 215, 234, 231, 209,
+         235, 217, 208, 218, 66, 219, 276, 264, 277, 220, 278, 232, 221, 54, 279, 224, 222, 223, 242, 241, 227, 240,
+         226, 255, 271, 237, 243, 244, 236, 256, 67, 272, 245, 246, 251, 257, 57, 247, 258, 253, 273, 248, 249, 259,
+         274, 250, 260, 225, 252, 58, 261, 265, 254, 239, 266, 262, 267, 263, 268, 275, 238, 270, 269, 288, 287, 282,
+         281, 290, 289, 280, 296, 293, 291, 295, 283, 284, 292, 285, 294, 286]
+SCALAR = (58, 62, 63, 64, 65, 67, 76, 80, 113, 120, 129, 134, 144, 146, 148, 150, 152, 161, 169, 172, 181, 190, 198,
+          202, 204, 205, 207, 208, 215, 227, 229, 232, 235, 239, 244, 248, 250, 255, 270, 278, 282, 288)
 
 
 def _bufs():
@@ -23,33 +39,31 @@ def _bufs():
         for k in kw:
             SCRATCH[k] = ("sbuf", [128, kw[k]], CODE)
             SCRATCH[k + "s"] = ("sbuf", [128, kw[k]], PLANE)
-    b(BF, tbx=1024, nzx=512, wx=512, ux=512, u4=8, eb=528, ct=1024, oh=512, vt=512, vt2=512, zb=128, hb=128, idn=128,
-      lt4=512, cmp=512, c1=256, s1=256)
-    parts("bconst", BF, m16=256, md16=256, r8=64, r32=256, md32=256, io=128, io64=128, mask=128, i32r=128)
-    parts("fconst", F32, hif=8, hi8=8, h16=8, h16b=8, wr=8, pf=8, c16r=8, c2=8, corr=8, corr32=8, wt=256)
-    parts("fown", F32, ft=8, sm=256, pos=8, ss=8, ds01=8, js=64, junk=512)
-    parts("flist", F32, xx=8, w256=8, tsum=64, tie5=64, tie=64, ri=64, ef=8, wc=8, x32=8,
-          ones=16, p256=64, tmp2=8, o0a=8, dd=64, nd=64, nl=8, nh=8, nj=8,
-          k1=64, cm=64, sc=64, ms=8, st=8, go=8, q0=64, g0=64, hit=64, hf=64, hfs=64, hh=64, hhs=64, tks=8, thr8=8,
-          thr=256, tmp=8, base1=8, wh8=8, w0=8, wh=64, cola=8, o0=8, sw=512, jr=512, ode=16, odc=16, odr=8,
-          k1b=64, x1b=64, cmb=64, scb=64, q1=64, g1=64, miss=64, bs=64, st0=8, t32=8, csj=128, dgo=128,
-          ds=128, lt=128, eq=128, jl=128, eqj=128, cnt=128, tp=64, cr=64, crw=64, sel=64, zf=32,
-          off=64, jws=64, frow=256, fs=256)
-    b(F32, vi=8, fiti=8, jt=512, yo=256)
-    parts("iconst", I32, pi=8, hx=8, ai=8, yi=8, ei=8, bi=8, l2i=16)
+    parts("big", BF, vt2=256, vt=128, lt=8, xt=16, nzx=256, wx=512)
+    b(BF, tbx=1024, ux=1024, u4=8, eb=528, oh=512, oh2=512, w4t=512, zb=128, cmp=256, junk=512, c1=272, s1=272)
+    parts("bconst", BF, io=128, tie=128, k2=256, qd4=128, m16=128, r34=272)
+    parts("fconst", F32, lo=8, pf=8, lo256=8, lom=8, q4f=8, qq4=8, ind4=8, corr=8, corr4=8, c4=16,
+          wt4=16, idx=16, c4x=8, c256=8, c32=8, xr=32, c35=32, rs8=64, m32=64, odw=16, gx0=8, p256=64, wt=128)
+    parts("fown", F32, ft=8, ss=8, s64=8, sa=256)
+    b(F32, jv=32, gb=96, cj=64, ntie=64, dn=256, dc=256, vi=8, yo=256, frow=256)
+    parts("flist", F32, k1=64, cm=64, sc=64, ms=8, st0=8, go=8, q0=64, miss0=64, fd=8, fde=64, hfs=64, hhs=64,
+          tk=8, ba=8, bb=8, bc=8, bd=8, kb=8, kx=64, nd=64, mi=32, st4=32, vv=40, ve=64, o1=8, kk=8,
+          k1b=64, x1b=64, cmb=64, scb=64, qx=64, miss=64, bs=64, t128=8, sel=16, off=16, xs=16,
+          ode=16, odc=16, odr=8, fs=256)
+    parts("iconst", I32, pi=8, pj=8, hi2=8, lo2=8, yx=8, bi=8, jc=8, hf=8, qi=8)
+    parts("ilist", I32, vint=8, fit8=16, kr=8)
     b(U16, vl=64)
-    parts("lists", U16, jl4=4, in32=4, ou32=4, lrs=4, lq7=4, grs=4, gr=4, gis=4, l256=16, ofa=2, ofx=2, of=16, ofc=4,
-          ofj=4, pl=4, jw=4, fl=16)
-    q(uq=128, tq=384, nq=128, wq=128, eh=512, cq=256, oq=128, sp=64, land=256, cd=128, xw=192, xs=32, cw=512,
-      sl=256, sb=256, cc=128, np=128, fw=448, oq2=256, hq=264, ll=128)
-    b(CODE, h3=128)
+    parts("lists", U16, jl4=4, l1=8, l8=8, l34=8, gx=4, lll=2, ofa=2, ofx=2, ofs=8, of=16,
+          ofc=4, jl=8, jw=16, l4=16, xl=4, fl=16)
+    q(uq=256, tq=256, xq=128, oq=256, lq=128, eh=512, lw=528, xw=160, cn=192, wl=144, sl=256, st=256, sb=192,
+      fw=320, oq2=256, w4q=128, cx=128, hq=256)
     SCRATCH["dv"] = ("psum", [128, 2048], F32)
     SCRATCH["pp"] = ("psum", [128, 2048], F32)
 
 
 _bufs()
 SEMAPHORES = ["cv", "cs", "ct_", "cg", "lo", "a_v", "a_c", "a_s", "b_c", "b_s", "c_c", "c_s", "s_c", "s_s", "h_c",
-              "h_s", "h_l", "l_c", "l_s", "a_cf", "b_cf", "h_3"] + ["d%d" % i for i in range(48)]
+              "h_s", "p_c", "p_s", "a_cf", "b_cf"] + ["d%d" % i for i in range(32)]
 
 
 def find_helpers(T, topo):
@@ -68,22 +82,23 @@ def bits(engines):
     return sum(1 << e for e in engines)
 
 
+def chip_ranks(T, topo, r):
+    return [x for x in range(len(T.cores)) if topo.chip(T.cores[x]) == topo.chip(T.cores[r])]
+
+
 def ways(core, T, topo, me):
-    far = [r for r in range(len(T.cores)) if r != me and topo.chip(T.cores[r]) != topo.chip(core)]
-    near = [r for r in range(len(T.cores)) if r != me and topo.chip(T.cores[r]) == topo.chip(core)]
+    n, here = len(T.cores), chip_ranks(T, topo, me)
+    far = [(here[-1] + 1 + i) % n for i in range(n - len(here))]
+    near = [r for r in here if r != me]
     out = topo.engines(core, T.cores[far[0]])
     inn = [e for e in topo.engines(core, T.cores[near[0]]) if e not in out]
     return far, near, out, inn
 
 
 def taken_by(T, topo, d):
-    n = len(T.cores)
-    here = [r for r in range(n) if topo.chip(T.cores[r]) == topo.chip(T.cores[d])]
-    far = [r for r in range(n) if r not in here]
-    cut = len([r for r in far if r < here[0]])
-    if cut in (0, len(far)):
-        cut = len(far) // 2
-    return far[:cut] if d == here[0] else far[cut:]
+    n, here = len(T.cores), chip_ranks(T, topo, d)
+    far = [(here[-1] + 1 + i) % n for i in range(n - len(here))]
+    return far[:len(far) // 2] if d == here[0] else far[len(far) // 2:]
 
 
 def dest(T, topo, r):
@@ -93,45 +108,54 @@ def dest(T, topo, r):
 
 def one_each(g, T, topo, to, src, dst, sem):
     g.remote_dma_fused([RemoteDMATransfer(dst_ids=[dest(T, topo, r)], dma_engine_mask=bits(e), remote_sem=sem,
-                                          src=src(r), dst=dst) for r, e in to], local_sem=T.sem.lo)
+                                          src=src(r), dst=dst(r)) for r, e in to], local_sem=T.sem.lo)
     return sum(len(e) for _, e in to)
 
 
 def same_to_all(g, T, topo, to, src, dst, sem):
     g.remote_dma_fused([RemoteDMATransfer(dst_ids=[dest(T, topo, r) for r in rs], dma_engine_mask=bits(e),
-                                          remote_sem=sem, srcs=[src], dsts=[dst] * len(rs)) for rs, e in to],
+                                          remote_sem=sem, srcs=[src], dsts=[dst(r) for r in rs]) for rs, e in to],
                        local_sem=T.sem.lo)
     return sum(len(e) for _, e in to)
 
 
-def hand_on(g, core, T, topo, r):
-    S = 32
-    c0, l0 = S * (len(T.cores) - 1 - r), 2 * (len(T.cores) - 1 - r)
+def slice_plan(core, T, topo, r):
     far, near, out, inn = ways(core, T, topo, r)
-    to = [(s, out[i:i + 1]) for i, s in enumerate(far)] + [(s, inn[:1]) for s in near]
-    lists = [(far, out), (near, inn[:2])]
-    g.wait_ge(T.sem.h_c, len(out) + len(inn))
-    n = one_each(g, T, topo, to, lambda s: T.hq[:, S * s:S * s + S].bitcast(dt.uint8),
-                 T.sl[:, c0:c0 + S].bitcast(dt.uint8), T.sem.s_c)
-    g.wait_ge(T.sem.h_l, len(inn))
-    n += same_to_all(g, T, topo, lists, T.hq[:, 256:258].bitcast(dt.uint8), T.ll[:, l0:l0 + 2].bitcast(dt.uint8),
-                     T.sem.l_c)
-    g.wait_ge(T.sem.h_s, len(inn))
-    n += same_to_all(g, T, topo, lists, T.hqs[:, 256:258], T.lls[:, l0:l0 + 2], T.sem.l_s)
-    n += one_each(g, T, topo, to, lambda s: T.hqs[:, S * s:S * s + S], T.sls[:, c0:c0 + S], T.sem.s_s)
-    r0, w = 4 - 4 * (r // 4), len(out) // 4
-    g.wait_ge(T.sem.h_3, len(inn))
-    n += one_each(g, T, topo, [(r0 + i, out[w * i:w * i + w]) for i in range(4)],
-                  lambda d: T.h3[:, S * (d - r0):S * (d - r0) + S].bitcast(dt.uint8),
-                  T.fw[:, S * r:S * r + S].bitcast(dt.uint8), T.sem.c_c)
-    g.wait_ge(T.sem.lo, n)
+    k = len(out) - len(far)
+    codes = [(s, out[2 * i:2 * i + 2]) for i, s in enumerate(far[:k])] + \
+            [(s, out[2 * k + i:2 * k + i + 1]) for i, s in enumerate(far[k:])]
+    m = len(far) - k
+    scales = [(s, out[i:i + 1]) for i, s in enumerate(far[:m])] + \
+             [(s, out[m + 2 * i:m + 2 * i + 2]) for i, s in enumerate(far[m:])]
+    return codes + [(s, inn[:2]) for s in near], scales + [(s, inn[2:4]) for s in near]
+
+
+def hand_on(g, core, T, topo, r):
+    S, n = 32, len(T.cores)
+    far, near, out, inn = ways(core, T, topo, r)
+    codes, scales = slice_plan(core, T, topo, r)
+    g.wait_ge(T.sem.h_c, len(out) + len(inn) + len(inn) // 2)
+    k = one_each(g, T, topo, codes, lambda s: T.hq[:, S * s:S * s + S].bitcast(dt.uint8),
+                 lambda s: T.sl[:, S * ((r - s) % n):S * ((r - s) % n) + S].bitcast(dt.uint8), T.sem.s_c)
+    g.wait_ge(T.sem.h_s, len(inn) // 2)
+    k += one_each(g, T, topo, scales, lambda s: T.hqs[:, S * s:S * s + S],
+                  lambda s: T.sls[:, S * ((r - s) % n):S * ((r - s) % n) + S], T.sem.s_s)
+    g.wait_ge(T.sem.lo, k)
+
+
+def apart(x, y):
+    if x["n"] in ("dv", "pp"):
+        return x["a"] // 512 != y["a"] // 512
+    if x["a"] >= y["b"] or y["a"] >= x["b"]:
+        return True
+    return x["st"] == y["st"] and x["st"] > 1 and (x["a"] - y["a"]) % x["st"] != 0
 
 
 def builder(g, T):
     queue = {"v": g.vector, "s": g.scalar, "t": g.tensor, "g": g, "y": g.sync}
     sem = {"v": "cv", "s": "cs", "t": "ct_", "g": "cg"}
     count = {"v": 0, "s": 0, "t": 0, "g": 0}
-    seen, log, dmas = {}, {}, [0]
+    seen, log, dmas, steps = {}, {}, [0], []
 
     def ap(n, a, b, st=1, p=None, bc=None, off=None):
         n, k = PART.get(n, (n, 0))
@@ -143,13 +167,6 @@ def builder(g, T):
         if off is not None:
             v = v.indirect(off["v"])
         return {"v": v, "n": n, "a": a, "b": b, "st": st, "off": off}
-
-    def apart(x, y):
-        if x["n"] in ("dv", "pp"):
-            return x["a"] // 512 != y["a"] // 512
-        if x["a"] >= y["b"] or y["a"] >= x["b"]:
-            return True
-        return x["st"] == y["st"] and x["st"] > 1 and (x["a"] - y["a"]) % x["st"] != 0
 
     def wait(q, tok):
         if seen.get((q, tok[0]), 0) < tok[1]:
@@ -176,37 +193,37 @@ def builder(g, T):
             for x in xs:
                 log.setdefault(x["n"], []).append((x, w, q, tok))
 
-    def full(xs):
-        return [x for x in xs if x] + [x["off"] for x in xs if x and x["off"]]
-
-    def run(q, fn, outs, ins):
-        ins = full(ins) + [x["off"] for x in outs if x["off"]]
-        need(q, outs, ins)
-        count[q] += 1
-        fn(queue[q]).then_inc(T.sem[sem[q]], 1)
-        note(q, outs, ins, (sem[q], count[q]))
-
-    def dma(q, out, in_, outs, ins):
-        need(q, outs, ins)
-        s = "d%d" % dmas[0]
-        dmas[0] += 1
-        queue[q].dma_start(out, in_).then_inc(T.sem[s], 16)
-        note("dma", outs, ins, (s, 16))
+    def step(kind, q, fn, outs, ins, other=None):
+        ins = [x for x in ins if x] + [x["off"] for x in ins + outs if x and x["off"]]
+        steps.append((kind, q, fn, outs, ins, other))
 
     def arrive(n, a, b, tok):
         x = {"n": n, "a": a, "b": b, "st": 1, "off": None}
         log.setdefault(n, []).append((x, True, "far", tok))
 
-    def ready(q, ins):
-        need(q, [], full(ins))
-
-    def finish(last=True):
-        for k in range(dmas[0]):
-            wait("y", ("d%d" % k, 16))
-        if last:
-            for q in count:
-                wait("y", (sem[q], count[q]))
-    return ap, run, dma, arrive, ready, finish
+    def issue():
+        order = ORDER or range(len(steps))
+        assert sorted(order) == list(range(len(steps)))
+        for k in order:
+            kind, q, fn, outs, ins, other = steps[k]
+            if k in SCALAR:
+                q, fn = "s", other
+            need(q, outs, ins)
+            if kind == "c":
+                count[q] += 1
+                fn(queue[q]).then_inc(T.sem[sem[q]], 1)
+                note(q, outs, ins, (sem[q], count[q]))
+            elif kind == "d":
+                s = "d%d" % dmas[0]
+                dmas[0] += 1
+                fn(queue[q]).then_inc(T.sem[s], 16)
+                note("dma", outs, ins, (s, 16))
+            else:
+                fn(g)
+        for tok in [(sem[q], count[q]) for q in count] + [("d%d" % k, 16) for k in range(dmas[0])]:
+            if max(seen.get((q, tok[0]), 0) for q in queue) < tok[1]:
+                wait("y", tok)
+    return ap, step, arrive, issue
 
 
 def rank_program(g, core, T, topo):
@@ -216,13 +233,16 @@ def rank_program(g, core, T, topo):
         if core in helpers:
             hand_on(g, core, T, topo, helpers.index(core))
         return
-    ap, run, dma, arrive, ready, finish = builder(g, T)
+    ap, step, arrive, issue = builder(g, T)
     u8, u32 = dt.uint8, dt.uint32
-    slot = 7 - me
+    N = len(T.cores)
     far, near, out, inn = ways(core, T, topo, me)
+    here = chip_ranks(T, topo, me)
     gates = [r for r in far if me in taken_by(T, topo, r)]
+    like = [r for r in far if chip_ranks(T, topo, r).index(r) == here.index(me)]
+    assert [(r - me) % N for r in like] == [2, 4, 6] and here[1] == here[0] + 1
     nv = len(far) * len(out) + len(near) * len(inn)
-    sent = [0]
+    sent = []
 
     def sca(x):
         return x["v"] if isinstance(x, dict) else x
@@ -232,90 +252,104 @@ def rank_program(g, core, T, topo):
 
     def ts(out, in0, s1, op0, s2=None, op1=None):
         if op1 is None:
-            run("v", lambda q: q.tensor_scalar(out["v"], in0["v"], sca(s1), None, op0), [out], dic(in0, s1))
+            step("c", "v", lambda q: q.tensor_scalar(out["v"], in0["v"], sca(s1), None, op0), [out], dic(in0, s1))
         else:
-            run("v", lambda q: q.tensor_scalar(out["v"], in0["v"], sca(s1), sca(s2), op0, op1), [out],
-                dic(in0, s1, s2))
+            step("c", "v", lambda q: q.tensor_scalar(out["v"], in0["v"], sca(s1), sca(s2), op0, op1), [out],
+                 dic(in0, s1, s2))
 
     def tt(out, in0, in1, op):
-        run("v", lambda q: q.tensor_tensor(out["v"], in0["v"], in1["v"], op), [out], [in0, in1])
+        step("c", "v", lambda q: q.tensor_tensor(out["v"], in0["v"], in1["v"], op), [out], [in0, in1])
 
     def scan(out, d0, d1, op0=A.mult, op1=A.add):
-        run("v", lambda q: q.tensor_tensor_scan(out["v"], d0["v"], d1["v"], 0.0, op0, op1), [out], [d0, d1])
+        step("c", "v", lambda q: q.tensor_tensor_scan(out["v"], d0["v"], d1["v"], 0.0, op0, op1), [out], [d0, d1])
 
     def cp(out, in_):
-        run("v", lambda q: q.tensor_copy(out["v"], in_["v"]), [out], [in_])
+        step("c", "v", lambda q: q.tensor_copy(out["v"], in_["v"]), [out], [in_])
 
     def fill(out, c):
-        run("v", lambda q: q.memset(out["v"], c), [out], [])
+        step("c", "v", lambda q: q.memset(out["v"], c), [out], [])
 
-    def red(out, in_):
-        run("v", lambda q: q.tensor_reduce(out["v"], in_["v"], AxisListType.X, A.add), [out], [in_])
-
-    def act(out, in_, func=None, bias=0.0, scale=1.0, accum=None):
-        plain = not dic(bias, scale) and bias == 0.0 and scale == 1.0
-        func = func or (F.Copy if plain else F.Identity)
-        kw = {} if plain else {"bias": sca(bias), "scale": sca(scale)}
+    def act(out, in_, func, bias=0.0, scale=1.0, accum=None):
+        kw = {} if func == F.Copy else {"bias": bias, "scale": scale}
         if accum:
             kw["accum_out"] = accum["v"]
-        run("s", lambda q: q.activation(out["v"], in_["v"], func, **kw), [out] + dic(accum), [in_] + dic(bias, scale))
+        step("c", "s", lambda q: q.activation(out["v"], in_["v"], func, **kw), [out] + dic(accum), [in_])
+
+    def aff(out, in_, scale=1.0, bias=0.0):
+        if scale == 1.0 and not dic(bias) and bias == 0.0:
+            step("c", "v", lambda q: q.tensor_copy(out["v"], in_["v"]), [out], [in_],
+                 lambda q: q.activation(out["v"], in_["v"], F.Copy))
+        else:
+            step("c", "v", lambda q: q.tensor_scalar(out["v"], in_["v"], scale, sca(bias), A.mult, A.add), [out],
+                 dic(in_, bias), lambda q: q.activation(out["v"], in_["v"], F.Identity, bias=sca(bias), scale=scale))
 
     def quant(n, a, b, tile, x0=0):
         o, p, x = ap(n, a, b), ap(n + "s", a, b), ap(tile, x0, x0 + 4 * (b - a))
-        run("v", lambda q: q.quantize_mx(o["v"], p["v"], x["v"]), [o, p], [x])
+        step("c", "v", lambda q: q.quantize_mx(o["v"], p["v"], x["v"]), [o, p], [x])
 
     def mm(out, l, la, r, ra, rb, start=True, stop=True):
         xs = [ap(l, la, la + 128), ap(l + "s", la, la + 128), ap(r, ra, rb), ap(r + "s", ra, rb)]
-        run("t", lambda q: q.matmul_mx(out["v"], xs[0]["v"], xs[1]["v"], xs[2]["v"], xs[3]["v"], start, stop),
-            [out], xs)
+        step("c", "t", lambda q: q.matmul_mx(out["v"], xs[0]["v"], xs[1]["v"], xs[2]["v"], xs[3]["v"], start, stop),
+             [out], xs)
 
     def pick(dn, c, d, sn, a, b, on, e, f):
-        off = ap(on, e, f)
-        cp(ap(dn, c, d, bc=u32), ap(sn, a, b, bc=u32, off=off))
-        act(ap(dn + "s", c, d), ap(sn + "s", a, b, off=off))
+        cp(ap(dn, c, d, bc=u32), ap(sn, a, b, bc=u32, off=ap(on, e, f)))
+        aff(ap(dn + "s", c, d), ap(sn + "s", a, b, off=ap(on, e, f)))
+
+    def dma(q, o, i, outs, ins):
+        step("d", q, lambda e: e.dma_start(o, i), outs, ins)
 
     def move(dn, c, sn, a, n):
-        o, i = ap(dn, c, c + n, bc=u8), ap(sn, a, a + n, bc=u8)
-        dma("y", o["v"], i["v"], [o], [i])
-        o, i = ap(dn + "s", c, c + n), ap(sn + "s", a, a + n)
-        dma("y", o["v"], i["v"], [o], [i])
+        for o, i in ((ap(dn, c, c + n, bc=u8), ap(sn, a, a + n, bc=u8)), (ap(dn + "s", c, c + n), ap(sn + "s", a, a + n))):
+            dma("y", o["v"], i["v"], [o], [i])
 
     def load(q, n, a, b, src):
         o = ap(n, a, b)
         dma(q, o["v"], src, [o], [])
 
-    def to_all(src, dst, sem, ranks):
-        ready("g", [src])
-        sent[0] += same_to_all(g, T, topo, [(ranks, out), (near, inn)], src["v"], dst["v"], T.sem[sem])
+    def to_all(n, a, w, k, bc, sem, ranks):
+        src = ap(n, a, a + k, bc=bc)
 
-    def slots(rs):
-        return 32 * (7 - rs[-1]), 32 * (8 - rs[0])
+        def dst(r):
+            return ap(n, a + w * ((me - r) % N), a + w * ((me - r) % N) + k, bc=bc)["v"]
+        step(sem, "g", lambda g: sent.append(
+            same_to_all(g, T, topo, [(ranks, out), (near, inn)], src["v"], dst, T.sem[sem])), [], [src])
 
-    def pass_on(n, ex):
+    def to_near(x, y, sem):
+        step(sem, "g", lambda g: sent.append(
+            same_to_all(g, T, topo, [(near, inn)], x["v"], lambda r: y["v"], T.sem[sem])), [], [x])
+
+    def to_helper(name, xs):
+        rid, pid, _ = topo.addr(helpers[me])
+
+        def call(g):
+            g.remote_dma_fused([RemoteDMATransfer(dst_ids=[DstId(rid=rid, pnc=pid)], dma_engine_mask=bits(e),
+                                                  remote_sem=T.sem[s], src=x["v"], dst=y["v"]) for x, y, e, s in xs],
+                               local_sem=T.sem.lo)
+            sent.append(sum(len(x[2]) for x in xs))
+        step(name, "g", call, [], [x[0] for x in xs])
+
+    def pass_on(a, w, ex):
+        def run_of(rs, at):
+            return a + w * ((rs[0] - at) % N), a + w * ((rs[-1] - at) % N + 1)
         own, other = taken_by(T, topo, me), taken_by(T, topo, near[0])
         tok = (ex + "_c", len(own) * len(out) + len(inn))
-        arrive(n, *slots(own), tok)
-        arrive(n, *slots(near), tok)
-        arrive(n, *slots(other), (ex + "_cf", len(inn)))
-        for rs in (own, near, other):
-            arrive(n + "s", *slots(rs), (ex + "_s", nv))
-        x = ap(n, *slots(own), bc=u8)
-        ready("g", [x])
-        sent[0] += same_to_all(g, T, topo, [(near, inn)], x["v"], x["v"], T.sem[ex + "_cf"])
+        arrive("lw", *run_of(own, me), tok)
+        arrive("lw", *run_of(near, me), tok)
+        arrive("lw", *run_of(other, me), (ex + "_cf", len(inn)))
+        arrive("lws", a + w, a + w * N, (ex + "_s", nv))
+        to_near(ap("lw", *run_of(own, me), bc=u8), ap("lw", *run_of(own, near[0]), bc=u8), ex + "_cf")
 
     def c(n, k=0):
         return ap(n, k, k + 1)
 
     def iota(n, k, pat, base=0, cm=0):
-        o, small = ap(n, 0, k), SCRATCH[PART[n][0]][2] != I32
+        o, small = ap(n, 0, k), SCRATCH[PART.get(n, (n, 0))[0]][2] != I32
         kw = {"allow_small_or_imprecise_dtypes": True} if small else {}
-        run("g", lambda q: q.iota(o["v"], pat, base, cm, **kw), [o], [])
+        step("c", "g", lambda q: q.iota(o["v"], pat, base, cm, **kw), [o], [])
 
-    def wrap(s, row, w):
-        scan(ap(s, 0, w), ap("wt", 0, w), row, A.add, A.max)
-
-    def listed(lst, s, w, corr="corr", a=0):
-        ts(ap(lst, a // 16, w // 16), ap(s, a + 15, w, 16), c(corr), A.add)
+    def bank(n, k, a=0, b=128, st=1):
+        return ap(n, 512 * k + a, 512 * k + b, st)
 
     load("s", "u4", 0, 4, T.u[:, 0:4])
     load("y", "tbx", 0, 512, T.tb[:, 0:512])
@@ -323,335 +357,275 @@ def rank_program(g, core, T, topo):
     load("y", "nzx", 0, 256, T.nz[:, 0:256])
     load("y", "wx", 0, 512, T.w[:, 0:512])
     iota("pi", 4, [[0, 4]], 0, 1)
-    iota("c16r", 4, [[16, 4]])
+    iota("pj", 2, [[128, 2]], 0, 1)
     iota("io", 128, [[1, 128]])
-    iota("io64", 128, [[0, 2], [1, 64]])
-    iota("md16", 256, [[0, 16], [1, 16]])
-    zb = ap("zb", 0, 128)
+    iota("k2", 256, [[0, 8], [2, 16], [32, 2]], -128)
+    iota("qd4", 128, [[0, 8], [1, 4], [0, 4]])
+    iota("xr", 32, [[-1, 4], [0, 8]])
+    iota("c4", 16, [[0, 4], [1, 4]])
+    iota("idx", 16, [[16, 4], [-508, 4]])
+    iota("c4x", 4, [[128 if me == here[0] else -128, 2], [16, 2]], 0 if me == here[0] else 128)
+    iota("c256", 8, [[2, 8]], 256)
+    iota("c32", 8, [[32, 8]])
+    iota("r34", 272, [[0, 8], [256, 34]])
+    iota("frow", 256, [[1, 256]])
+    iota("p256", 64, [[16, 4], [1, 4], [4, 4]], 256)
+    zb, pi, lo, pf, io = ap("zb", 0, 128), ap("pi", 0, 4), c("lo"), c("pf"), "io"
     fill(zb, 0.0)
-    fill(ap("ct", 512, 1024), 0.0)
-    pi, ai, yi = ap("pi", 0, 4), ap("ai", 0, 4), ap("yi", 0, 4)
-    ts(ai, pi, 15, A.bitwise_and)
-    ts(c("hx"), c("pi"), 4, A.logical_shift_right)
-    ts(yi, pi, 7, A.bitwise_and)
-    tt(c("h16"), c("pi"), c("ai"), A.subtract)
-    cp(c("hif"), c("hx"))
-    tt(ap("wr", 0, 4), ai, ap("c16r", 0, 4), A.add)
-    cp(c("pf"), c("pi"))
-    ts(c("h16b"), c("h16"), 128.0, A.add)
-    ts(c("hi8"), c("hif"), 8.0, A.add)
-    hi, lo = c("hif"), c("wr")
-    for t, col in ((0, c("h16")), (1, c("h16b")), (2, lo), (3, lo)):
-        act(ap("ct", t, 512, 4), zb, bias=col)
-    act(c("ct", 512), c("zb"), bias=hi)
-    act(c("ct", 513), c("zb"), bias=c("hi8"))
-    act(ap("ct", 518, 520), ap("zb", 0, 2), bias=lo)
-    fill(ap("hb", 0, 128), 0.5)
-    o, i = ap("idn", 0, 128), ap("hb", 0, 128)
-    run("g", lambda q: q.affine_select(o["v"], i["v"], [[-1, 128]], A.is_equal, 0.0, 0, 1), [o], [i])
+    fill(ap("xt", 0, 16), 0.0)
+    fill(ap("rs8", 0, 64), -100.0)
+    fill(ap("rs8", 0, 64, 8), 3.5)
+    fill(ap("m32", 0, 64), -32.0)
     fill(ap("eb", 0, 528), 0.0)
-    iota("tsum", 64, [[1, 8], [1, 8]])
-    iota("ri", 64, [[0, 8], [1, 8]])
-    iota("c2", 4, [[2, 4]])
-    ts(ap("mask", 0, 128), ap("io", 0, 128), c("pf"), A.is_lt)
-    ts(c("corr"), lo, 512.0, A.mult, -7680.0, A.add)
-    fill(ap("vt", 128, 512), 0.0)
-    fill(ap("nzx", 256, 512), 0.0)
-    fill(ap("zf", 0, 32), 0.5)
-    fill(ap("lt4", 0, 512), 0.0)
-    for t in (0, 1, 2, 3):
-        if t < 2:
-            act(ap("ux", t, 512, 4), zb, bias=c("u4", t))
-        else:
-            ts(ap("ux", t, 512, 4), zb, c("u4", t), A.add)
-    quant("uq", 0, 128, "ux")
-
-    P0, P1, P2, P3 = 0, 512, 1024, 1536
-    quant("tq", 0, 128, "tbx")
-    mm(ap("pp", P1, P1 + 128), "tq", 0, "uq", 0, 128)
-    mm(ap("pp", P0, P0 + 128), "uq", 0, "tq", 0, 128)
-    quant("tq", 128, 256, "tbx", 512)
-    mm(ap("pp", P2, P2 + 128), "tq", 128, "uq", 0, 128)
-    mm(ap("pp", P3, P3 + 128), "uq", 0, "tq", 128, 256)
-    mm(ap("dv", 0, 256), "uq", 0, "tq", 0, 256)
-    rid, pid, _ = topo.addr(helpers[me])
-
-    def to_helper(n, o, sem, engines):
-        ready("g", [n])
-        g.remote_dma(o["v"], n["v"], T.sem[sem], T.sem.lo, pid, rid, bits(engines))
-        sent[0] += len(engines)
-    to_helper(ap("tq", 0, 256, bc=u8), ap("hq", 0, 256, bc=u8), "h_c", out + inn)
-    low, high = ap("pp", P0, P0 + 128), ap("pp", P3, P3 + 128)
-    s0, s1 = c("ss", 0), c("ss", 1)
-    for h, pk in ((0, P1), (1, P2)):
-        act(c("ss", h), c("pp", pk))
-        act(c("ds01", h), c("pp", pk), F.Abs, bias=2.0 ** -120, scale=0.7 * 2.0 ** -23)
-    quant("cq", 0, 256, "ct")
-    ts(ap("sm", 0, 128), ap("mask", 0, 128), c("ds01", 0), A.mult, s0, A.add)
-    act(ap("sm", 128, 256), ap("mask", 0, 128), bias=s1, scale=c("ds01", 1))
-    ts(ap("cmp", 0, 128), high, s0, A.is_lt)
-    ts(ap("cmp", 256, 384), low, s1, A.is_le)
-    tt(ap("cmp", 128, 256), low, ap("sm", 0, 128), A.is_lt)
-    tt(ap("cmp", 384, 512), high, ap("sm", 128, 256), A.is_lt)
-    act(ap("junk", 256, 384), ap("cmp", 256, 384), accum=c("pos", 1))
-    act(ap("junk", 0, 256), ap("cmp", 0, 256), accum=c("pos", 0))
-    act(ap("junk", 256, 512), ap("dv", 0, 256), F.Sign, bias=-2.0 ** -100, accum=c("ft"))
-    ts(ap("m16", 0, 256), ap("md16", 0, 256), lo, A.is_equal)
-    act(ap("wt", 0, 256), ap("m16", 0, 256), scale=-1000512.0, bias=512.0)
-    red(c("pos", 4), ap("cmp", 384, 512))
-    for t in (1, 3):
-        ts(ap("oh", t, 512, 4), ap("io64", 0, 128), c("pos", 1), A.subtract, c("pos", 4), A.is_equal)
-    for t in (0, 2):
-        ts(ap("oh", t, 512, 4), ap("io64", 0, 128), c("pos", 0), A.is_equal)
-    v = c("vl", 8 * slot)
-    ts(v, c("ft"), 256.0, A.add)
-    to_all(v, v, "a_v", far)
-    quant("oq", 0, 128, "oh")
-    mm(ap("dv", 512, 640), "oq", 0, "cq", 128, 256)
-    mm(ap("pp", P0, P0 + 128), "cq", 0, "oq", 0, 128)
-    ts(ap("bi", 0, 4), ai, 3, A.logical_shift_right)
-    cp(ap("lq7", 0, 4), yi)
-    ts(ap("gis", 0, 4), yi, -8.0, A.mult, 63.0, A.add)
-    ts(ap("in32", 0, 4), yi, 32.0, A.mult, 31.0, A.add)
-    act(ap("r8", 0, 64), ap("ri", 0, 64), F.Sign)
-    act(ap("eb", 3, 515, 4), ap("idn", 0, 128))
-    wrap("js", ap("pp", P0, P0 + 64), 64)
-    xx = ap("xx", 0, 4)
-    tt(xx, ap("bi", 0, 4), ap("c2", 0, 4), A.add)
-    listed("jl4", "js", 32)
-    pick("sp", 0, 32, "tq", 0, 256, "jl4", 0, 2)
-    listed("jl4", "js", 64, a=32)
-
-    to_all(ap("sp", 0, 32, bc=u8), ap("land", 32 * slot, 32 * slot + 32, bc=u8), "a_c", gates)
-    to_all(ap("sps", 0, 32), ap("lands", 32 * slot, 32 * slot + 32), "a_s", far)
-    cp(ap("lt4", 0, 2), ap("dv", 512, 514))
-    quant("tq", 256, 384, "lt4")
-    to_helper(ap("tq", 256, 258, bc=u8), ap("hq", 256, 258, bc=u8), "h_l", inn)
-    to_helper(ap("tqs", 0, 258), ap("hqs", 0, 258), "h_s", inn)
-    move("land", 32 * slot, "sp", 0, 32)
-    move("cd", 0, "tq", 0, 128)
-
-    act(ap("tie", 0, 64), ap("tsum", 0, 64), F.Sign, bias=7.5, scale=-1.0)
-    act(ap("wc", 0, 8), ap("zb", 0, 8), bias=32.0)
-    ts(ap("lrs", 0, 4), xx, -1.0, A.mult, 7.0, A.add)
-    pick("sp", 32, 64, "tq", 0, 256, "jl4", 2, 4)
-    move("xw", 128, "sp", 0, 64)
-    move("sl", 32 * slot, "tq", 32 * me, 32)
-    move("ll", 2 * slot, "tq", 256, 2)
-    move("ll", 16, "tq", 0, 112)
-    act(ap("tie5", 0, 64), ap("tie", 0, 64), scale=0.5)
-    act(c("wh8"), c("zb"))
-    act(c("w0"), c("zb"))
-    act(ap("ones", 0, 16), ap("zb", 0, 16), bias=1.0)
-    act(c("corr32"), c("corr"), bias=32.0)
+    fill(ap("fit8", 8, 16), 0)
+    fill(ap("vv", 32, 40), 0.0)
+    fill(ap("odw", 0, 16), -1.0)
+    fill(ap("odw", N - 1 - me, 16, 8), 7.0)
+    cp(pf, c("pi"))
+    ts(ap("hi2", 0, 2), ap("pj", 0, 2), 240, A.bitwise_and)
+    ts(ap("lo2", 0, 2), ap("pj", 0, 2), 15, A.bitwise_and)
+    cp(lo, c("lo2"))
+    for a, n in ((0, "hi2"), (6, "hi2"), (8, "lo2"), (14, "lo2")):
+        cp(ap("xt", a, a + 2), ap(n, 0, 2))
+    ts(ap("tie", 0, 128), ap(io, 0, 128), pf, A.is_lt, TINY, A.mult)
+    ts(ap("eb", 3, 515, 4), ap(io, 0, 128), pf, A.is_equal, 0.5, A.mult)
     for b in range(4):
         quant("eh", 128 * b, 128 * b + 128, "eb", 3 - b)
-    quant("nq", 0, 128, "nzx")
-    for b in range(4):
-        mm(ap("dv", 512 * b, 512 * b + 128), "eh", 128 * b, "nq", 0, 128, True, False)
-    ts(ap("grs", 0, 4), xx, -8.0, A.mult, 63.0, A.add)
-    iota("l2i", 16, [[1, 8], [0, 2]])
-    pass_on("land", "a")
-    iota("md32", 256, [[0, 8], [1, 32]])
-    iota("x32", 8, [[32, 8]], 256)
-    iota("p256", 64, [[1, 64]], 256)
-    iota("frow", 256, [[1, 256]])
+    ts(ap("yx", 0, 4), pi, 7, A.bitwise_and)
+    ts(ap("bi", 0, 4), pi, 3, A.logical_shift_right, 1, A.bitwise_and)
+    tt(ap("yx", 4, 8), ap("bi", 0, 4), ap(io, 0, 8, 2), A.add)
+    cp(ap("l1", 0, 8), ap("yx", 0, 8))
+    ts(ap("l8", 0, 8), ap("yx", 0, 8), 8.0, A.mult, 7.0, A.add)
+    ts(ap("l34", 0, 8), ap("yx", 0, 8), 34.0, A.mult, 31.0, A.add)
+    ts(ap("gx0", 0, 4), ap("yx", 4, 8), 16.0, A.mult, -41.0, A.add)
+    ts(ap("gx", 0, 4), ap("gx0", 0, 4), 7.0, A.max, 55.0, A.min)
+    lq7, lrs, gis, grs = ap("l1", 0, 4), ap("l1", 4, 8), ap("l8", 0, 4), ap("l8", 4, 8)
+    ts(ap("jc", 0, 2), ap("pi", 0, 2), 3, A.bitwise_and)
+    ts(c("jc", 2), c("pi"), 4, A.logical_shift_right, 3, A.bitwise_and)
+    ts(ap("jc", 3, 7), pi, 4, A.logical_shift_right, 1, A.bitwise_and)
+    ts(ap("jc", 5, 7), ap("jc", 5, 7), 2.0, A.add)
+    cp(c("q4f"), c("jc"))
+    ts(c("qi"), c("pi"), 2, A.logical_shift_right, 3, A.bitwise_and)
+    cp(c("qq4"), c("qi"))
+    aff(c("corr4"), c("q4f"), 512.0, c("qq4"))
+    ts(ap("wt4", 0, 16), ap("c4", 0, 16), c("q4f"), A.is_equal, -1000000.0, A.mult)
+    ts(c("hf"), c("pi"), 1, A.logical_shift_right, 7, A.bitwise_and)
+    ts(c("lll"), c("hf"), 32.0, A.mult, lo, A.add)
+    aff(c("lo256"), lo, 1.0, 256.0)
+    aff(c("lom"), lo, 2.0, -128.0)
+    aff(c("corr"), lo, 512.0, -7680.0)
+    aff(ap("c35", 0, 32), ap("xr", 0, 32), 1.0, 3.5)
+    ts(ap("m16", 0, 128), ap("k2", 0, 256, 2), c("lom"), A.is_equal)
+    aff(ap("wt", 0, 128), ap("m16", 0, 128), -1000512.0, 512.0)
+    ts(c("ind4"), pf, 64.0, A.is_lt, 4.0, A.mult)
+    for t in range(4):
+        ts(ap("w4t", t, 512, 4), ap("qd4", 0, 128), float(t), A.is_equal, c("ind4"), A.mult)
+    quant("w4q", 0, 128, "w4t")
+    quant("xq", 0, 128, "xt")
+    quant("wl", 16, 144, "wx")
+    for t in range(4):
+        aff(ap("ux", t, 512, 4), zb, 1.0, c("u4", t))
+    for t in range(4):
+        aff(ap("ux", 512 + t, 1024, 4), ap("ux", t, 512, 4), -1.0)
+    quant("uq", 0, 128, "ux")
+    quant("uq", 128, 256, "ux", 512)
 
-    n8 = len(far) * len(out) + len(near) * 2
-    arrive("vl", 0, 8 * slot, ("a_v", nv))
-    arrive("vl", 8 * slot + 8, 64, ("a_v", nv))
+    quant("tq", 0, 128, "tbx")
+    quant("tq", 128, 256, "tbx", 512)
+    to_helper("h1", [(ap("tq", 0, 128, bc=u8), ap("hq", 0, 128, bc=u8), out + inn, "h_c")])
+    h = len(inn) // 4
+    to_helper("h2", [(ap("tq", 128, 192, bc=u8), ap("hq", 128, 192, bc=u8), inn[:h], "h_c"),
+                     (ap("tq", 192, 256, bc=u8), ap("hq", 192, 256, bc=u8), inn[h:2 * h], "h_c"),
+                     (ap("tqs", 0, 256), ap("hqs", 0, 256), inn[2 * h:], "h_s")])
+    move("sl", 0, "tq", 32 * me, 32)
+    mm(bank("dv", 0), "uq", 0, "tq", 0, 128)
+    mm(bank("dv", 1), "uq", 0, "tq", 128, 256)
+    for k, (own, oth) in enumerate(((0, 0), (0, 128), (128, 0), (128, 128))):
+        first = own <= oth and k != 3
+        if first and k:
+            mm(bank("pp", k), "tq", own, "uq", 128, 256, True, False)
+            mm(bank("pp", k), "uq", 0, "tq", oth, oth + 128, False, True)
+        else:
+            mm(bank("pp", k), "uq", 0, "tq", oth, oth + 128, True, False)
+            mm(bank("pp", k), "tq", own, "uq", 128, 256, False, True)
+    act(ap("junk", 0, 128), bank("dv", 0), F.Sign, bias=-TINY, accum=c("ft", 0))
+    aff(c("ft", 2), c("ft", 0), 1.0, 256.0 + (N - 1 - me) / 4.0)
+    act(ap("junk", 128, 256), bank("dv", 1), F.Sign, bias=-TINY, accum=c("ft", 1))
+    act(ap("junk", 256, 384), bank("pp", 1), F.Sign, bias=-TINY, scale=-1.0, accum=c("ss", 0))
+    act(ap("junk", 384, 512), bank("pp", 2), F.Sign, bias=TINY, scale=-1.0, accum=c("ss", 1))
+    ts(c("vl"), c("ft", 1), c("ft", 2), A.add, 4.0, A.mult)
+    to_all("vl", 0, 8, 1, None, "a_v", far)
+    for h, k in ((0, 0), (1, 3)):
+        w = ap("cmp", 128 * h, 128 * h + 128)
+        tt(w, bank("pp", k), ap("tie", 0, 128), A.is_lt)
+        scan(ap("sa", 128 * h, 128 * h + 128), w, w, A.add, A.add)
+    aff(ap("s64", 0, 2), ap("ss", 0, 2), 1.0, -64.0)
+    for e, (tile, s) in enumerate((("oh", "ss"), ("oh2", "s64"))):
+        for h in (0, 1):
+            ts(ap(tile, h, 512, 2), ap("k2", 0, 256), c(s, h), A.subtract, c("sa", 128 * h + 127), A.is_equal)
+        quant("oq", 128 * e, 128 * e + 128, tile)
+        mm(bank("dv", 2 + e), "oq", 128 * e, "xq", 0, 128)
+        for k in (0, 1):
+            ts(c("jl4", 2 * e + k), bank("dv", 2 + e, k, k + 1), bank("dv", 2 + e, k + 2, k + 3), A.add)
+        aff(ap("lt", 4 * e, 4 * e + 4), bank("dv", 2 + e, 0, 4))
+    pick("lw", 0, 32, "tq", 0, 256, "jl4", 0, 2)
+
+    to_all("lw", 0, 32, 32, u8, "a_c", gates)
+    to_all("lws", 0, 32, 32, None, "a_s", far)
+    pass_on(0, 32, "a")
+    pick("xw", 128, 160, "tq", 0, 256, "jl4", 2, 4)
+    quant("lq", 0, 128, "lt")
+    move("lw", 288, "lq", 0, 2)
+    quant("cn", 64, 192, "nzx")
+    for b in range(4):
+        mm(bank("dv", b), "eh", 128 * b, "cn", 64, 192, True, False)
+    for b in range(4):
+        mm(bank("pp", b), "eh", 128 * b, "cn", 64, 192)
+        aff(ap("dn", b, 256, 4), bank("pp", b, 32, 96))
+
+    arrive("vl", 8, 64, ("a_v", nv))
     cp(ap("vi", 0, 8), ap("vl", 0, 64, 8))
-    ts(ap("ou32", 0, 4), xx, -32.0, A.mult, 255.0, A.add)
-    lq7, lrs, r8 = ap("lq7", 0, 4), ap("lrs", 0, 4), ap("r8", 0, 64)
-    tt(ap("k1", 0, 64), ap("vi", 0, 8, off=lrs), ap("tie", 0, 64), A.add)
-    act(ap("fiti", 0, 8), ap("vi", 0, 8), scale=0.5)
-    ts(ap("gr", 0, 4), xx, 8.0, A.mult, 7.0, A.add)
+    aff(ap("k1", 0, 64), ap("vi", 0, 8, off=lrs))
     tt(ap("cm", 0, 64), ap("vi", 0, 8, off=lq7), ap("k1", 0, 64), A.is_gt)
-    ts(c("ei"), c("pi"), 31, A.bitwise_and)
-    scan(ap("sc", 0, 64), r8, ap("cm", 0, 64))
-    cp(c("ef"), c("ei"))
-    mine = c("sc", 8 * me + 7)
-    ts(ap("ms", 0, 8), ap("sc", 7, 64, 8), mine, A.add, 7.0, A.not_equal)
-    ts(c("go"), mine, 3.5, A.is_lt, 160.0, A.mult)
-    scan(ap("st", 0, 8), ap("wc", 0, 8), ap("ms", 0, 8), A.add, A.mult)
-    ts(ap("ofx", 0, 2), ap("wr", 0, 2), c("go"), A.add)
-    ts(ap("ofa", 0, 2), ap("wr", 0, 2), c("st", 7), A.add)
-    gi, grs = ap("gis", 0, 4), ap("grs", 0, 4)
-    act(ap("q0", 0, 64), ap("sc", 0, 64, off=grs), F.Abs, bias=-3.5)
-    act(ap("g0", 0, 64), ap("sc", 0, 64, off=gi), scale=-1.0, bias=3.5)
-    ts(ap("ode", 0, 8), ap("sc", 7, 64, 8), c("pf"), A.not_equal)
-    pick("cd", 0, 32, "land", 0, 256, "ofa", 0, 2)
+    scan(ap("sc", 0, 64), ap("rs8", 0, 64), ap("cm", 0, 64), A.max, A.subtract)
+    g0, mine, c16 = ap("sc", 7, 64, 8), c("sc", 7), ap(io, 0, 32, 16)
+    ts(ap("ms", 0, 8), g0, mine, A.add, 0.0, A.not_equal)
+    scan(ap("st0", 0, 8), ap("ms", 0, 8), ap("m32", 0, 8))
+    ts(ap("ofa", 0, 2), c16, c("st0", 7), A.add, c("lo256"), A.add)
+    ts(c("go"), mine, 0.0, A.is_gt, 128.0, A.mult)
+    ts(ap("ofx", 0, 2), c16, c("go"), A.add, lo, A.add)
+    pick("cn", 32, 64, "lw", 0, 256, "ofa", 0, 2)
     for b in range(4):
-        mm(ap("dv", 512 * b, 512 * b + 128), "eh", 128 * b, "cd", 0, 128, False, True)
+        mm(bank("dv", b), "eh", 128 * b, "cn", 32, 160, False, True)
+        aff(ap("vt", b, 128, 4), bank("dv", b, 0, 32))
+    quant("xw", 0, 128, "vt")
+    pick("lw", 256, 288, "xw", 0, 160, "ofx", 0, 2)
 
-    def packed(vt, w, out, a):
-        for b in (0, 1, 2, 3):
-            o, i = ap(vt, b, 4 * w, 4), ap("dv", 512 * b, 512 * b + w)
-            if b % 2:
-                cp(o, i)
-            else:
-                act(o, i)
-        quant(out, a, a + 128, vt)
-    tt(ap("hit", 0, 64), ap("g0", 0, 64), ap("q0", 0, 64), A.is_equal)
-    ts(ap("tks", 0, 8), ap("g0", 0, 8), 0.0, A.is_lt)
-    tt(ap("hf", 0, 64), ap("fiti", 0, 8, off=lq7), ap("hit", 0, 64), A.mult)
-    tt(ap("hh", 0, 64), ap("hit", 0, 64), ap("ri", 0, 64), A.mult)
-    packed("vt", 32, "xw", 0)
-    ts(ap("thr8", 0, 8), ap("tks", 0, 8), -1e29, A.mult, 1e29, A.add)
-    pick("xs", 0, 32, "xw", 0, 192, "ofx", 0, 2)
+    to_all("lw", 256, 34, 34, u8, "b_c", gates)
+    to_all("lws", 256, 34, 34, None, "b_s", far)
+    pass_on(256, 34, "b")
 
-    to_all(ap("xs", 0, 32, bc=u8), ap("cw", 32 * slot, 32 * slot + 32, bc=u8), "b_c", gates)
-    to_all(ap("xss", 0, 32), ap("cws", 32 * slot, 32 * slot + 32), "b_s", far)
-    pass_on("cw", "b")
-    move("cw", 32 * slot, "xs", 0, 32)
+    plans = [slice_plan(helpers[r], T, topo, r) for r in range(N) if r != me]
+    for k, n, s in ((0, "sl", "s_c"), (1, "sls", "s_s")):
+        arrive(n, 32, 256, (s, sum(len(e) for p in plans for d, e in p[k] if d == me)))
+    tt(ap("mi", 0, 32), ap("sc", 0, 64, off=ap("l8", 0, 2)), ap("c35", 0, 32), A.not_equal)
+    scan(ap("st4", 0, 32), ap("mi", 0, 32), ap("m32", 0, 32))
+    ts(ap("ofs", 0, 8, 2), ap("st4", 7, 32, 8), lo, A.add, 256.0, A.add)
+    ts(ap("ofs", 1, 8, 2), ap("st4", 7, 32, 8), lo, A.add, 272.0, A.add)
+    pick("st", 0, 128, "sl", 0, 256, "ofs", 0, 8)
+    for n, b, sem in (("st", u8, "p_c"), ("sts", None, "p_s")):
+        to_near(ap(n, 0, 128, bc=b), ap(n, 128, 256, bc=b), sem)
+        arrive(n, 128, 256, (sem, len(inn)))
 
-    move("cw", 256, "land", 0, 256)
-    move("cc", 64, "tq", 0, 64)
-    move("np", 64, "nq", 64, 64)
-    for k in ((0, 2 * slot), (2 * slot + 2, 16)):
-        arrive("ll", k[0], k[1], ("l_c", n8))
-        arrive("lls", k[0], k[1], ("l_s", n8))
-    mm(ap("pp", P2, P2 + 128), "eh", 0, "ll", 0, 128)
-    mm(ap("pp", P3, P3 + 128), "eh", 128, "ll", 0, 128)
-    mm(ap("pp", P1, P1 + 256), "uq", 0, "land", 0, 256)
-    scan(ap("hfs", 0, 64), r8, ap("hf", 0, 64))
-    scan(ap("hhs", 0, 64), r8, ap("hh", 0, 64))
-    cp(ap("l256", 0, 16), ap("l2i", 0, 16))
+    cp(ap("vint", 0, 8), ap("vl", 0, 64, 8))
+    ts(ap("fit8", 0, 8), ap("vint", 0, 8), 65528, A.bitwise_and)
+    ts(ap("kr", 0, 8), ap("vint", 0, 8), 7, A.bitwise_and)
+    act(ap("q0", 0, 64), ap("sc", 0, 64, off=grs), F.Abs)
+    tt(ap("fd", 0, 8), ap("fit8", 0, 8), ap("fit8", 1, 9), A.subtract)
+    tt(ap("miss0", 0, 64), ap("sc", 0, 64, off=gis), ap("q0", 0, 64), A.not_equal)
+    aff(ap("fde", 0, 64), ap("fd", 0, 8, off=lq7))
+    scan(ap("hfs", 0, 64), ap("miss0", 0, 64), ap("fde", 0, 64))
+    scan(ap("hhs", 0, 64), ap("miss0", 0, 64), ap("m32", 0, 64))
     fh = ap("hfs", 7, 64, 8)
-    act(ap("tmp", 0, 8), fh, F.Relu, bias=-224.0)
-    act(ap("nh", 0, 8), ap("pp", P2, P2 + 16, 2), scale=32.0)
-    tt(ap("wh8", 1, 8), ap("hhs", 7, 56, 8), ap("hhs", 15, 64, 8), A.subtract)
-    ts(ap("nl", 0, 8), ap("pp", P3, P3 + 16, 2), 2.0, A.mult)
-    tt(ap("tmp2", 0, 8), ap("tmp", 0, 8), ap("tks", 0, 8), A.mult)
-    tt(ap("nj", 0, 8), ap("nh", 0, 8), ap("nl", 0, 8), A.add)
-    o, i = ap("jt", 0, 512, p=(0, 1)), ap("nj", 0, 8, p=(0, 64))
-    dma("y", o["v"], i["v"], [o], [i])
-    jr = ap("jr", 0, 512)
-    run("g", lambda q: q.partition_broadcast(jr["v"], o["v"], 128), [jr], [o])
-    z2, z1 = ap("vt2", 256, 512), ap("vt", 256, 512)
-    dma("y", z2["v"], z1["v"], [z2], [z1])
-    act(ap("o0a", 0, 8), ap("tks", 0, 8), scale=-256.0)
-    act(ap("thr", 0, 256), ap("thr8", 0, 8, off=ap("l256", 0, 16)))
-    act(ap("r32", 0, 256), ap("md32", 0, 256), F.Sign)
-    act(c("cola", 2), c("hhs", 63), scale=32.0)
-    act(ap("wh", 0, 64), ap("wh8", 0, 8, off=lq7), scale=32.0)
-    act(ap("cola", 0, 2), ap("wr", 0, 2), bias=c("cola", 2))
-    act(ap("w256", 0, 4), ap("wr", 0, 4), scale=256.0, bias=c("cola", 2))
-    act(ap("sw", 256, 512), ap("pp", P1, P1 + 256))
-    tt(ap("base1", 0, 8), fh, ap("tmp2", 0, 8), A.subtract)
-    ts(ap("i32r", 0, 64), ap("md32", 0, 64), c("ef"), A.is_equal)
-    tt(ap("dd", 0, 64), ap("base1", 0, 8, off=lrs), ap("tie5", 0, 64), A.add)
-    tt(ap("o0", 0, 8), ap("o0a", 0, 8), ap("x32", 0, 8), A.add)
-    tt(ap("nd", 0, 64), ap("base1", 0, 8, off=lq7), ap("dd", 0, 64), A.subtract)
-    tt(ap("w0", 1, 8), ap("o0", 0, 7), ap("o0", 1, 8), A.subtract)
-    quant("wq", 0, 128, "wx")
+    ts(ap("ba", 0, 8), g0, 0.0, A.is_gt, 256.0, A.mult)
+    tt(ap("bb", 0, 8), ap("ba", 0, 8), fh, A.add)
+    ts(ap("bc", 0, 8), ap("bb", 0, 8), 1792.0, A.max, 2048.0, A.min)
+    tt(ap("bd", 0, 8), fh, ap("bc", 0, 8), A.subtract)
+    tt(ap("kb", 0, 8), ap("bd", 0, 8), ap("kr", 0, 8), A.add)
+    aff(ap("kx", 0, 64), ap("kb", 0, 8, off=lrs))
+    tt(ap("nd", 0, 64), ap("kb", 0, 8, off=lq7), ap("kx", 0, 64), A.subtract)
+    ts(ap("tk", 0, 8), g0, 0.0, A.is_lt)
+    tt(ap("o1", 0, 8), ap("tk", 0, 8), ap("c256", 0, 8), A.mult)
+    aff(ap("vv", 0, 8), ap("q0", 0, 64, 8), -32.0, 112.0)
+    tt(ap("vv", 8, 16), ap("o1", 0, 8), ap("c32", 0, 8), A.add)
+    aff(ap("vv", 16, 24), ap("hhs", 7, 64, 8), 1.0625, 528.0)
+    aff(ap("vv", 24, 32), ap("hhs", 7, 64, 8), 0.125, 32.0)
+    tt(ap("ve", 0, 32), ap("vv", 0, 32), ap("vv", 1, 33), A.subtract)
+    aff(ap("ve", 32, 64), ap("ve", 0, 8, off=ap("l1", 0, 2)))
+    aff(ap("kk", 0, 3), ap("vv", 8, 32, 8), 1.0, lo)
+    ts(ap("ode", 0, 8), g0, pf, A.add, 3.5, A.not_equal)
 
-    for k in ((0, 32 * slot), (32 * slot + 32, 256)):
-        arrive("sl", k[0], k[1], ("s_c", 7))
-        arrive("sls", k[0], k[1], ("s_s", 7))
-    mm(ap("pp", P0, P0 + 128), "uq", 0, "cw", 0, 128)
-    mm(ap("pp", P3, P3 + 128), "uq", 0, "cw", 128, 256)
-    for k, pk in ((0, P0), (128, P3)):
-        tt(ap("c1", k, k + 128), ap("pp", pk, pk + 128), ap("thr", k, k + 128), A.is_gt)
-    scan(ap("s1", 0, 256), ap("r32", 0, 256), ap("c1", 0, 256))
-    act(ap("x1b", 0, 64), ap("s1", 0, 256, off=ap("ou32", 0, 4)))
-    tt(ap("k1b", 0, 64), ap("s1", 0, 256, off=ap("in32", 0, 4)), ap("nd", 0, 64), A.add)
-    for k, pk in ((0, P0), (128, P3)):
-        act(ap("sw", k, k + 128), ap("pp", pk, pk + 128))
+    for k, pk in ((0, 0), (136, 3)):
+        mm(bank("pp", pk, 0, 136), "uq", 0, "lw", 256 + k, 392 + k)
+        ts(ap("c1", k, k + 136), bank("pp", pk, 0, 136), 0.0, A.is_gt, 8.0, A.mult)
+    scan(ap("s1", 0, 272), ap("r34", 0, 272), ap("c1", 0, 272), A.min, A.add)
+    aff(ap("x1b", 0, 64), ap("s1", 0, 272, off=ap("l34", 4, 8)))
+    tt(ap("k1b", 0, 64), ap("s1", 0, 272, off=ap("l34", 0, 4)), ap("nd", 0, 64), A.add)
     tt(ap("cmb", 0, 64), ap("x1b", 0, 64), ap("k1b", 0, 64), A.is_lt)
-    scan(ap("scb", 0, 64), r8, ap("cmb", 0, 64))
-    act(ap("q1", 0, 64), ap("scb", 0, 64, off=ap("gr", 0, 4)), F.Abs, bias=-3.5)
-    ts(ap("g1", 0, 64), ap("scb", 0, 64, off=gi), -1.0, A.mult, 3.5, A.add)
-    ts(c("t32"), c("scb", 8 * me + 7), 3.5, A.is_gt, 32.0, A.mult)
-    tt(ap("miss", 0, 64), ap("g1", 0, 64), ap("q1", 0, 64), A.not_equal)
-    ts(ap("ode", 8, 16), ap("scb", 7, 64, 8), c("pf"), A.not_equal)
-    scan(ap("bs", 0, 64), ap("wh", 0, 64), ap("miss", 0, 64), A.add, A.mult)
-    scan(ap("st0", 0, 8), ap("w0", 0, 8), ap("miss", 8 * me, 8 * me + 8), A.add, A.mult)
-    mh = 4 * (me // 4)
-    halves = (4 - mh, mh)
-    ts(ap("of", 0, 16, 2), ap("bs", 7, 64, 8), c("cola", 0), A.add)
-    ts(ap("of", 1, 16, 2), ap("bs", 7, 64, 8), c("cola", 1), A.add)
-    mb = c("bs", 8 * me + 7)
-    ts(ap("ofj", 0, 4), ap("w256", 0, 4), mb, A.add, 1.0 / 32, A.mult)
-    for r0 in halves:
-        pick("sb", 32 * r0, 32 * r0 + 128, "sl", 0, 256, "of", 2 * r0, 2 * r0 + 8)
-        if r0 != mh:
-            ts(ap("ofc", 0, 2), ap("wr", 0, 2), c("st0", 7), A.add, c("o0", 7), A.add)
-            ts(ap("ofc", 2, 4), ap("cola", 0, 2), mb, A.add)
+    scan(ap("scb", 0, 64), ap("rs8", 0, 64), ap("cmb", 0, 64), A.max, A.subtract)
+    act(ap("qx", 0, 64), ap("scb", 0, 64, off=ap("gx", 0, 4)), F.Abs)
+    tt(ap("miss", 0, 64), ap("scb", 0, 64, off=gis), ap("qx", 0, 64), A.not_equal)
+    scan(ap("bs", 0, 64), ap("miss", 0, 64), ap("ve", 0, 64))
+    c4x = ap("c4x", 0, 4)
+    for k, s in enumerate((39, 47, 55, 7)):
+        ts(ap("of", 4 * k, 4 * k + 4), c4x, c("bs", s), A.add, c("kk", 0), A.add)
+    pick("sb", 0, 192, "st", 0, 256, "of", 0, 12)
+    pick("wl", 0, 16, "lw", 288, 528, "lll", 0, 1)
+    for k in (0, 1):
+        mm(bank("pp", 1 + k), "eh", 128 * k, "wl", 0, 128, True, False)
+        mm(bank("pp", 1 + k), "eh", 128 * k + 256, "wl", 0, 128, False, True)
+        aff(ap("jv", k, 32, 2), bank("pp", 1 + k, 0, 16), 2.0)
 
-    to_helper(ap("sb", 32 * halves[0], 32 * halves[0] + 128, bc=u8), ap("h3", 0, 128, bc=u8), "h_3", inn)
-    for n, b, sem, r0 in (("sbs", None, "c_s", halves[0]), ("sb", u8, "c_c", mh), ("sbs", None, "c_s", mh)):
-        to = [r for r in range(r0, r0 + 4) if r in far]
-        w = len(out) // len(to)
-        to = [(r, out[w * i:w * i + w]) for i, r in enumerate(to)] + [(r, inn) for r in near if r0 == mh]
-        ready("g", [ap(n, 32 * r0, 32 * r0 + 128)])
-        sent[0] += one_each(g, T, topo, to, lambda r: ap(n, 32 * r, 32 * r + 32, bc=b)["v"],
-                            ap("fw" + n[2:], 32 * me, 32 * me + 32, bc=b)["v"], T.sem[sem])
-    n3 = 4 * len(out) // 4 + 2 * len(out) // 2 + len(inn)
-    move("fw", 32 * me, "sb", 32 * me, 32)
+    w, col = len(out) // 4, 32 * here[0]
 
-    cs, cj, cr, tp = ap("csj", 0, 64), ap("csj", 64, 128), ap("cr", 0, 64), ap("tp", 0, 64)
-    cp(cj, ap("jr", 0, 512, off=ap("ofj", 0, 4)))
-    cp(cs, ap("sw", 0, 512, off=ap("ofc", 0, 4)))
-    tt(ap("dgo", 64, 128), cj, ap("i32r", 0, 64), A.mult)
-    tt(ap("dgo", 0, 64), cs, ap("i32r", 0, 64), A.mult)
-    wrap("jws", cj, 64)
-    scan(ap("ds", 0, 128), ap("r32", 0, 128), ap("dgo", 0, 128))
-    pick("cc", 0, 64, "cw", 0, 512, "ofc", 0, 4)
-    move("fw", 256, "cc", 0, 64)
+    def to_like(n, b, sem, es):
+        step(sem, "g", lambda g: sent.append(one_each(
+            g, T, topo, list(zip(like, es)), lambda r: ap(n, 64 * like.index(r), 64 * like.index(r) + 64, bc=b)["v"],
+            lambda r: ap("fw" + n[2:], col, col + 64, bc=b)["v"], T.sem[sem])), [], [ap(n, 0, 192)])
+    to_like("sb", u8, "c_c", (out[:2 * w], out[2 * w:3 * w], out[3 * w:]))
+    to_like("sbs", None, "c_s", (out[2 * w:], out[:w], out[w:2 * w]))
+    pick("fw", col, col + 64, "st", 0, 256, "of", 12, 16)
+
+    ts(ap("ofc", 0, 2), c16, c("bs", 15), A.add, c("kk", 1), A.add)
+    ts(ap("ofc", 2, 4), c16, c("bs", 23), A.add, c("kk", 2), A.add)
+    ts(ap("jl", 0, 7), ap("jc", 0, 7), c("bs", 31), A.add)
+    pick("cn", 0, 64, "lw", 0, 528, "ofc", 0, 4)
+    mm(bank("pp", 0), "uq", 0, "cn", 0, 128, True, False)
+    mm(bank("pp", 0), "cn", 0, "uq", 128, 256, False, True)
     for b in range(4):
-        mm(ap("dv", 512 * b, 512 * b + 128), "eh", 128 * b, "cc", 0, 128, True, False)
-    two = [(e, (64 * e, 64 * e + 64)) for e in (0, 1)]
-    for e, w in two:
-        act(ap("jl", *w), cj, F.Sign, bias=c("ds", 64 + 32 * e + 31), scale=-1.0)
-        ts(ap("eq", *w), cs, c("ds", 32 * e + 31), A.is_equal)
-    for e, w in two:
-        act(ap("lt", *w), cs, F.Sign, bias=c("ds", 32 * e + 31), scale=-1.0)
-        tt(ap("eqj", *w), ap("eq", *w), ap("jl", *w), A.mult)
-    listed("jw", "jws", 64)
-    for e, w in two:
-        scan(ap("cnt", *w), ap("lt", *w), ap("eqj", *w), A.add, A.add)
-    for e, w in two:
-        ts(ap("tp", 32 * e, 32 * e + 32), ap("zf", 0, 32), c("cnt", 64 * e + 63), A.mult, 31.5, A.add)
-    scan(ap("odc", 0, 16), ap("ones", 0, 16), ap("ode", 0, 16), A.add, A.mult)
-    run("v", lambda q: q.transpose(cr["v"], tp["v"]), [cr], [tp])
-    finish(False)
-    act(ap("odr", 0, 2), ap("odc", 7, 16, 8), scale=-1.0, bias=7.0)
+        mm(bank("dv", b), "eh", 128 * b, "cn", 0, 128)
+        aff(ap("dc", b, 256, 4), bank("dv", b, 0, 64))
+    aff(ap("gb", 16, 96), ap("jv", 0, 32, off=ap("jl", 2, 7)))
+    o, i = ap("cj", 0, 64), ap("gb", 32, 96)
+    step("c", "v", lambda q: q.transpose(o["v"], i["v"]), [o], [i])
+    ts(ap("ntie", 0, 64), ap("cj", 0, 64), c("gb", 16), A.is_gt, -TINY, A.mult)
+    tt(ap("oh", 0, 64), bank("pp", 0, 0, 64), ap("ntie", 0, 64), A.is_gt)
+    quant("cx", 0, 128, "oh")
+    mm(bank("pp", 3), "w4q", 0, "cx", 0, 128)
+    ts(ap("l4", 0, 16), bank("pp", 3, 0, 16), c("q4f"), A.add)
+    tt(ap("vt2", 0, 256), ap("dn", 0, 256, off=ap("l4", 0, 16)), ap("dc", 0, 256), A.add)
+    quant("cn", 64, 192, "vt2")
+    ts(c("t128"), c("scb", 7), 0.0, A.is_lt, 128.0, A.mult)
+    ts(ap("sel", 0, 16), bank("pp", 3, 0, 16), c("t128"), A.is_lt, 64.0, A.mult)
+    tt(ap("off", 0, 16), ap("sel", 0, 16), ap("idx", 0, 16), A.add)
+    scan(ap("xs", 0, 16), ap("wt4", 0, 16), ap("off", 0, 16), A.add, A.max)
+    ts(ap("xl", 0, 4), ap("xs", 3, 16, 4), c("corr4"), A.add)
+    pick("fw", 256, 320, "cn", 0, 128, "xl", 0, 4)
+    cp(ap("jw", 0, 16), ap("jv", 0, 32, off=ap("jl", 0, 1)))
+    cp(ap("frow", 0, 256, off=ap("jw", 0, 4)), ap("p256", 0, 64))
+    for k in (0, 1):
+        scan(ap("fs", 128 * k, 128 * k + 128), ap("wt", 0, 128), ap("frow", 128 * k, 128 * k + 128), A.add, A.max)
+    ts(ap("fl", 0, 16), ap("fs", 15, 256, 16), c("corr"), A.add)
+    ts(ap("ode", 8, 16), ap("scb", 7, 64, 8), pf, A.add, 3.5, A.not_equal)
+    scan(ap("odc", 0, 16), ap("ode", 0, 16), ap("odw", 0, 16))
+    aff(ap("odr", 0, 2), ap("odc", 7, 16, 8), 1.0, float(me))
     for t in (0, 1):
         x = ap("odr", t, t + 1, p=(0, 8))
         dma("y", T.od[t:t + 1, 0:8], x["v"], [], [x])
-    wrap("crw", cr, 64)
-    ts(ap("sel", 0, 64), cr, c("t32"), A.is_lt, 64.0, A.mult)
-    listed("pl", "crw", 64, "corr32")
-    tt(ap("off", 0, 64), ap("sel", 0, 64), ap("p256", 0, 64), A.add)
-    pick("np", 0, 64, "nq", 0, 128, "pl", 0, 4)
-    for b in range(4):
-        mm(ap("dv", 512 * b, 512 * b + 128), "eh", 128 * b, "np", 0, 128, False, True)
-    cp(ap("frow", 0, 256, off=ap("jw", 0, 4)), ap("off", 0, 64))
-    wrap("fs", ap("frow", 0, 256), 256)
-    packed("vt2", 64, "fw", 320)
-    listed("fl", "fs", 256)
 
-    for k in ((0, 32 * me), (32 * me + 32, 256)):
-        arrive("fw", k[0], k[1], ("c_c", n3))
-        arrive("fws", k[0], k[1], ("c_s", n3))
-    for k, pk in ((0, P2), (1, P3)):
-        pick("oq2", 128 * k, 128 * k + 128, "fw", 0, 448, "fl", 8 * k, 8 * k + 8)
-        mm(ap("pp", pk, pk + 128), "wq", 0, "oq2", 128 * k, 128 * k + 128)
-    x = ap("oq2", 0, 256, bc=u8)
-    dma("y", T.oc[:, 0:1024], x["v"], [], [x])
-
-    def scales_out(k, q):
-        x = ap("oq2s", 0, 256, p=(32 * k, 32 * k + 4))
-        dma(q, T.osc[4 * k:4 * k + 4, 0:256], x["v"], [], [x])
-    scales_out(0, "y")
-    scales_out(1, "y")
-    act(ap("yo", 0, 128), ap("pp", P2, P2 + 128))
-    cp(ap("yo", 128, 256), ap("pp", P3, P3 + 128))
-    for k, q in ((0, "s"), (1, "y")):
+    for k in ((0, col), (col + 64, 256)):
+        arrive("fw", k[0], k[1], ("c_c", len(out)))
+        arrive("fws", k[0], k[1], ("c_s", len(out)))
+    for k in (0, 1):
+        pick("oq2", 128 * k, 128 * k + 128, "fw", 0, 320, "fl", 8 * k, 8 * k + 8)
+        mm(bank("pp", 1 + k), "wl", 16, "oq2", 128 * k, 128 * k + 128)
+        x = ap("oq2", 128 * k, 128 * k + 128, bc=u8)
+        dma("y", T.oc[:, 512 * k:512 * k + 512], x["v"], [], [x])
         x = ap("yo", 128 * k, 128 * k + 128)
-        dma(q, T.y[:, 128 * k:128 * k + 128], x["v"], [], [x])
-    scales_out(2, "s")
-    scales_out(3, "s")
-    finish()
-    g.wait_ge(T.sem.lo, sent[0])
+        aff(x, bank("pp", 1 + k))
+        dma("sy"[k], T.y[:, 128 * k:128 * k + 128], x["v"], [], [x])
+    for k in range(4):
+        x = ap("oq2s", 0, 256, p=(32 * k, 32 * k + 4))
+        dma("yyss"[k], T.osc[4 * k:4 * k + 4, 0:256], x["v"], [], [x])
+    issue()
+    g.wait_ge(T.sem.lo, sum(sent))

@@ -6,21 +6,9 @@ F = ActivationFunctionType
 CODE, PLANE, F32, BF, I32, U16 = "float8_e4m3fn_x4", "uint8", "float32", "bfloat16", "int32", "uint16"
 SCRATCH, PART = {}, {}
 TINY = 2.0 ** -100
-ORDER = [0, 1, 5, 24, 2, 4, 3, 6, 19, 7, 21, 44, 23, 31, 26, 30, 29, 10, 20, 38, 43, 8, 36, 40, 33, 35, 45, 76, 79, 78,
-         77, 83, 82, 86, 80, 84, 88, 81, 87, 98, 92, 85, 94, 32, 102, 100, 46, 99, 34, 37, 101, 138, 95, 106, 96, 74,
-         97, 111, 89, 93, 103, 105, 109, 112, 110, 104, 115, 114, 113, 107, 116, 62, 108, 39, 117, 121, 143, 118, 139,
-         119, 27, 120, 128, 122, 129, 130, 41, 65, 47, 131, 123, 147, 145, 151, 22, 124, 25, 152, 141, 42, 144, 125,
-         184, 149, 153, 140, 126, 127, 132, 154, 185, 142, 15, 155, 187, 135, 18, 188, 156, 136, 193, 90, 190, 137,
-         158, 9, 91, 189, 157, 176, 161, 160, 14, 134, 200, 192, 17, 166, 159, 168, 133, 164, 177, 167, 169, 162, 191,
-         165, 163, 150, 68, 170, 13, 171, 172, 178, 205, 194, 173, 179, 51, 63, 174, 195, 75, 11, 146, 186, 70, 52,
-         181, 48, 72, 196, 56, 55, 202, 71, 197, 180, 148, 175, 198, 201, 183, 28, 59, 64, 182, 60, 49, 203, 16, 204,
-         199, 210, 69, 61, 53, 206, 73, 207, 212, 211, 229, 12, 213, 228, 214, 230, 50, 233, 216, 215, 234, 231, 209,
-         235, 217, 208, 218, 66, 219, 276, 264, 277, 220, 278, 232, 221, 54, 279, 224, 222, 223, 242, 241, 227, 240,
-         226, 255, 271, 237, 243, 244, 236, 256, 67, 272, 245, 246, 251, 257, 57, 247, 258, 253, 273, 248, 249, 259,
-         274, 250, 260, 225, 252, 58, 261, 265, 254, 239, 266, 262, 267, 263, 268, 275, 238, 270, 269, 288, 287, 282,
-         281, 290, 289, 280, 296, 293, 291, 295, 283, 284, 292, 285, 294, 286]
-SCALAR = (58, 62, 63, 64, 65, 67, 76, 80, 113, 120, 129, 134, 144, 146, 148, 150, 152, 161, 169, 172, 181, 190, 198,
-          202, 204, 205, 207, 208, 215, 227, 229, 232, 235, 239, 244, 248, 250, 255, 270, 278, 282, 288)
+ORDER = [23, 5, 19, 0, 6, 18, 77, 7, 1, 31, 29, 30, 2, 44, 63, 78, 55, 45, 38, 79, 96, 95, 94, 104, 10, 97, 99, 102, 105, 15, 98, 100, 3, 43, 101, 75, 42, 111, 103, 119, 35, 117, 112, 113, 39, 37, 114, 4, 121, 118, 159, 130, 122, 124, 125, 120, 132, 131, 34, 8, 20, 133, 33, 36, 115, 116, 106, 136, 123, 126, 76, 135, 92, 137, 56, 134, 143, 138, 80, 127, 107, 41, 14, 139, 140, 128, 9, 142, 149, 32, 81, 67, 129, 40, 144, 57, 24, 168, 28, 150, 64, 82, 161, 69, 21, 47, 48, 166, 172, 173, 74, 151, 141, 152, 145, 73, 148, 170, 22, 65, 26, 174, 175, 49, 46, 162, 176, 147, 27, 146, 177, 167, 156, 178, 83, 163, 164, 72, 181, 160, 11, 13, 179, 153, 216, 68, 180, 182, 154, 158, 184, 157, 155, 215, 217, 185, 192, 165, 218, 110, 188, 189, 207, 108, 186, 219, 53, 193, 187, 190, 191, 183, 194, 208, 221, 195, 16, 109, 196, 197, 232, 220, 198, 86, 222, 199, 51, 231, 54, 171, 66, 223, 71, 228, 233, 201, 234, 52, 224, 200, 209, 238, 210, 203, 70, 229, 225, 226, 50, 59, 87, 202, 230, 211, 227, 204, 93, 205, 237, 25, 84, 240, 212, 88, 169, 239, 58, 85, 241, 206, 60, 253, 89, 242, 90, 252, 243, 235, 236, 91, 244, 254, 288, 213, 245, 300, 265, 246, 214, 264, 255, 257, 258, 248, 256, 247, 266, 259, 268, 267, 273, 250, 279, 269, 280, 17, 260, 271, 295, 251, 270, 274, 249, 281, 296, 282, 301, 283, 297, 298, 275, 62, 277, 262, 276, 261, 284, 289, 285, 278, 272, 12, 61, 290, 286, 302, 291, 287, 292, 263, 299, 293, 304, 294, 303, 312, 311, 313, 305, 314, 315, 308, 306, 318, 320, 319, 316, 307, 309, 310, 317]
+SCALAR = (61, 65, 69, 70, 71, 72, 85, 97, 98, 101, 110, 127, 128, 134, 141, 148, 150, 155, 158, 165, 167, 169, 171, 172, 173, 185, 189, 196, 212, 219, 226, 229, 231, 234, 236, 237, 239, 251, 253, 256, 259, 263, 268, 272, 274, 276, 278, 279, 294, 302, 306, 312)
+VIA = 6
 
 
 def _bufs():
@@ -40,30 +28,31 @@ def _bufs():
             SCRATCH[k] = ("sbuf", [128, kw[k]], CODE)
             SCRATCH[k + "s"] = ("sbuf", [128, kw[k]], PLANE)
     parts("big", BF, vt2=256, vt=128, lt=8, xt=16, nzx=256, wx=512)
-    b(BF, tbx=1024, ux=1024, u4=8, eb=528, oh=512, oh2=512, w4t=512, zb=128, cmp=256, junk=512, c1=272, s1=272)
-    parts("bconst", BF, io=128, tie=128, k2=256, qd4=128, m16=128, r34=272)
+    b(BF, tbx=1024, ux=1024, u4=8, eb=528, oh=512, oh2=512, w4t=512, zb=128, cmp=256, junk=512, v0=8, vn=8, f0=16,
+      cb=64, f1=72)
+    parts("bconst", BF, io=128, tie=128, k2=256, qd4=128, m16=128)
     parts("fconst", F32, lo=8, pf=8, lo256=8, lom=8, q4f=8, qq4=8, ind4=8, corr=8, corr4=8, c4=16,
-          wt4=16, idx=16, c4x=8, c256=8, c32=8, xr=32, c35=32, rs8=64, m32=64, odw=16, gx0=8, p256=64, wt=128)
-    parts("fown", F32, ft=8, ss=8, s64=8, sa=256)
-    b(F32, jv=32, gb=96, cj=64, ntie=64, dn=256, dc=256, vi=8, yo=256, frow=256)
-    parts("flist", F32, k1=64, cm=64, sc=64, ms=8, st0=8, go=8, q0=64, miss0=64, fd=8, fde=64, hfs=64, hhs=64,
-          tk=8, ba=8, bb=8, bc=8, bd=8, kb=8, kx=64, nd=64, mi=32, st4=32, vv=40, ve=64, o1=8, kk=8,
+          wt4=16, idx=16, c4x=8, c256=8, c32=8, xr=32, c35=32, rs8=64, m32=64, odw=16, gx0=8, p256=64, wt=128,
+          mo=8, frac=8, fr=8, lv0=8, lv1=8, c14=8, c270=8, h14=8, l14=8)
+    parts("fown", F32, ft=8, ss=8, s64=8, sa=256, vm=8)
+    b(F32, jv=32, gb=96, cj=64, ntie=64, dn=256, dc=256, xk=64, ak=64, ak2=64, yo=256, frow=256)
+    parts("flist", F32, cm=64, sc=64, ms=8, st0=8, go=8, q0=64, miss0=64, fd=8, fde=64, hfs=64, hhs=64,
+          tk=8, bb=8, bc=8, bd=8, kb=8, kx=64, nd=64, mi=32, st4=32, vv=40, ve=64, o1=8, kk=8,
           k1b=64, x1b=64, cmb=64, scb=64, qx=64, miss=64, bs=64, t128=8, sel=16, off=16, xs=16,
-          ode=16, odc=16, odr=8, fs=256)
-    parts("iconst", I32, pi=8, pj=8, hi2=8, lo2=8, yx=8, bi=8, jc=8, hf=8, qi=8)
-    parts("ilist", I32, vint=8, fit8=16, kr=8)
-    b(U16, vl=64)
-    parts("lists", U16, jl4=4, l1=8, l8=8, l34=8, gx=4, lll=2, ofa=2, ofx=2, ofs=8, of=16,
-          ofc=4, jl=8, jw=16, l4=16, xl=4, fl=16)
-    q(uq=256, tq=256, xq=128, oq=256, lq=128, eh=512, lw=528, xw=160, cn=192, wl=144, sl=256, st=256, sb=192,
+          ode=16, odc=16, odr=8, fs=256, fit=16, w1=8, w2=8)
+    parts("iconst", I32, pi=8, pj=8, hi2=8, lo2=8, yx=8, bi=8, jc=8, hf=8, qi=8, r0=8, r1=8, r2=8, r3=8, r4=8)
+    parts("lists", U16, jl4=4, l1=8, l8=8, lv=8, gx=4, lll=2, ofa=2, ofx=2, ofs=8, of=16,
+          ofc=4, jl=8, jw=16, l4=16, xl=4, fl=16, lz=4, lme=2, lq1=2)
+    q(uq=256, tq=256, xq=128, oq=256, lq=128, eh=512, lw=556, xw=160, cn=192, wl=144, sl=256, st=256, sb=192,
       fw=320, oq2=256, w4q=128, cx=128, hq=256)
+    b(PLANE, hb=34)
     SCRATCH["dv"] = ("psum", [128, 2048], F32)
     SCRATCH["pp"] = ("psum", [128, 2048], F32)
 
 
 _bufs()
-SEMAPHORES = ["cv", "cs", "ct_", "cg", "lo", "a_v", "a_c", "a_s", "b_c", "b_s", "c_c", "c_s", "s_c", "s_s", "h_c",
-              "h_s", "p_c", "p_s", "a_cf", "b_cf"] + ["d%d" % i for i in range(32)]
+SEMAPHORES = ["cv", "cs", "ct_", "cg", "lo", "a_n", "a_v", "a_c", "a_s", "b_c", "b_s", "b_cn", "b_sn", "b_v", "c_c",
+              "c_s", "s_c", "s_s", "h_c", "h_s", "h_b", "p_c", "p_s", "a_cf", "b_cf"] + ["d%d" % i for i in range(32)]
 
 
 def find_helpers(T, topo):
@@ -78,12 +67,16 @@ def find_helpers(T, topo):
     return out
 
 
-def bits(engines):
-    return sum(1 << e for e in engines)
-
-
 def chip_ranks(T, topo, r):
     return [x for x in range(len(T.cores)) if topo.chip(T.cores[x]) == topo.chip(T.cores[r])]
+
+
+def slot(T, topo, r, at):
+    return (r - chip_ranks(T, topo, at)[0]) % len(T.cores)
+
+
+def place2(s):
+    return 256 + 34 * s + 14 * min(s, 2)
 
 
 def ways(core, T, topo, me):
@@ -101,22 +94,14 @@ def taken_by(T, topo, d):
     return far[:len(far) // 2] if d == here[0] else far[len(far) // 2:]
 
 
-def dest(T, topo, r):
-    rid, pid, _ = topo.addr(T.cores[r])
-    return DstId(rid=rid, pnc=pid)
-
-
-def one_each(g, T, topo, to, src, dst, sem):
-    g.remote_dma_fused([RemoteDMATransfer(dst_ids=[dest(T, topo, r)], dma_engine_mask=bits(e), remote_sem=sem,
-                                          src=src(r), dst=dst(r)) for r, e in to], local_sem=T.sem.lo)
-    return sum(len(e) for _, e in to)
-
-
-def same_to_all(g, T, topo, to, src, dst, sem):
-    g.remote_dma_fused([RemoteDMATransfer(dst_ids=[dest(T, topo, r) for r in rs], dma_engine_mask=bits(e),
-                                          remote_sem=sem, srcs=[src], dsts=[dst(r) for r in rs]) for rs, e in to],
+def fused(g, T, topo, xs):
+    def at(c):
+        rid, pid, _ = topo.addr(c)
+        return DstId(rid=rid, pnc=pid)
+    g.remote_dma_fused([RemoteDMATransfer(dst_ids=[at(c) for c in cs], dma_engine_mask=sum(1 << k for k in e),
+                                          remote_sem=T.sem[s], srcs=[x], dsts=ys) for cs, e, x, ys, s in xs],
                        local_sem=T.sem.lo)
-    return sum(len(e) for _, e in to)
+    return sum(len(x[1]) for x in xs)
 
 
 def slice_plan(core, T, topo, r):
@@ -131,15 +116,23 @@ def slice_plan(core, T, topo, r):
 
 
 def hand_on(g, core, T, topo, r):
-    S, n = 32, len(T.cores)
+    S = 32
     far, near, out, inn = ways(core, T, topo, r)
     codes, scales = slice_plan(core, T, topo, r)
-    g.wait_ge(T.sem.h_c, len(out) + len(inn) + len(inn) // 2)
-    k = one_each(g, T, topo, codes, lambda s: T.hq[:, S * s:S * s + S].bitcast(dt.uint8),
-                 lambda s: T.sl[:, S * ((r - s) % n):S * ((r - s) % n) + S].bitcast(dt.uint8), T.sem.s_c)
-    g.wait_ge(T.sem.h_s, len(inn) // 2)
-    k += one_each(g, T, topo, scales, lambda s: T.hqs[:, S * s:S * s + S],
-                  lambda s: T.sls[:, S * ((r - s) % n):S * ((r - s) % n) + S], T.sem.s_s)
+
+    def part(t, s, k):
+        return t[:, S * s:S * s + S].bitcast(dt.uint8) if k == 0 else t[:, S * s:S * s + S]
+    g.wait_ge(T.sem.h_c, len(out) + 2 * len(inn))
+    k = fused(g, T, topo, [([T.cores[s]], e, part(T.hq, s, 0), [part(T.sl, slot(T, topo, r, s), 0)], "s_c")
+                           for s, e in codes])
+    g.wait_ge(T.sem.h_s, len(inn))
+    k += fused(g, T, topo, [([T.cores[s]], e, part(T.hqs, s, 1), [part(T.sls, slot(T, topo, r, s), 1)], "s_s")
+                            for s, e in scales])
+    if VIA:
+        g.wait_ge(T.sem.h_b, len(inn) // 2)
+        at = [place2(slot(T, topo, r, s)) for s in far[:VIA]]
+        k += fused(g, T, topo, [([T.cores[s] for s in far[:VIA]], out, T.hb[:, 0:34], [T.lws[:, a:a + 34] for a in at],
+                                 "b_s")])
     g.wait_ge(T.sem.lo, k)
 
 
@@ -238,10 +231,10 @@ def rank_program(g, core, T, topo):
     N = len(T.cores)
     far, near, out, inn = ways(core, T, topo, me)
     here = chip_ranks(T, topo, me)
+    h0, o = here[0], here.index(me)
     gates = [r for r in far if me in taken_by(T, topo, r)]
-    like = [r for r in far if chip_ranks(T, topo, r).index(r) == here.index(me)]
-    assert [(r - me) % N for r in like] == [2, 4, 6] and here[1] == here[0] + 1
-    nv = len(far) * len(out) + len(near) * len(inn)
+    like = [r for r in far if chip_ranks(T, topo, r).index(r) == o]
+    assert [(r - me) % N for r in like] == [2, 4, 6] and here[1] == h0 + 1
     sent = []
 
     def sca(x):
@@ -266,6 +259,9 @@ def rank_program(g, core, T, topo):
     def cp(out, in_):
         step("c", "v", lambda q: q.tensor_copy(out["v"], in_["v"]), [out], [in_])
 
+    def turn(x, y):
+        step("c", "v", lambda q: q.transpose(x["v"], y["v"]), [x], [y])
+
     def fill(out, c):
         step("c", "v", lambda q: q.memset(out["v"], c), [out], [])
 
@@ -280,8 +276,9 @@ def rank_program(g, core, T, topo):
             step("c", "v", lambda q: q.tensor_copy(out["v"], in_["v"]), [out], [in_],
                  lambda q: q.activation(out["v"], in_["v"], F.Copy))
         else:
-            step("c", "v", lambda q: q.tensor_scalar(out["v"], in_["v"], scale, sca(bias), A.mult, A.add), [out],
-                 dic(in_, bias), lambda q: q.activation(out["v"], in_["v"], F.Identity, bias=sca(bias), scale=scale))
+            step("c", "v", lambda q: q.tensor_scalar(out["v"], in_["v"], sca(scale), sca(bias), A.mult, A.add), [out],
+                 dic(in_, scale, bias),
+                 lambda q: q.activation(out["v"], in_["v"], F.Identity, bias=sca(bias), scale=sca(scale)))
 
     def quant(n, a, b, tile, x0=0):
         o, p, x = ap(n, a, b), ap(n + "s", a, b), ap(tile, x0, x0 + 4 * (b - a))
@@ -299,46 +296,29 @@ def rank_program(g, core, T, topo):
     def dma(q, o, i, outs, ins):
         step("d", q, lambda e: e.dma_start(o, i), outs, ins)
 
-    def move(dn, c, sn, a, n):
-        for o, i in ((ap(dn, c, c + n, bc=u8), ap(sn, a, a + n, bc=u8)), (ap(dn + "s", c, c + n), ap(sn + "s", a, a + n))):
-            dma("y", o["v"], i["v"], [o], [i])
-
     def load(q, n, a, b, src):
         o = ap(n, a, b)
         dma(q, o["v"], src, [o], [])
 
-    def to_all(n, a, w, k, bc, sem, ranks):
-        src = ap(n, a, a + k, bc=bc)
+    def send(*xs):
+        ys = [([T.cores[r] for r in rs] if rs else [helpers[me]], e, x["v"], [y(r)["v"] for r in rs or [me]], s)
+              for rs, e, x, y, s in xs]
+        step("r", "g", lambda g: sent.append(fused(g, T, topo, ys)), [], [x[2] for x in xs])
 
-        def dst(r):
-            return ap(n, a + w * ((me - r) % N), a + w * ((me - r) % N) + k, bc=bc)["v"]
-        step(sem, "g", lambda g: sent.append(
-            same_to_all(g, T, topo, [(ranks, out), (near, inn)], src["v"], dst, T.sem[sem])), [], [src])
+    def slots(n, first, k, bc=None):
+        def at(r):
+            a = first(slot(T, topo, me, r))
+            return ap(n, a, a + k, bc=bc)
+        return at(me), at
 
-    def to_near(x, y, sem):
-        step(sem, "g", lambda g: sent.append(
-            same_to_all(g, T, topo, [(near, inn)], x["v"], lambda r: y["v"], T.sem[sem])), [], [x])
-
-    def to_helper(name, xs):
-        rid, pid, _ = topo.addr(helpers[me])
-
-        def call(g):
-            g.remote_dma_fused([RemoteDMATransfer(dst_ids=[DstId(rid=rid, pnc=pid)], dma_engine_mask=bits(e),
-                                                  remote_sem=T.sem[s], src=x["v"], dst=y["v"]) for x, y, e, s in xs],
-                               local_sem=T.sem.lo)
-            sent.append(sum(len(x[2]) for x in xs))
-        step(name, "g", call, [], [x[0] for x in xs])
-
-    def pass_on(a, w, ex):
-        def run_of(rs, at):
-            return a + w * ((rs[0] - at) % N), a + w * ((rs[-1] - at) % N + 1)
+    def pass_on(first, ex):
+        def run_of(rs):
+            return first(slot(T, topo, rs[0], me)), first(slot(T, topo, rs[-1], me) + 1)
         own, other = taken_by(T, topo, me), taken_by(T, topo, near[0])
-        tok = (ex + "_c", len(own) * len(out) + len(inn))
-        arrive("lw", *run_of(own, me), tok)
-        arrive("lw", *run_of(near, me), tok)
-        arrive("lw", *run_of(other, me), (ex + "_cf", len(inn)))
-        arrive("lws", a + w, a + w * N, (ex + "_s", nv))
-        to_near(ap("lw", *run_of(own, me), bc=u8), ap("lw", *run_of(own, near[0]), bc=u8), ex + "_cf")
+        arrive("lw", *run_of(own), (ex + "_c", len(own) * len(out)))
+        arrive("lw", *run_of(other), (ex + "_cf", len(inn)))
+        x = ap("lw", *run_of(own), bc=u8)
+        send((near, inn, x, lambda r: x, ex + "_cf"))
 
     def c(n, k=0):
         return ap(n, k, k + 1)
@@ -364,10 +344,9 @@ def rank_program(g, core, T, topo):
     iota("xr", 32, [[-1, 4], [0, 8]])
     iota("c4", 16, [[0, 4], [1, 4]])
     iota("idx", 16, [[16, 4], [-508, 4]])
-    iota("c4x", 4, [[128 if me == here[0] else -128, 2], [16, 2]], 0 if me == here[0] else 128)
+    iota("c4x", 4, [[128 - 256 * o, 2], [16, 2]], 128 * o)
     iota("c256", 8, [[2, 8]], 256)
     iota("c32", 8, [[32, 8]])
-    iota("r34", 272, [[0, 8], [256, 34]])
     iota("frow", 256, [[1, 256]])
     iota("p256", 64, [[16, 4], [1, 4], [4, 4]], 256)
     zb, pi, lo, pf, io = ap("zb", 0, 128), ap("pi", 0, 4), c("lo"), c("pf"), "io"
@@ -377,14 +356,16 @@ def rank_program(g, core, T, topo):
     fill(ap("rs8", 0, 64, 8), 3.5)
     fill(ap("m32", 0, 64), -32.0)
     fill(ap("eb", 0, 528), 0.0)
-    fill(ap("fit8", 8, 16), 0)
+    fill(ap("fit", 8, 16), 0.0)
     fill(ap("vv", 32, 40), 0.0)
     fill(ap("odw", 0, 16), -1.0)
-    fill(ap("odw", N - 1 - me, 16, 8), 7.0)
+    fill(ap("odw", N - 1 - h0, 16, 8), 7.0)
+    fill(ap("f0", 0, 7), 0.0)
     cp(pf, c("pi"))
     ts(ap("hi2", 0, 2), ap("pj", 0, 2), 240, A.bitwise_and)
     ts(ap("lo2", 0, 2), ap("pj", 0, 2), 15, A.bitwise_and)
     cp(lo, c("lo2"))
+    c16 = ap(io, 0, 32, 16)
     for a, n in ((0, "hi2"), (6, "hi2"), (8, "lo2"), (14, "lo2")):
         cp(ap("xt", a, a + 2), ap(n, 0, 2))
     ts(ap("tie", 0, 128), ap(io, 0, 128), pf, A.is_lt, TINY, A.mult)
@@ -396,25 +377,43 @@ def rank_program(g, core, T, topo):
     tt(ap("yx", 4, 8), ap("bi", 0, 4), ap(io, 0, 8, 2), A.add)
     cp(ap("l1", 0, 8), ap("yx", 0, 8))
     ts(ap("l8", 0, 8), ap("yx", 0, 8), 8.0, A.mult, 7.0, A.add)
-    ts(ap("l34", 0, 8), ap("yx", 0, 8), 34.0, A.mult, 31.0, A.add)
-    ts(ap("gx0", 0, 4), ap("yx", 4, 8), 16.0, A.mult, -41.0, A.add)
-    ts(ap("gx", 0, 4), ap("gx0", 0, 4), 7.0, A.max, 55.0, A.min)
+    ts(ap("lv0", 0, 8), ap("yx", 0, 8), 1.0, A.min, 31.0, A.mult)
+    tt(ap("lv1", 0, 8), ap("lv0", 0, 8), ap("yx", 0, 8), A.add)
+    ts(ap("lv", 0, 8), ap("lv1", 0, 8), 31.0, A.add)
+    ts(ap("gx0", 0, 4), ap("yx", 4, 8), 16.0, A.mult, 8.0 * o - 41.0, A.add)
+    ts(ap("gx", 0, 4), ap("gx0", 0, 4), 8.0 * o + 7.0, A.max, 8.0 * o + 55.0, A.min)
     lq7, lrs, gis, grs = ap("l1", 0, 4), ap("l1", 4, 8), ap("l8", 0, 4), ap("l8", 4, 8)
     ts(ap("jc", 0, 2), ap("pi", 0, 2), 3, A.bitwise_and)
     ts(c("jc", 2), c("pi"), 4, A.logical_shift_right, 3, A.bitwise_and)
     ts(ap("jc", 3, 7), pi, 4, A.logical_shift_right, 1, A.bitwise_and)
     ts(ap("jc", 5, 7), ap("jc", 5, 7), 2.0, A.add)
+    ts(ap("lz", 0, 4), ap("jc", 3, 7), 7.0, A.add)
     cp(c("q4f"), c("jc"))
     ts(c("qi"), c("pi"), 2, A.logical_shift_right, 3, A.bitwise_and)
     cp(c("qq4"), c("qi"))
     aff(c("corr4"), c("q4f"), 512.0, c("qq4"))
     ts(ap("wt4", 0, 16), ap("c4", 0, 16), c("q4f"), A.is_equal, -1000000.0, A.mult)
     ts(c("hf"), c("pi"), 1, A.logical_shift_right, 7, A.bitwise_and)
-    ts(c("lll"), c("hf"), 32.0, A.mult, lo, A.add)
+    ts(c("h14"), c("hf"), 2.0, A.min, 14.0, A.mult)
+    aff(c("l14"), c("h14"), 1.0, lo)
+    ts(c("lll"), c("hf"), 32.0, A.mult, c("l14"), A.add)
+    ts(ap("c14", 0, 8), ap("c32", 0, 8), 64.0, A.min, 0.4375, A.mult)
+    tt(ap("c270", 0, 8), ap("c14", 0, 8), ap("c256", 0, 8), A.add)
     aff(c("lo256"), lo, 1.0, 256.0)
     aff(c("lom"), lo, 2.0, -128.0)
     aff(c("corr"), lo, 512.0, -7680.0)
     aff(ap("c35", 0, 32), ap("xr", 0, 32), 1.0, 3.5)
+    ts(ap("lme", 0, 2), c16, lo, A.add, 32.0 * me, A.add)
+    cp(c("lq1"), lo)
+    ts(c("mo", 0), c("bi"), float(o), A.is_equal)
+    ts(c("mo", 1), c("bi"), float(o), A.not_equal)
+    ts(ap("r0", 0, 2), ap("pi", 0, 2), 3, A.logical_shift_right, 3, A.bitwise_and)
+    tt(ap("r1", 0, 2), ap("r0", 0, 2), ap(io, h0, h0 + 8, 4), A.add)
+    ts(ap("r2", 0, 2), ap("r1", 0, 2), 7, A.bitwise_and)
+    ts(ap("frac", 0, 2), ap("r2", 0, 2), -0.125, A.mult, 0.875, A.add)
+    cp(ap("r3", 0, 8), ap(io, h0, h0 + 8))
+    ts(ap("r4", 0, 8), ap("r3", 0, 8), 7, A.bitwise_and)
+    ts(ap("fr", 0, 8), ap("r4", 0, 8), -0.125, A.mult, 0.875, A.add)
     ts(ap("m16", 0, 128), ap("k2", 0, 256, 2), c("lom"), A.is_equal)
     aff(ap("wt", 0, 128), ap("m16", 0, 128), -1000512.0, 512.0)
     ts(c("ind4"), pf, 64.0, A.is_lt, 4.0, A.mult)
@@ -432,12 +431,10 @@ def rank_program(g, core, T, topo):
 
     quant("tq", 0, 128, "tbx")
     quant("tq", 128, 256, "tbx", 512)
-    to_helper("h1", [(ap("tq", 0, 128, bc=u8), ap("hq", 0, 128, bc=u8), out + inn, "h_c")])
-    h = len(inn) // 4
-    to_helper("h2", [(ap("tq", 128, 192, bc=u8), ap("hq", 128, 192, bc=u8), inn[:h], "h_c"),
-                     (ap("tq", 192, 256, bc=u8), ap("hq", 192, 256, bc=u8), inn[h:2 * h], "h_c"),
-                     (ap("tqs", 0, 256), ap("hqs", 0, 256), inn[2 * h:], "h_s")])
-    move("sl", 0, "tq", 32 * me, 32)
+    send(([], out + inn, ap("tq", 0, 128, bc=u8), lambda r: ap("hq", 0, 128, bc=u8), "h_c"))
+    send(([], inn, ap("tq", 128, 256, bc=u8), lambda r: ap("hq", 128, 256, bc=u8), "h_c"))
+    send(([], inn, ap("tqs", 0, 256), lambda r: ap("hqs", 0, 256), "h_s"))
+    pick("sl", 32 * o, 32 * o + 32, "tq", 0, 256, "lme", 0, 2)
     mm(bank("dv", 0), "uq", 0, "tq", 0, 128)
     mm(bank("dv", 1), "uq", 0, "tq", 128, 256)
     for k, (own, oth) in enumerate(((0, 0), (0, 128), (128, 0), (128, 128))):
@@ -449,12 +446,16 @@ def rank_program(g, core, T, topo):
             mm(bank("pp", k), "uq", 0, "tq", oth, oth + 128, True, False)
             mm(bank("pp", k), "tq", own, "uq", 128, 256, False, True)
     act(ap("junk", 0, 128), bank("dv", 0), F.Sign, bias=-TINY, accum=c("ft", 0))
-    aff(c("ft", 2), c("ft", 0), 1.0, 256.0 + (N - 1 - me) / 4.0)
     act(ap("junk", 128, 256), bank("dv", 1), F.Sign, bias=-TINY, accum=c("ft", 1))
     act(ap("junk", 256, 384), bank("pp", 1), F.Sign, bias=-TINY, scale=-1.0, accum=c("ss", 0))
     act(ap("junk", 384, 512), bank("pp", 2), F.Sign, bias=TINY, scale=-1.0, accum=c("ss", 1))
-    ts(c("vl"), c("ft", 1), c("ft", 2), A.add, 4.0, A.mult)
-    to_all("vl", 0, 8, 1, None, "a_v", far)
+    ts(c("v0"), c("ft", 1), c("ft", 0), A.add, 0.5, A.mult)
+    send((near, inn, c("v0"), lambda r: c("vn"), "a_n"))
+    arrive("vn", 0, 1, ("a_n", len(inn)))
+    aff(c("vm"), c("v0"), c("mo", 0))
+    aff(c("f0", 7), c("vn"), c("mo", 1), c("vm"))
+    send((like, out, c("f0", 7), lambda r: c("f0", 7 + slot(T, topo, h0, r) // 2), "a_v"))
+    arrive("f0", 8, 11, ("a_v", len(like) * len(out)))
     for h, k in ((0, 0), (1, 3)):
         w = ap("cmp", 128 * h, 128 * h + 128)
         tt(w, bank("pp", k), ap("tie", 0, 128), A.is_lt)
@@ -468,14 +469,21 @@ def rank_program(g, core, T, topo):
         for k in (0, 1):
             ts(c("jl4", 2 * e + k), bank("dv", 2 + e, k, k + 1), bank("dv", 2 + e, k + 2, k + 3), A.add)
         aff(ap("lt", 4 * e, 4 * e + 4), bank("dv", 2 + e, 0, 4))
-    pick("lw", 0, 32, "tq", 0, 256, "jl4", 0, 2)
+    pick("lw", 32 * o, 32 * o + 32, "tq", 0, 256, "jl4", 0, 2)
 
-    to_all("lw", 0, 32, 32, u8, "a_c", gates)
-    to_all("lws", 0, 32, 32, None, "a_s", far)
-    pass_on(0, 32, "a")
+    x, y = slots("lw", lambda s: 32 * s, 32, u8)
+    send((gates, out, x, y, "a_c"), (near, inn, x, y, "a_s"))
+    x, y = slots("lws", lambda s: 32 * s, 32)
+    send((far, out, x, y, "a_s"), (near, inn, x, y, "a_s"))
+    tok = ("a_s", len(far) * len(out) + 2 * len(inn))
+    arrive("lw", 32 - 32 * o, 64 - 32 * o, tok)
+    arrive("lws", 32 - 32 * o, 64 - 32 * o, tok)
+    arrive("lws", 64, 256, tok)
+    pass_on(lambda s: 32 * s, "a")
     pick("xw", 128, 160, "tq", 0, 256, "jl4", 2, 4)
     quant("lq", 0, 128, "lt")
-    move("lw", 288, "lq", 0, 2)
+    mine2, near2 = place2(o), place2(1 - o)
+    pick("lw", mine2 + 32, mine2 + 48, "lq", 0, 128, "lq1", 0, 1)
     quant("cn", 64, 192, "nzx")
     for b in range(4):
         mm(bank("dv", b), "eh", 128 * b, "cn", 64, 192, True, False)
@@ -483,74 +491,91 @@ def rank_program(g, core, T, topo):
         mm(bank("pp", b), "eh", 128 * b, "cn", 64, 192)
         aff(ap("dn", b, 256, 4), bank("pp", b, 32, 96))
 
-    arrive("vl", 8, 64, ("a_v", nv))
-    cp(ap("vi", 0, 8), ap("vl", 0, 64, 8))
-    aff(ap("k1", 0, 64), ap("vi", 0, 8, off=lrs))
-    tt(ap("cm", 0, 64), ap("vi", 0, 8, off=lq7), ap("k1", 0, 64), A.is_gt)
+    for b in (0, 1):
+        aff(ap("xk", 32 * b, 32 * b + 32), ap("f0", 0, 11, off=ap("lz", 2 * b, 2 * b + 2)), 1.0, c("frac", b))
+    turn(ap("ak", 0, 64), ap("xk", 0, 64))
+    turn(ap("ak2", 0, 64), ap("xk", 0, 64))
+    tt(ap("cm", 0, 64), ap("ak2", 0, 64, off=gis), ap("ak", 0, 64), A.is_gt)
     scan(ap("sc", 0, 64), ap("rs8", 0, 64), ap("cm", 0, 64), A.max, A.subtract)
-    g0, mine, c16 = ap("sc", 7, 64, 8), c("sc", 7), ap(io, 0, 32, 16)
+    g0, mine = ap("sc", 7, 64, 8), c("sc", 8 * o + 7)
     ts(ap("ms", 0, 8), g0, mine, A.add, 0.0, A.not_equal)
     scan(ap("st0", 0, 8), ap("ms", 0, 8), ap("m32", 0, 8))
     ts(ap("ofa", 0, 2), c16, c("st0", 7), A.add, c("lo256"), A.add)
     ts(c("go"), mine, 0.0, A.is_gt, 128.0, A.mult)
     ts(ap("ofx", 0, 2), c16, c("go"), A.add, lo, A.add)
+    ts(ap("tk", 0, 8), g0, 0.0, A.is_lt)
     pick("cn", 32, 64, "lw", 0, 256, "ofa", 0, 2)
     for b in range(4):
         mm(bank("dv", b), "eh", 128 * b, "cn", 32, 160, False, True)
         aff(ap("vt", b, 128, 4), bank("dv", b, 0, 32))
     quant("xw", 0, 128, "vt")
-    pick("lw", 256, 288, "xw", 0, 160, "ofx", 0, 2)
+    pick("lw", mine2, mine2 + 32, "xw", 0, 160, "ofx", 0, 2)
 
-    to_all("lw", 256, 34, 34, u8, "b_c", gates)
-    to_all("lws", 256, 34, 34, None, "b_s", far)
-    pass_on(256, 34, "b")
+    def count(k, pk, n, a, at):
+        mm(bank("pp", pk), "uq", 0, n, a, a + 128)
+        ts(ap("cb", 32 * k, 32 * k + 32), bank("pp", pk, at, at + 32), 0.0, A.is_gt, c("tk", k), A.mult)
+        scan(ap("f1", 32 * k, 32 * k + 32), ap("cb", 32 * k, 32 * k + 32), ap("zb", 0, 32), A.add, A.add)
+    count(o, 0, "xw", 0, 0)
+    x, y = slots("lw", place2, 34, u8)
+    send((gates, out, x, y, "b_c"), (near, inn, x, y, "b_cn"))
+    x, y = slots("lws", place2, 34)
+    h = len(inn) // 2
+    if VIA:
+        send((near, inn[:h], x, y, "b_sn"), ([], inn[h:], x, lambda r: ap("hb", 0, 34), "h_b"))
+    else:
+        send((near, inn, x, y, "b_sn"))
+    send((far, out, c("f1", 32 * o + 31), lambda r: c("f1", 62 + slot(T, topo, me, r)), "b_v"))
+    if far[VIA:]:
+        send((far[VIA:], out, x, y, "b_s"))
+    arrive("lw", near2, near2 + 34, ("b_cn", len(inn)))
+    arrive("lws", near2, near2 + 34, ("b_sn", h if VIA else len(inn)))
+    arrive("lws", place2(2), place2(N), ("b_s", len(far) * len(out)))
+    arrive("f1", 64, 70, ("b_v", len(far) * len(out)))
+    count(1 - o, 3, "lw", near2 - 94, 94)
+    pass_on(place2, "b")
 
     plans = [slice_plan(helpers[r], T, topo, r) for r in range(N) if r != me]
     for k, n, s in ((0, "sl", "s_c"), (1, "sls", "s_s")):
-        arrive(n, 32, 256, (s, sum(len(e) for p in plans for d, e in p[k] if d == me)))
+        tok = (s, sum(len(e) for p in plans for d, e in p[k] if d == me))
+        arrive(n, 32 - 32 * o, 64 - 32 * o, tok)
+        arrive(n, 64, 256, tok)
     tt(ap("mi", 0, 32), ap("sc", 0, 64, off=ap("l8", 0, 2)), ap("c35", 0, 32), A.not_equal)
     scan(ap("st4", 0, 32), ap("mi", 0, 32), ap("m32", 0, 32))
     ts(ap("ofs", 0, 8, 2), ap("st4", 7, 32, 8), lo, A.add, 256.0, A.add)
     ts(ap("ofs", 1, 8, 2), ap("st4", 7, 32, 8), lo, A.add, 272.0, A.add)
     pick("st", 0, 128, "sl", 0, 256, "ofs", 0, 8)
     for n, b, sem in (("st", u8, "p_c"), ("sts", None, "p_s")):
-        to_near(ap(n, 0, 128, bc=b), ap(n, 128, 256, bc=b), sem)
+        send((near, inn, ap(n, 0, 128, bc=b), lambda r, n=n, b=b: ap(n, 128, 256, bc=b), sem))
         arrive(n, 128, 256, (sem, len(inn)))
 
-    cp(ap("vint", 0, 8), ap("vl", 0, 64, 8))
-    ts(ap("fit8", 0, 8), ap("vint", 0, 8), 65528, A.bitwise_and)
-    ts(ap("kr", 0, 8), ap("vint", 0, 8), 7, A.bitwise_and)
     act(ap("q0", 0, 64), ap("sc", 0, 64, off=grs), F.Abs)
-    tt(ap("fd", 0, 8), ap("fit8", 0, 8), ap("fit8", 1, 9), A.subtract)
+    tt(ap("fit", 0, 8), ap("ak", 0, 64, 8), ap("fr", 0, 8), A.subtract)
+    tt(ap("fd", 0, 8), ap("fit", 0, 8), ap("fit", 1, 9), A.subtract)
     tt(ap("miss0", 0, 64), ap("sc", 0, 64, off=gis), ap("q0", 0, 64), A.not_equal)
     aff(ap("fde", 0, 64), ap("fd", 0, 8, off=lq7))
     scan(ap("hfs", 0, 64), ap("miss0", 0, 64), ap("fde", 0, 64))
     scan(ap("hhs", 0, 64), ap("miss0", 0, 64), ap("m32", 0, 64))
     fh = ap("hfs", 7, 64, 8)
-    ts(ap("ba", 0, 8), g0, 0.0, A.is_gt, 256.0, A.mult)
-    tt(ap("bb", 0, 8), ap("ba", 0, 8), fh, A.add)
-    ts(ap("bc", 0, 8), ap("bb", 0, 8), 1792.0, A.max, 2048.0, A.min)
+    tt(ap("bb", 0, 8), ap("tk", 0, 8), fh, A.mult)
+    ts(ap("bc", 0, 8), ap("bb", 0, 8), 96.0, A.max)
     tt(ap("bd", 0, 8), fh, ap("bc", 0, 8), A.subtract)
-    tt(ap("kb", 0, 8), ap("bd", 0, 8), ap("kr", 0, 8), A.add)
+    tt(ap("kb", 0, 8), ap("bd", 0, 8), ap("fr", 0, 8), A.add)
     aff(ap("kx", 0, 64), ap("kb", 0, 8, off=lrs))
     tt(ap("nd", 0, 64), ap("kb", 0, 8, off=lq7), ap("kx", 0, 64), A.subtract)
-    ts(ap("tk", 0, 8), g0, 0.0, A.is_lt)
-    tt(ap("o1", 0, 8), ap("tk", 0, 8), ap("c256", 0, 8), A.mult)
+    tt(ap("o1", 0, 8), ap("tk", 0, 8), ap("c270", 0, 8), A.mult)
     aff(ap("vv", 0, 8), ap("q0", 0, 64, 8), -32.0, 112.0)
     tt(ap("vv", 8, 16), ap("o1", 0, 8), ap("c32", 0, 8), A.add)
-    aff(ap("vv", 16, 24), ap("hhs", 7, 64, 8), 1.0625, 528.0)
+    aff(ap("w1", 0, 8), ap("hhs", 7, 64, 8), 1.0625, 640.0)
+    ts(ap("w2", 0, 8), ap("hhs", 7, 64, 8), -192.0, A.min, 0.4375, A.mult)
+    tt(ap("vv", 16, 24), ap("w1", 0, 8), ap("w2", 0, 8), A.add)
     aff(ap("vv", 24, 32), ap("hhs", 7, 64, 8), 0.125, 32.0)
     tt(ap("ve", 0, 32), ap("vv", 0, 32), ap("vv", 1, 33), A.subtract)
     aff(ap("ve", 32, 64), ap("ve", 0, 8, off=ap("l1", 0, 2)))
     aff(ap("kk", 0, 3), ap("vv", 8, 32, 8), 1.0, lo)
     ts(ap("ode", 0, 8), g0, pf, A.add, 3.5, A.not_equal)
 
-    for k, pk in ((0, 0), (136, 3)):
-        mm(bank("pp", pk, 0, 136), "uq", 0, "lw", 256 + k, 392 + k)
-        ts(ap("c1", k, k + 136), bank("pp", pk, 0, 136), 0.0, A.is_gt, 8.0, A.mult)
-    scan(ap("s1", 0, 272), ap("r34", 0, 272), ap("c1", 0, 272), A.min, A.add)
-    aff(ap("x1b", 0, 64), ap("s1", 0, 272, off=ap("l34", 4, 8)))
-    tt(ap("k1b", 0, 64), ap("s1", 0, 272, off=ap("l34", 0, 4)), ap("nd", 0, 64), A.add)
+    aff(ap("x1b", 0, 64), ap("f1", 0, 70, off=ap("lv", 4, 8)))
+    tt(ap("k1b", 0, 64), ap("f1", 0, 70, off=ap("lv", 0, 4)), ap("nd", 0, 64), A.add)
     tt(ap("cmb", 0, 64), ap("x1b", 0, 64), ap("k1b", 0, 64), A.is_lt)
     scan(ap("scb", 0, 64), ap("rs8", 0, 64), ap("cmb", 0, 64), A.max, A.subtract)
     act(ap("qx", 0, 64), ap("scb", 0, 64, off=ap("gx", 0, 4)), F.Abs)
@@ -560,34 +585,30 @@ def rank_program(g, core, T, topo):
     for k, s in enumerate((39, 47, 55, 7)):
         ts(ap("of", 4 * k, 4 * k + 4), c4x, c("bs", s), A.add, c("kk", 0), A.add)
     pick("sb", 0, 192, "st", 0, 256, "of", 0, 12)
-    pick("wl", 0, 16, "lw", 288, 528, "lll", 0, 1)
+    pick("wl", 0, 16, "lw", 288, 556, "lll", 0, 1)
     for k in (0, 1):
         mm(bank("pp", 1 + k), "eh", 128 * k, "wl", 0, 128, True, False)
         mm(bank("pp", 1 + k), "eh", 128 * k + 256, "wl", 0, 128, False, True)
         aff(ap("jv", k, 32, 2), bank("pp", 1 + k, 0, 16), 2.0)
 
-    w, col = len(out) // 4, 32 * here[0]
-
-    def to_like(n, b, sem, es):
-        step(sem, "g", lambda g: sent.append(one_each(
-            g, T, topo, list(zip(like, es)), lambda r: ap(n, 64 * like.index(r), 64 * like.index(r) + 64, bc=b)["v"],
-            lambda r: ap("fw" + n[2:], col, col + 64, bc=b)["v"], T.sem[sem])), [], [ap(n, 0, 192)])
-    to_like("sb", u8, "c_c", (out[:2 * w], out[2 * w:3 * w], out[3 * w:]))
-    to_like("sbs", None, "c_s", (out[2 * w:], out[:w], out[w:2 * w]))
+    w, col = len(out) // 4, 32 * h0
+    for n, b, sem, es in (("", u8, "c_c", (out[:2 * w], out[2 * w:3 * w], out[3 * w:])),
+                          ("s", None, "c_s", (out[2 * w:], out[:w], out[w:2 * w]))):
+        y = ap("fw" + n, col, col + 64, bc=b)
+        send(*[([r], es[k], ap("sb" + n, 64 * k, 64 * k + 64, bc=b), lambda r, y=y: y, sem) for k, r in enumerate(like)])
     pick("fw", col, col + 64, "st", 0, 256, "of", 12, 16)
 
     ts(ap("ofc", 0, 2), c16, c("bs", 15), A.add, c("kk", 1), A.add)
     ts(ap("ofc", 2, 4), c16, c("bs", 23), A.add, c("kk", 2), A.add)
     ts(ap("jl", 0, 7), ap("jc", 0, 7), c("bs", 31), A.add)
-    pick("cn", 0, 64, "lw", 0, 528, "ofc", 0, 4)
+    pick("cn", 0, 64, "lw", 0, 556, "ofc", 0, 4)
     mm(bank("pp", 0), "uq", 0, "cn", 0, 128, True, False)
     mm(bank("pp", 0), "cn", 0, "uq", 128, 256, False, True)
     for b in range(4):
         mm(bank("dv", b), "eh", 128 * b, "cn", 0, 128)
         aff(ap("dc", b, 256, 4), bank("dv", b, 0, 64))
     aff(ap("gb", 16, 96), ap("jv", 0, 32, off=ap("jl", 2, 7)))
-    o, i = ap("cj", 0, 64), ap("gb", 32, 96)
-    step("c", "v", lambda q: q.transpose(o["v"], i["v"]), [o], [i])
+    turn(ap("cj", 0, 64), ap("gb", 32, 96))
     ts(ap("ntie", 0, 64), ap("cj", 0, 64), c("gb", 16), A.is_gt, -TINY, A.mult)
     tt(ap("oh", 0, 64), bank("pp", 0, 0, 64), ap("ntie", 0, 64), A.is_gt)
     quant("cx", 0, 128, "oh")
@@ -595,7 +616,7 @@ def rank_program(g, core, T, topo):
     ts(ap("l4", 0, 16), bank("pp", 3, 0, 16), c("q4f"), A.add)
     tt(ap("vt2", 0, 256), ap("dn", 0, 256, off=ap("l4", 0, 16)), ap("dc", 0, 256), A.add)
     quant("cn", 64, 192, "vt2")
-    ts(c("t128"), c("scb", 7), 0.0, A.is_lt, 128.0, A.mult)
+    ts(c("t128"), c("scb", 8 * o + 7), 0.0, A.is_lt, 128.0, A.mult)
     ts(ap("sel", 0, 16), bank("pp", 3, 0, 16), c("t128"), A.is_lt, 64.0, A.mult)
     tt(ap("off", 0, 16), ap("sel", 0, 16), ap("idx", 0, 16), A.add)
     scan(ap("xs", 0, 16), ap("wt4", 0, 16), ap("off", 0, 16), A.add, A.max)
@@ -608,7 +629,7 @@ def rank_program(g, core, T, topo):
     ts(ap("fl", 0, 16), ap("fs", 15, 256, 16), c("corr"), A.add)
     ts(ap("ode", 8, 16), ap("scb", 7, 64, 8), pf, A.add, 3.5, A.not_equal)
     scan(ap("odc", 0, 16), ap("ode", 0, 16), ap("odw", 0, 16))
-    aff(ap("odr", 0, 2), ap("odc", 7, 16, 8), 1.0, float(me))
+    aff(ap("odr", 0, 2), ap("odc", 7, 16, 8), 1.0, float(h0))
     for t in (0, 1):
         x = ap("odr", t, t + 1, p=(0, 8))
         dma("y", T.od[t:t + 1, 0:8], x["v"], [], [x])

from concourse.bass import DstId, RemoteDMATransfer
from concourse.mybir import dt, AluOpType, AxisListType, ActivationFunctionType

A = AluOpType
F = ActivationFunctionType
CODE, PLANE, F32, BF, I32, U16 = "float8_e4m3fn_x4", "uint8", "float32", "bfloat16", "int32", "uint16"
SCRATCH, PART = {}, {}
TINY = 2.0 ** -100
ORDER = [23, 5, 19, 0, 6, 18, 77, 7, 1, 31, 29, 30, 2, 44, 63, 78, 55, 45, 38, 79, 96, 95, 94, 104, 10, 97, 99, 102, 105, 15, 98, 100, 3, 43, 101, 75, 42, 111, 103, 119, 35, 117, 112, 113, 39, 37, 114, 4, 121, 118, 159, 130, 122, 124, 125, 120, 132, 131, 34, 8, 20, 133, 33, 36, 115, 116, 106, 136, 123, 126, 76, 135, 92, 137, 56, 134, 143, 138, 80, 127, 107, 41, 14, 139, 140, 128, 9, 142, 149, 32, 81, 67, 129, 40, 144, 57, 24, 168, 28, 150, 64, 82, 161, 69, 21, 47, 48, 166, 172, 173, 74, 151, 141, 152, 145, 73, 148, 170, 22, 65, 26, 174, 175, 49, 46, 162, 176, 147, 27, 146, 177, 167, 156, 178, 83, 163, 164, 72, 181, 160, 11, 13, 179, 153, 216, 68, 180, 182, 154, 158, 184, 157, 155, 215, 217, 185, 192, 165, 218, 110, 188, 189, 207, 108, 186, 219, 53, 193, 187, 190, 191, 183, 194, 208, 221, 195, 16, 109, 196, 197, 232, 220, 198, 86, 222, 199, 51, 231, 54, 171, 66, 223, 71, 228, 233, 201, 234, 52, 224, 200, 209, 238, 210, 203, 70, 229, 225, 226, 50, 59, 87, 202, 230, 211, 227, 204, 93, 205, 237, 25, 84, 240, 212, 88, 169, 239, 58, 85, 241, 206, 60, 253, 89, 242, 90, 252, 243, 235, 236, 91, 244, 254, 288, 213, 245, 300, 265, 246, 214, 264, 255, 257, 258, 248, 256, 247, 266, 259, 268, 267, 273, 250, 279, 269, 280, 17, 260, 271, 295, 251, 270, 274, 249, 281, 296, 282, 301, 283, 297, 298, 275, 62, 277, 262, 276, 261, 284, 289, 285, 278, 272, 12, 61, 290, 286, 302, 291, 287, 292, 263, 299, 293, 304, 294, 303, 312, 311, 313, 305, 314, 315, 308, 306, 318, 320, 319, 316, 307, 309, 310, 317]
SCALAR = (61, 65, 69, 70, 71, 72, 85, 97, 98, 101, 110, 127, 128, 134, 141, 148, 150, 155, 158, 165, 167, 169, 171, 172, 173, 185, 189, 196, 212, 219, 226, 229, 231, 234, 236, 237, 239, 251, 253, 256, 259, 263, 268, 272, 274, 276, 278, 279, 294, 302, 306, 312)
VIA = 6


def _bufs():
    def b(dtype, **kw):
        for k in kw:
            SCRATCH[k] = ("sbuf", [128, kw[k]], dtype)

    def parts(name, dtype, **kw):
        n = 0
        for k in kw:
            PART[k] = (name, n)
            n += kw[k]
        SCRATCH[name] = ("sbuf", [128, n], dtype)

    def q(**kw):
        for k in kw:
            SCRATCH[k] = ("sbuf", [128, kw[k]], CODE)
            SCRATCH[k + "s"] = ("sbuf", [128, kw[k]], PLANE)
    parts("big", BF, vt2=256, vt=128, lt=8, xt=16, nzx=256, wx=512)
    b(BF, tbx=1024, ux=1024, u4=8, eb=528, oh=512, oh2=512, w4t=512, zb=128, cmp=256, junk=512, v0=8, vn=8, f0=16,
      cb=64, f1=72)
    parts("bconst", BF, io=128, tie=128, k2=256, qd4=128, m16=128)
    parts("fconst", F32, lo=8, pf=8, lo256=8, lom=8, q4f=8, qq4=8, ind4=8, corr=8, corr4=8, c4=16,
          wt4=16, idx=16, c4x=8, c256=8, c32=8, xr=32, c35=32, rs8=64, m32=64, odw=16, gx0=8, p256=64, wt=128,
          mo=8, frac=8, fr=8, lv0=8, lv1=8, c14=8, c270=8, h14=8, l14=8)
    parts("fown", F32, ft=8, ss=8, s64=8, sa=256, vm=8)
    b(F32, jv=32, gb=96, cj=64, ntie=64, dn=256, dc=256, xk=64, ak=64, ak2=64, yo=256, frow=256)
    parts("flist", F32, cm=64, sc=64, ms=8, st0=8, go=8, q0=64, miss0=64, fd=8, fde=64, hfs=64, hhs=64,
          tk=8, bb=8, bc=8, bd=8, kb=8, kx=64, nd=64, mi=32, st4=32, vv=40, ve=64, o1=8, kk=8,
          k1b=64, x1b=64, cmb=64, scb=64, qx=64, miss=64, bs=64, t128=8, sel=16, off=16, xs=16,
          ode=16, odc=16, odr=8, fs=256, fit=16, w1=8, w2=8)
    parts("iconst", I32, pi=8, pj=8, hi2=8, lo2=8, yx=8, bi=8, jc=8, hf=8, qi=8, r0=8, r1=8, r2=8, r3=8, r4=8)
    parts("lists", U16, jl4=4, l1=8, l8=8, lv=8, gx=4, lll=2, ofa=2, ofx=2, ofs=8, of=16,
          ofc=4, jl=8, jw=16, l4=16, xl=4, fl=16, lz=4, lme=2, lq1=2)
    q(uq=256, tq=256, xq=128, oq=256, lq=128, eh=512, lw=556, xw=160, cn=192, wl=144, sl=256, st=256, sb=192,
      fw=320, oq2=256, w4q=128, cx=128, hq=256)
    b(PLANE, hb=34)
    SCRATCH["dv"] = ("psum", [128, 2048], F32)
    SCRATCH["pp"] = ("psum", [128, 2048], F32)


_bufs()
SEMAPHORES = ["cv", "cs", "ct_", "cg", "lo", "a_n", "a_v", "a_c", "a_s", "b_c", "b_s", "b_cn", "b_sn", "b_v", "c_c",
              "c_s", "s_c", "s_s", "h_c", "h_s", "h_b", "p_c", "p_s", "a_cf", "b_cf"] + ["d%d" % i for i in range(32)]


def find_helpers(T, topo):
    out = []
    for c in T.cores:
        for k in topo.cores_of(c):
            if k in T.cores or k in out or topo.die(k) == topo.die(c):
                continue
            if all(topo.may_write(k, x) for x in T.cores):
                out.append(k)
                break
    return out


def chip_ranks(T, topo, r):
    return [x for x in range(len(T.cores)) if topo.chip(T.cores[x]) == topo.chip(T.cores[r])]


def slot(T, topo, r, at):
    return (r - chip_ranks(T, topo, at)[0]) % len(T.cores)


def place2(s):
    return 256 + 34 * s + 14 * min(s, 2)


def ways(core, T, topo, me):
    n, here = len(T.cores), chip_ranks(T, topo, me)
    far = [(here[-1] + 1 + i) % n for i in range(n - len(here))]
    near = [r for r in here if r != me]
    out = topo.engines(core, T.cores[far[0]])
    inn = [e for e in topo.engines(core, T.cores[near[0]]) if e not in out]
    return far, near, out, inn


def taken_by(T, topo, d):
    n, here = len(T.cores), chip_ranks(T, topo, d)
    far = [(here[-1] + 1 + i) % n for i in range(n - len(here))]
    return far[:len(far) // 2] if d == here[0] else far[len(far) // 2:]


def fused(g, T, topo, xs):
    def at(c):
        rid, pid, _ = topo.addr(c)
        return DstId(rid=rid, pnc=pid)
    g.remote_dma_fused([RemoteDMATransfer(dst_ids=[at(c) for c in cs], dma_engine_mask=sum(1 << k for k in e),
                                          remote_sem=T.sem[s], srcs=[x], dsts=ys) for cs, e, x, ys, s in xs],
                       local_sem=T.sem.lo)
    return sum(len(x[1]) for x in xs)


def slice_plan(core, T, topo, r):
    far, near, out, inn = ways(core, T, topo, r)
    k = len(out) - len(far)
    codes = [(s, out[2 * i:2 * i + 2]) for i, s in enumerate(far[:k])] + \
            [(s, out[2 * k + i:2 * k + i + 1]) for i, s in enumerate(far[k:])]
    m = len(far) - k
    scales = [(s, out[i:i + 1]) for i, s in enumerate(far[:m])] + \
             [(s, out[m + 2 * i:m + 2 * i + 2]) for i, s in enumerate(far[m:])]
    return codes + [(s, inn[:2]) for s in near], scales + [(s, inn[2:4]) for s in near]


def hand_on(g, core, T, topo, r):
    S = 32
    far, near, out, inn = ways(core, T, topo, r)
    codes, scales = slice_plan(core, T, topo, r)

    def part(t, s, k):
        return t[:, S * s:S * s + S].bitcast(dt.uint8) if k == 0 else t[:, S * s:S * s + S]
    g.wait_ge(T.sem.h_c, len(out) + 2 * len(inn))
    k = fused(g, T, topo, [([T.cores[s]], e, part(T.hq, s, 0), [part(T.sl, slot(T, topo, r, s), 0)], "s_c")
                           for s, e in codes])
    g.wait_ge(T.sem.h_s, len(inn))
    k += fused(g, T, topo, [([T.cores[s]], e, part(T.hqs, s, 1), [part(T.sls, slot(T, topo, r, s), 1)], "s_s")
                            for s, e in scales])
    if VIA:
        g.wait_ge(T.sem.h_b, len(inn) // 2)
        at = [place2(slot(T, topo, r, s)) for s in far[:VIA]]
        k += fused(g, T, topo, [([T.cores[s] for s in far[:VIA]], out, T.hb[:, 0:34], [T.lws[:, a:a + 34] for a in at],
                                 "b_s")])
    g.wait_ge(T.sem.lo, k)


def apart(x, y):
    if x["n"] in ("dv", "pp"):
        return x["a"] // 512 != y["a"] // 512
    if x["a"] >= y["b"] or y["a"] >= x["b"]:
        return True
    return x["st"] == y["st"] and x["st"] > 1 and (x["a"] - y["a"]) % x["st"] != 0


def builder(g, T):
    queue = {"v": g.vector, "s": g.scalar, "t": g.tensor, "g": g, "y": g.sync}
    sem = {"v": "cv", "s": "cs", "t": "ct_", "g": "cg"}
    count = {"v": 0, "s": 0, "t": 0, "g": 0}
    seen, log, dmas, steps = {}, {}, [0], []

    def ap(n, a, b, st=1, p=None, bc=None, off=None):
        n, k = PART.get(n, (n, 0))
        a, b, t = a + k, b + k, T[n]
        rows = slice(None) if p is None else slice(p[0], p[1])
        v = t[rows, a:b] if st == 1 else t[rows, a:b:st]
        if bc is not None:
            v = v.bitcast(bc)
        if off is not None:
            v = v.indirect(off["v"])
        return {"v": v, "n": n, "a": a, "b": b, "st": st, "off": off}

    def wait(q, tok):
        if seen.get((q, tok[0]), 0) < tok[1]:
            queue[q].wait_ge(T.sem[tok[0]], tok[1])
            seen[(q, tok[0])] = tok[1]

    def need(q, outs, ins):
        toks = {}
        for w, xs in ((True, outs), (False, ins)):
            for x in xs:
                for (y, yw, yq, tok) in log.get(x["n"], []):
                    if apart(x, y):
                        continue
                    psum = x["n"] in ("dv", "pp")
                    if yw or (w and yq != q) or (psum and yq != q):
                        if yq == q == "t" and yw and w:
                            continue
                        toks[tok[0]] = max(toks.get(tok[0], 0), tok[1])
        for k in toks:
            wait(q, (k, toks[k]))

    def note(q, outs, ins, tok):
        for w, xs in ((True, outs), (False, ins)):
            for x in xs:
                log.setdefault(x["n"], []).append((x, w, q, tok))

    def step(kind, q, fn, outs, ins, other=None):
        ins = [x for x in ins if x] + [x["off"] for x in ins + outs if x and x["off"]]
        steps.append((kind, q, fn, outs, ins, other))

    def arrive(n, a, b, tok):
        x = {"n": n, "a": a, "b": b, "st": 1, "off": None}
        log.setdefault(n, []).append((x, True, "far", tok))

    def issue():
        order = ORDER or range(len(steps))
        assert sorted(order) == list(range(len(steps)))
        for k in order:
            kind, q, fn, outs, ins, other = steps[k]
            if k in SCALAR:
                q, fn = "s", other
            need(q, outs, ins)
            if kind == "c":
                count[q] += 1
                fn(queue[q]).then_inc(T.sem[sem[q]], 1)
                note(q, outs, ins, (sem[q], count[q]))
            elif kind == "d":
                s = "d%d" % dmas[0]
                dmas[0] += 1
                fn(queue[q]).then_inc(T.sem[s], 16)
                note("dma", outs, ins, (s, 16))
            else:
                fn(g)
        for tok in [(sem[q], count[q]) for q in count] + [("d%d" % k, 16) for k in range(dmas[0])]:
            if max(seen.get((q, tok[0]), 0) for q in queue) < tok[1]:
                wait("y", tok)
    return ap, step, arrive, issue


def rank_program(g, core, T, topo):
    me = T.rank_of(core)
    helpers = find_helpers(T, topo)
    if me is None:
        if core in helpers:
            hand_on(g, core, T, topo, helpers.index(core))
        return
    ap, step, arrive, issue = builder(g, T)
    u8, u32 = dt.uint8, dt.uint32
    N = len(T.cores)
    far, near, out, inn = ways(core, T, topo, me)
    here = chip_ranks(T, topo, me)
    h0, o = here[0], here.index(me)
    gates = [r for r in far if me in taken_by(T, topo, r)]
    like = [r for r in far if chip_ranks(T, topo, r).index(r) == o]
    assert [(r - me) % N for r in like] == [2, 4, 6] and here[1] == h0 + 1
    sent = []

    def sca(x):
        return x["v"] if isinstance(x, dict) else x

    def dic(*xs):
        return [x for x in xs if isinstance(x, dict)]

    def ts(out, in0, s1, op0, s2=None, op1=None):
        if op1 is None:
            step("c", "v", lambda q: q.tensor_scalar(out["v"], in0["v"], sca(s1), None, op0), [out], dic(in0, s1))
        else:
            step("c", "v", lambda q: q.tensor_scalar(out["v"], in0["v"], sca(s1), sca(s2), op0, op1), [out],
                 dic(in0, s1, s2))

    def tt(out, in0, in1, op):
        step("c", "v", lambda q: q.tensor_tensor(out["v"], in0["v"], in1["v"], op), [out], [in0, in1])

    def scan(out, d0, d1, op0=A.mult, op1=A.add):
        step("c", "v", lambda q: q.tensor_tensor_scan(out["v"], d0["v"], d1["v"], 0.0, op0, op1), [out], [d0, d1])

    def cp(out, in_):
        step("c", "v", lambda q: q.tensor_copy(out["v"], in_["v"]), [out], [in_])

    def turn(x, y):
        step("c", "v", lambda q: q.transpose(x["v"], y["v"]), [x], [y])

    def fill(out, c):
        step("c", "v", lambda q: q.memset(out["v"], c), [out], [])

    def act(out, in_, func, bias=0.0, scale=1.0, accum=None):
        kw = {} if func == F.Copy else {"bias": bias, "scale": scale}
        if accum:
            kw["accum_out"] = accum["v"]
        step("c", "s", lambda q: q.activation(out["v"], in_["v"], func, **kw), [out] + dic(accum), [in_])

    def aff(out, in_, scale=1.0, bias=0.0):
        if scale == 1.0 and not dic(bias) and bias == 0.0:
            step("c", "v", lambda q: q.tensor_copy(out["v"], in_["v"]), [out], [in_],
                 lambda q: q.activation(out["v"], in_["v"], F.Copy))
        else:
            step("c", "v", lambda q: q.tensor_scalar(out["v"], in_["v"], sca(scale), sca(bias), A.mult, A.add), [out],
                 dic(in_, scale, bias),
                 lambda q: q.activation(out["v"], in_["v"], F.Identity, bias=sca(bias), scale=sca(scale)))

    def quant(n, a, b, tile, x0=0):
        o, p, x = ap(n, a, b), ap(n + "s", a, b), ap(tile, x0, x0 + 4 * (b - a))
        step("c", "v", lambda q: q.quantize_mx(o["v"], p["v"], x["v"]), [o, p], [x])

    def mm(out, l, la, r, ra, rb, start=True, stop=True):
        xs = [ap(l, la, la + 128), ap(l + "s", la, la + 128), ap(r, ra, rb), ap(r + "s", ra, rb)]
        step("c", "t", lambda q: q.matmul_mx(out["v"], xs[0]["v"], xs[1]["v"], xs[2]["v"], xs[3]["v"], start, stop),
             [out], xs)

    def pick(dn, c, d, sn, a, b, on, e, f):
        cp(ap(dn, c, d, bc=u32), ap(sn, a, b, bc=u32, off=ap(on, e, f)))
        aff(ap(dn + "s", c, d), ap(sn + "s", a, b, off=ap(on, e, f)))

    def dma(q, o, i, outs, ins):
        step("d", q, lambda e: e.dma_start(o, i), outs, ins)

    def load(q, n, a, b, src):
        o = ap(n, a, b)
        dma(q, o["v"], src, [o], [])

    def send(*xs):
        ys = [([T.cores[r] for r in rs] if rs else [helpers[me]], e, x["v"], [y(r)["v"] for r in rs or [me]], s)
              for rs, e, x, y, s in xs]
        step("r", "g", lambda g: sent.append(fused(g, T, topo, ys)), [], [x[2] for x in xs])

    def slots(n, first, k, bc=None):
        def at(r):
            a = first(slot(T, topo, me, r))
            return ap(n, a, a + k, bc=bc)
        return at(me), at

    def pass_on(first, ex):
        def run_of(rs):
            return first(slot(T, topo, rs[0], me)), first(slot(T, topo, rs[-1], me) + 1)
        own, other = taken_by(T, topo, me), taken_by(T, topo, near[0])
        arrive("lw", *run_of(own), (ex + "_c", len(own) * len(out)))
        arrive("lw", *run_of(other), (ex + "_cf", len(inn)))
        x = ap("lw", *run_of(own), bc=u8)
        send((near, inn, x, lambda r: x, ex + "_cf"))

    def c(n, k=0):
        return ap(n, k, k + 1)

    def iota(n, k, pat, base=0, cm=0):
        o, small = ap(n, 0, k), SCRATCH[PART.get(n, (n, 0))[0]][2] != I32
        kw = {"allow_small_or_imprecise_dtypes": True} if small else {}
        step("c", "g", lambda q: q.iota(o["v"], pat, base, cm, **kw), [o], [])

    def bank(n, k, a=0, b=128, st=1):
        return ap(n, 512 * k + a, 512 * k + b, st)

    load("s", "u4", 0, 4, T.u[:, 0:4])
    load("y", "tbx", 0, 512, T.tb[:, 0:512])
    load("s", "tbx", 512, 1024, T.tb[:, 512:1024])
    load("y", "nzx", 0, 256, T.nz[:, 0:256])
    load("y", "wx", 0, 512, T.w[:, 0:512])
    iota("pi", 4, [[0, 4]], 0, 1)
    iota("pj", 2, [[128, 2]], 0, 1)
    iota("io", 128, [[1, 128]])
    iota("k2", 256, [[0, 8], [2, 16], [32, 2]], -128)
    iota("qd4", 128, [[0, 8], [1, 4], [0, 4]])
    iota("xr", 32, [[-1, 4], [0, 8]])
    iota("c4", 16, [[0, 4], [1, 4]])
    iota("idx", 16, [[16, 4], [-508, 4]])
    iota("c4x", 4, [[128 - 256 * o, 2], [16, 2]], 128 * o)
    iota("c256", 8, [[2, 8]], 256)
    iota("c32", 8, [[32, 8]])
    iota("frow", 256, [[1, 256]])
    iota("p256", 64, [[16, 4], [1, 4], [4, 4]], 256)
    zb, pi, lo, pf, io = ap("zb", 0, 128), ap("pi", 0, 4), c("lo"), c("pf"), "io"
    fill(zb, 0.0)
    fill(ap("xt", 0, 16), 0.0)
    fill(ap("rs8", 0, 64), -100.0)
    fill(ap("rs8", 0, 64, 8), 3.5)
    fill(ap("m32", 0, 64), -32.0)
    fill(ap("eb", 0, 528), 0.0)
    fill(ap("fit", 8, 16), 0.0)
    fill(ap("vv", 32, 40), 0.0)
    fill(ap("odw", 0, 16), -1.0)
    fill(ap("odw", N - 1 - h0, 16, 8), 7.0)
    fill(ap("f0", 0, 7), 0.0)
    cp(pf, c("pi"))
    ts(ap("hi2", 0, 2), ap("pj", 0, 2), 240, A.bitwise_and)
    ts(ap("lo2", 0, 2), ap("pj", 0, 2), 15, A.bitwise_and)
    cp(lo, c("lo2"))
    c16 = ap(io, 0, 32, 16)
    for a, n in ((0, "hi2"), (6, "hi2"), (8, "lo2"), (14, "lo2")):
        cp(ap("xt", a, a + 2), ap(n, 0, 2))
    ts(ap("tie", 0, 128), ap(io, 0, 128), pf, A.is_lt, TINY, A.mult)
    ts(ap("eb", 3, 515, 4), ap(io, 0, 128), pf, A.is_equal, 0.5, A.mult)
    for b in range(4):
        quant("eh", 128 * b, 128 * b + 128, "eb", 3 - b)
    ts(ap("yx", 0, 4), pi, 7, A.bitwise_and)
    ts(ap("bi", 0, 4), pi, 3, A.logical_shift_right, 1, A.bitwise_and)
    tt(ap("yx", 4, 8), ap("bi", 0, 4), ap(io, 0, 8, 2), A.add)
    cp(ap("l1", 0, 8), ap("yx", 0, 8))
    ts(ap("l8", 0, 8), ap("yx", 0, 8), 8.0, A.mult, 7.0, A.add)
    ts(ap("lv0", 0, 8), ap("yx", 0, 8), 1.0, A.min, 31.0, A.mult)
    tt(ap("lv1", 0, 8), ap("lv0", 0, 8), ap("yx", 0, 8), A.add)
    ts(ap("lv", 0, 8), ap("lv1", 0, 8), 31.0, A.add)
    ts(ap("gx0", 0, 4), ap("yx", 4, 8), 16.0, A.mult, 8.0 * o - 41.0, A.add)
    ts(ap("gx", 0, 4), ap("gx0", 0, 4), 8.0 * o + 7.0, A.max, 8.0 * o + 55.0, A.min)
    lq7, lrs, gis, grs = ap("l1", 0, 4), ap("l1", 4, 8), ap("l8", 0, 4), ap("l8", 4, 8)
    ts(ap("jc", 0, 2), ap("pi", 0, 2), 3, A.bitwise_and)
    ts(c("jc", 2), c("pi"), 4, A.logical_shift_right, 3, A.bitwise_and)
    ts(ap("jc", 3, 7), pi, 4, A.logical_shift_right, 1, A.bitwise_and)
    ts(ap("jc", 5, 7), ap("jc", 5, 7), 2.0, A.add)
    ts(ap("lz", 0, 4), ap("jc", 3, 7), 7.0, A.add)
    cp(c("q4f"), c("jc"))
    ts(c("qi"), c("pi"), 2, A.logical_shift_right, 3, A.bitwise_and)
    cp(c("qq4"), c("qi"))
    aff(c("corr4"), c("q4f"), 512.0, c("qq4"))
    ts(ap("wt4", 0, 16), ap("c4", 0, 16), c("q4f"), A.is_equal, -1000000.0, A.mult)
    ts(c("hf"), c("pi"), 1, A.logical_shift_right, 7, A.bitwise_and)
    ts(c("h14"), c("hf"), 2.0, A.min, 14.0, A.mult)
    aff(c("l14"), c("h14"), 1.0, lo)
    ts(c("lll"), c("hf"), 32.0, A.mult, c("l14"), A.add)
    ts(ap("c14", 0, 8), ap("c32", 0, 8), 64.0, A.min, 0.4375, A.mult)
    tt(ap("c270", 0, 8), ap("c14", 0, 8), ap("c256", 0, 8), A.add)
    aff(c("lo256"), lo, 1.0, 256.0)
    aff(c("lom"), lo, 2.0, -128.0)
    aff(c("corr"), lo, 512.0, -7680.0)
    aff(ap("c35", 0, 32), ap("xr", 0, 32), 1.0, 3.5)
    ts(ap("lme", 0, 2), c16, lo, A.add, 32.0 * me, A.add)
    cp(c("lq1"), lo)
    ts(c("mo", 0), c("bi"), float(o), A.is_equal)
    ts(c("mo", 1), c("bi"), float(o), A.not_equal)
    ts(ap("r0", 0, 2), ap("pi", 0, 2), 3, A.logical_shift_right, 3, A.bitwise_and)
    tt(ap("r1", 0, 2), ap("r0", 0, 2), ap(io, h0, h0 + 8, 4), A.add)
    ts(ap("r2", 0, 2), ap("r1", 0, 2), 7, A.bitwise_and)
    ts(ap("frac", 0, 2), ap("r2", 0, 2), -0.125, A.mult, 0.875, A.add)
    cp(ap("r3", 0, 8), ap(io, h0, h0 + 8))
    ts(ap("r4", 0, 8), ap("r3", 0, 8), 7, A.bitwise_and)
    ts(ap("fr", 0, 8), ap("r4", 0, 8), -0.125, A.mult, 0.875, A.add)
    ts(ap("m16", 0, 128), ap("k2", 0, 256, 2), c("lom"), A.is_equal)
    aff(ap("wt", 0, 128), ap("m16", 0, 128), -1000512.0, 512.0)
    ts(c("ind4"), pf, 64.0, A.is_lt, 4.0, A.mult)
    for t in range(4):
        ts(ap("w4t", t, 512, 4), ap("qd4", 0, 128), float(t), A.is_equal, c("ind4"), A.mult)
    quant("w4q", 0, 128, "w4t")
    quant("xq", 0, 128, "xt")
    quant("wl", 16, 144, "wx")
    for t in range(4):
        aff(ap("ux", t, 512, 4), zb, 1.0, c("u4", t))
    for t in range(4):
        aff(ap("ux", 512 + t, 1024, 4), ap("ux", t, 512, 4), -1.0)
    quant("uq", 0, 128, "ux")
    quant("uq", 128, 256, "ux", 512)

    quant("tq", 0, 128, "tbx")
    quant("tq", 128, 256, "tbx", 512)
    send(([], out + inn, ap("tq", 0, 128, bc=u8), lambda r: ap("hq", 0, 128, bc=u8), "h_c"))
    send(([], inn, ap("tq", 128, 256, bc=u8), lambda r: ap("hq", 128, 256, bc=u8), "h_c"))
    send(([], inn, ap("tqs", 0, 256), lambda r: ap("hqs", 0, 256), "h_s"))
    pick("sl", 32 * o, 32 * o + 32, "tq", 0, 256, "lme", 0, 2)
    mm(bank("dv", 0), "uq", 0, "tq", 0, 128)
    mm(bank("dv", 1), "uq", 0, "tq", 128, 256)
    for k, (own, oth) in enumerate(((0, 0), (0, 128), (128, 0), (128, 128))):
        first = own <= oth and k != 3
        if first and k:
            mm(bank("pp", k), "tq", own, "uq", 128, 256, True, False)
            mm(bank("pp", k), "uq", 0, "tq", oth, oth + 128, False, True)
        else:
            mm(bank("pp", k), "uq", 0, "tq", oth, oth + 128, True, False)
            mm(bank("pp", k), "tq", own, "uq", 128, 256, False, True)
    act(ap("junk", 0, 128), bank("dv", 0), F.Sign, bias=-TINY, accum=c("ft", 0))
    act(ap("junk", 128, 256), bank("dv", 1), F.Sign, bias=-TINY, accum=c("ft", 1))
    act(ap("junk", 256, 384), bank("pp", 1), F.Sign, bias=-TINY, scale=-1.0, accum=c("ss", 0))
    act(ap("junk", 384, 512), bank("pp", 2), F.Sign, bias=TINY, scale=-1.0, accum=c("ss", 1))
    ts(c("v0"), c("ft", 1), c("ft", 0), A.add, 0.5, A.mult)
    send((near, inn, c("v0"), lambda r: c("vn"), "a_n"))
    arrive("vn", 0, 1, ("a_n", len(inn)))
    aff(c("vm"), c("v0"), c("mo", 0))
    aff(c("f0", 7), c("vn"), c("mo", 1), c("vm"))
    send((like, out, c("f0", 7), lambda r: c("f0", 7 + slot(T, topo, h0, r) // 2), "a_v"))
    arrive("f0", 8, 11, ("a_v", len(like) * len(out)))
    for h, k in ((0, 0), (1, 3)):
        w = ap("cmp", 128 * h, 128 * h + 128)
        tt(w, bank("pp", k), ap("tie", 0, 128), A.is_lt)
        scan(ap("sa", 128 * h, 128 * h + 128), w, w, A.add, A.add)
    aff(ap("s64", 0, 2), ap("ss", 0, 2), 1.0, -64.0)
    for e, (tile, s) in enumerate((("oh", "ss"), ("oh2", "s64"))):
        for h in (0, 1):
            ts(ap(tile, h, 512, 2), ap("k2", 0, 256), c(s, h), A.subtract, c("sa", 128 * h + 127), A.is_equal)
        quant("oq", 128 * e, 128 * e + 128, tile)
        mm(bank("dv", 2 + e), "oq", 128 * e, "xq", 0, 128)
        for k in (0, 1):
            ts(c("jl4", 2 * e + k), bank("dv", 2 + e, k, k + 1), bank("dv", 2 + e, k + 2, k + 3), A.add)
        aff(ap("lt", 4 * e, 4 * e + 4), bank("dv", 2 + e, 0, 4))
    pick("lw", 32 * o, 32 * o + 32, "tq", 0, 256, "jl4", 0, 2)

    x, y = slots("lw", lambda s: 32 * s, 32, u8)
    send((gates, out, x, y, "a_c"), (near, inn, x, y, "a_s"))
    x, y = slots("lws", lambda s: 32 * s, 32)
    send((far, out, x, y, "a_s"), (near, inn, x, y, "a_s"))
    tok = ("a_s", len(far) * len(out) + 2 * len(inn))
    arrive("lw", 32 - 32 * o, 64 - 32 * o, tok)
    arrive("lws", 32 - 32 * o, 64 - 32 * o, tok)
    arrive("lws", 64, 256, tok)
    pass_on(lambda s: 32 * s, "a")
    pick("xw", 128, 160, "tq", 0, 256, "jl4", 2, 4)
    quant("lq", 0, 128, "lt")
    mine2, near2 = place2(o), place2(1 - o)
    pick("lw", mine2 + 32, mine2 + 48, "lq", 0, 128, "lq1", 0, 1)
    quant("cn", 64, 192, "nzx")
    for b in range(4):
        mm(bank("dv", b), "eh", 128 * b, "cn", 64, 192, True, False)
    for b in range(4):
        mm(bank("pp", b), "eh", 128 * b, "cn", 64, 192)
        aff(ap("dn", b, 256, 4), bank("pp", b, 32, 96))

    for b in (0, 1):
        aff(ap("xk", 32 * b, 32 * b + 32), ap("f0", 0, 11, off=ap("lz", 2 * b, 2 * b + 2)), 1.0, c("frac", b))
    turn(ap("ak", 0, 64), ap("xk", 0, 64))
    turn(ap("ak2", 0, 64), ap("xk", 0, 64))
    tt(ap("cm", 0, 64), ap("ak2", 0, 64, off=gis), ap("ak", 0, 64), A.is_gt)
    scan(ap("sc", 0, 64), ap("rs8", 0, 64), ap("cm", 0, 64), A.max, A.subtract)
    g0, mine = ap("sc", 7, 64, 8), c("sc", 8 * o + 7)
    ts(ap("ms", 0, 8), g0, mine, A.add, 0.0, A.not_equal)
    scan(ap("st0", 0, 8), ap("ms", 0, 8), ap("m32", 0, 8))
    ts(ap("ofa", 0, 2), c16, c("st0", 7), A.add, c("lo256"), A.add)
    ts(c("go"), mine, 0.0, A.is_gt, 128.0, A.mult)
    ts(ap("ofx", 0, 2), c16, c("go"), A.add, lo, A.add)
    ts(ap("tk", 0, 8), g0, 0.0, A.is_lt)
    pick("cn", 32, 64, "lw", 0, 256, "ofa", 0, 2)
    for b in range(4):
        mm(bank("dv", b), "eh", 128 * b, "cn", 32, 160, False, True)
        aff(ap("vt", b, 128, 4), bank("dv", b, 0, 32))
    quant("xw", 0, 128, "vt")
    pick("lw", mine2, mine2 + 32, "xw", 0, 160, "ofx", 0, 2)

    def count(k, pk, n, a, at):
        mm(bank("pp", pk), "uq", 0, n, a, a + 128)
        ts(ap("cb", 32 * k, 32 * k + 32), bank("pp", pk, at, at + 32), 0.0, A.is_gt, c("tk", k), A.mult)
        scan(ap("f1", 32 * k, 32 * k + 32), ap("cb", 32 * k, 32 * k + 32), ap("zb", 0, 32), A.add, A.add)
    count(o, 0, "xw", 0, 0)
    x, y = slots("lw", place2, 34, u8)
    send((gates, out, x, y, "b_c"), (near, inn, x, y, "b_cn"))
    x, y = slots("lws", place2, 34)
    h = len(inn) // 2
    if VIA:
        send((near, inn[:h], x, y, "b_sn"), ([], inn[h:], x, lambda r: ap("hb", 0, 34), "h_b"))
    else:
        send((near, inn, x, y, "b_sn"))
    send((far, out, c("f1", 32 * o + 31), lambda r: c("f1", 62 + slot(T, topo, me, r)), "b_v"))
    if far[VIA:]:
        send((far[VIA:], out, x, y, "b_s"))
    arrive("lw", near2, near2 + 34, ("b_cn", len(inn)))
    arrive("lws", near2, near2 + 34, ("b_sn", h if VIA else len(inn)))
    arrive("lws", place2(2), place2(N), ("b_s", len(far) * len(out)))
    arrive("f1", 64, 70, ("b_v", len(far) * len(out)))
    count(1 - o, 3, "lw", near2 - 94, 94)
    pass_on(place2, "b")

    plans = [slice_plan(helpers[r], T, topo, r) for r in range(N) if r != me]
    for k, n, s in ((0, "sl", "s_c"), (1, "sls", "s_s")):
        tok = (s, sum(len(e) for p in plans for d, e in p[k] if d == me))
        arrive(n, 32 - 32 * o, 64 - 32 * o, tok)
        arrive(n, 64, 256, tok)
    tt(ap("mi", 0, 32), ap("sc", 0, 64, off=ap("l8", 0, 2)), ap("c35", 0, 32), A.not_equal)
    scan(ap("st4", 0, 32), ap("mi", 0, 32), ap("m32", 0, 32))
    ts(ap("ofs", 0, 8, 2), ap("st4", 7, 32, 8), lo, A.add, 256.0, A.add)
    ts(ap("ofs", 1, 8, 2), ap("st4", 7, 32, 8), lo, A.add, 272.0, A.add)
    pick("st", 0, 128, "sl", 0, 256, "ofs", 0, 8)
    for n, b, sem in (("st", u8, "p_c"), ("sts", None, "p_s")):
        send((near, inn, ap(n, 0, 128, bc=b), lambda r, n=n, b=b: ap(n, 128, 256, bc=b), sem))
        arrive(n, 128, 256, (sem, len(inn)))

    act(ap("q0", 0, 64), ap("sc", 0, 64, off=grs), F.Abs)
    tt(ap("fit", 0, 8), ap("ak", 0, 64, 8), ap("fr", 0, 8), A.subtract)
    tt(ap("fd", 0, 8), ap("fit", 0, 8), ap("fit", 1, 9), A.subtract)
    tt(ap("miss0", 0, 64), ap("sc", 0, 64, off=gis), ap("q0", 0, 64), A.not_equal)
    aff(ap("fde", 0, 64), ap("fd", 0, 8, off=lq7))
    scan(ap("hfs", 0, 64), ap("miss0", 0, 64), ap("fde", 0, 64))
    scan(ap("hhs", 0, 64), ap("miss0", 0, 64), ap("m32", 0, 64))
    fh = ap("hfs", 7, 64, 8)
    tt(ap("bb", 0, 8), ap("tk", 0, 8), fh, A.mult)
    ts(ap("bc", 0, 8), ap("bb", 0, 8), 96.0, A.max)
    tt(ap("bd", 0, 8), fh, ap("bc", 0, 8), A.subtract)
    tt(ap("kb", 0, 8), ap("bd", 0, 8), ap("fr", 0, 8), A.add)
    aff(ap("kx", 0, 64), ap("kb", 0, 8, off=lrs))
    tt(ap("nd", 0, 64), ap("kb", 0, 8, off=lq7), ap("kx", 0, 64), A.subtract)
    tt(ap("o1", 0, 8), ap("tk", 0, 8), ap("c270", 0, 8), A.mult)
    aff(ap("vv", 0, 8), ap("q0", 0, 64, 8), -32.0, 112.0)
    tt(ap("vv", 8, 16), ap("o1", 0, 8), ap("c32", 0, 8), A.add)
    aff(ap("w1", 0, 8), ap("hhs", 7, 64, 8), 1.0625, 640.0)
    ts(ap("w2", 0, 8), ap("hhs", 7, 64, 8), -192.0, A.min, 0.4375, A.mult)
    tt(ap("vv", 16, 24), ap("w1", 0, 8), ap("w2", 0, 8), A.add)
    aff(ap("vv", 24, 32), ap("hhs", 7, 64, 8), 0.125, 32.0)
    tt(ap("ve", 0, 32), ap("vv", 0, 32), ap("vv", 1, 33), A.subtract)
    aff(ap("ve", 32, 64), ap("ve", 0, 8, off=ap("l1", 0, 2)))
    aff(ap("kk", 0, 3), ap("vv", 8, 32, 8), 1.0, lo)
    ts(ap("ode", 0, 8), g0, pf, A.add, 3.5, A.not_equal)

    aff(ap("x1b", 0, 64), ap("f1", 0, 70, off=ap("lv", 4, 8)))
    tt(ap("k1b", 0, 64), ap("f1", 0, 70, off=ap("lv", 0, 4)), ap("nd", 0, 64), A.add)
    tt(ap("cmb", 0, 64), ap("x1b", 0, 64), ap("k1b", 0, 64), A.is_lt)
    scan(ap("scb", 0, 64), ap("rs8", 0, 64), ap("cmb", 0, 64), A.max, A.subtract)
    act(ap("qx", 0, 64), ap("scb", 0, 64, off=ap("gx", 0, 4)), F.Abs)
    tt(ap("miss", 0, 64), ap("scb", 0, 64, off=gis), ap("qx", 0, 64), A.not_equal)
    scan(ap("bs", 0, 64), ap("miss", 0, 64), ap("ve", 0, 64))
    c4x = ap("c4x", 0, 4)
    for k, s in enumerate((39, 47, 55, 7)):
        ts(ap("of", 4 * k, 4 * k + 4), c4x, c("bs", s), A.add, c("kk", 0), A.add)
    pick("sb", 0, 192, "st", 0, 256, "of", 0, 12)
    pick("wl", 0, 16, "lw", 288, 556, "lll", 0, 1)
    for k in (0, 1):
        mm(bank("pp", 1 + k), "eh", 128 * k, "wl", 0, 128, True, False)
        mm(bank("pp", 1 + k), "eh", 128 * k + 256, "wl", 0, 128, False, True)
        aff(ap("jv", k, 32, 2), bank("pp", 1 + k, 0, 16), 2.0)

    w, col = len(out) // 4, 32 * h0
    for n, b, sem, es in (("", u8, "c_c", (out[:2 * w], out[2 * w:3 * w], out[3 * w:])),
                          ("s", None, "c_s", (out[2 * w:], out[:w], out[w:2 * w]))):
        y = ap("fw" + n, col, col + 64, bc=b)
        send(*[([r], es[k], ap("sb" + n, 64 * k, 64 * k + 64, bc=b), lambda r, y=y: y, sem) for k, r in enumerate(like)])
    pick("fw", col, col + 64, "st", 0, 256, "of", 12, 16)

    ts(ap("ofc", 0, 2), c16, c("bs", 15), A.add, c("kk", 1), A.add)
    ts(ap("ofc", 2, 4), c16, c("bs", 23), A.add, c("kk", 2), A.add)
    ts(ap("jl", 0, 7), ap("jc", 0, 7), c("bs", 31), A.add)
    pick("cn", 0, 64, "lw", 0, 556, "ofc", 0, 4)
    mm(bank("pp", 0), "uq", 0, "cn", 0, 128, True, False)
    mm(bank("pp", 0), "cn", 0, "uq", 128, 256, False, True)
    for b in range(4):
        mm(bank("dv", b), "eh", 128 * b, "cn", 0, 128)
        aff(ap("dc", b, 256, 4), bank("dv", b, 0, 64))
    aff(ap("gb", 16, 96), ap("jv", 0, 32, off=ap("jl", 2, 7)))
    turn(ap("cj", 0, 64), ap("gb", 32, 96))
    ts(ap("ntie", 0, 64), ap("cj", 0, 64), c("gb", 16), A.is_gt, -TINY, A.mult)
    tt(ap("oh", 0, 64), bank("pp", 0, 0, 64), ap("ntie", 0, 64), A.is_gt)
    quant("cx", 0, 128, "oh")
    mm(bank("pp", 3), "w4q", 0, "cx", 0, 128)
    ts(ap("l4", 0, 16), bank("pp", 3, 0, 16), c("q4f"), A.add)
    tt(ap("vt2", 0, 256), ap("dn", 0, 256, off=ap("l4", 0, 16)), ap("dc", 0, 256), A.add)
    quant("cn", 64, 192, "vt2")
    ts(c("t128"), c("scb", 8 * o + 7), 0.0, A.is_lt, 128.0, A.mult)
    ts(ap("sel", 0, 16), bank("pp", 3, 0, 16), c("t128"), A.is_lt, 64.0, A.mult)
    tt(ap("off", 0, 16), ap("sel", 0, 16), ap("idx", 0, 16), A.add)
    scan(ap("xs", 0, 16), ap("wt4", 0, 16), ap("off", 0, 16), A.add, A.max)
    ts(ap("xl", 0, 4), ap("xs", 3, 16, 4), c("corr4"), A.add)
    pick("fw", 256, 320, "cn", 0, 128, "xl", 0, 4)
    cp(ap("jw", 0, 16), ap("jv", 0, 32, off=ap("jl", 0, 1)))
    cp(ap("frow", 0, 256, off=ap("jw", 0, 4)), ap("p256", 0, 64))
    for k in (0, 1):
        scan(ap("fs", 128 * k, 128 * k + 128), ap("wt", 0, 128), ap("frow", 128 * k, 128 * k + 128), A.add, A.max)
    ts(ap("fl", 0, 16), ap("fs", 15, 256, 16), c("corr"), A.add)
    ts(ap("ode", 8, 16), ap("scb", 7, 64, 8), pf, A.add, 3.5, A.not_equal)
    scan(ap("odc", 0, 16), ap("ode", 0, 16), ap("odw", 0, 16))
    aff(ap("odr", 0, 2), ap("odc", 7, 16, 8), 1.0, float(h0))
    for t in (0, 1):
        x = ap("odr", t, t + 1, p=(0, 8))
        dma("y", T.od[t:t + 1, 0:8], x["v"], [], [x])

    for k in ((0, col), (col + 64, 256)):
        arrive("fw", k[0], k[1], ("c_c", len(out)))
        arrive("fws", k[0], k[1], ("c_s", len(out)))
    for k in (0, 1):
        pick("oq2", 128 * k, 128 * k + 128, "fw", 0, 320, "fl", 8 * k, 8 * k + 8)
        mm(bank("pp", 1 + k), "wl", 16, "oq2", 128 * k, 128 * k + 128)
        x = ap("oq2", 128 * k, 128 * k + 128, bc=u8)
        dma("y", T.oc[:, 512 * k:512 * k + 512], x["v"], [], [x])
        x = ap("yo", 128 * k, 128 * k + 128)
        aff(x, bank("pp", 1 + k))
        dma("sy"[k], T.y[:, 128 * k:128 * k + 128], x["v"], [], [x])
    for k in range(4):
        x = ap("oq2s", 0, 256, p=(32 * k, 32 * k + 4))
        dma("yyss"[k], T.osc[4 * k:4 * k + 4, 0:256], x["v"], [], [x])
    issue()
    g.wait_ge(T.sem.lo, sum(sent))
